import numpy as np, ml_dtypes
CORES = [35,38,43,46]
N = 4
BF = ml_dtypes.bfloat16
def gentries(a):
    return np.ascontiguousarray(a.reshape(8, 16, -1).transpose(0, 2, 1)).reshape(8, -1)
def gtable(e):
    e = np.asarray(e); return np.ascontiguousarray(e.reshape(8, -1, 16).transpose(0, 2, 1)).reshape(128, -1).astype(np.int32)
V, S, L, DS = 4096, 128, 16, (1, 2, 3)
W = N * V
def mix(rng, a):
    return np.take_along_axis(a, np.argsort(rng.random(a.shape), axis=-1), -1)
def some(rng, pool, shape, n):
    q = len(pool) // n
    return pool[np.arange(n) * q + rng.integers(0, q, shape + (n,))]
def parts(rng):
    x = (256 * np.sqrt(rng.random((N, 8, 1, V))) * rng.random((N, 8, 16, V))).astype(np.int64)
    sl = np.empty((N, 8, S, L), np.int64)
    for g in range(8):
        p = rng.permutation(W); a = p[:3 * L][np.argsort(rng.random((N, S, 3 * L)), axis=-1)[..., :L]]
        sl[:, g] = np.where(np.arange(L) < rng.integers(0, L + 1, (N, S, 1)), a, some(rng, p[3 * L:], (N, S), L))
    return x, mix(rng, sl), rng.integers(0, S * L, (N, 8, V))
def pack(x, sl, pr):
    return {"x": np.ascontiguousarray(x.reshape(N, 128, V)).astype(np.float32).astype(BF), "sl": np.stack([gtable(a.reshape(8, -1)) for a in sl]), "prey": np.stack([gtable(a) for a in pr])}
def setup_inputs(rng):
    return pack(*parts(rng))
def setup_inputs_pools(rng):
    x, sl, pr = parts(rng)
    for g in range(8):
        x[:, g] = rng.integers(0, 256, 16)[np.argsort(rng.random((N, 16, V)), axis=1)]
    ms = np.array([0, 1, 2, L // 2, L - 1, L])
    for a in range(N):
        b = a ^ DS[0]
        if a < b:
            for g in range(8):
                e = some(rng, rng.permutation(W), (S,), 2 * L); m = rng.choice(ms, (S, 1)); m[:6, 0] = ms
                if g == 2: m[:] = 0
                if g == 5: m[:] = L
                sl[a, g] = mix(rng, e[:, :L]); sl[b, g] = mix(rng, np.where(np.arange(L) < m, e[:, L:], e[:, :L]))
    return pack(x, sl, pr)
def setup_inputs_ties(rng):
    x, sl, pr = parts(rng)
    kind = rng.integers(0, 4, (N, 8, V)); proto = rng.integers(0, 256, (8, 16, 4))
    proto[1, :, 1] = proto[1, ::-1, 0]; proto[1, :, 3] = proto[1, ::-1, 2]; proto[0] = rng.integers(0, 256, (1, 1))
    for q in range(N):
        for g in range(8): x[q, g] = proto[g][:, kind[q, g]]
    return pack(x, sl, pr)
def setup_inputs_few(rng):
    x, sl, pr = parts(rng); o = rng.permutation(N)
    for g in (0, 4):
        c = np.concatenate([np.array([0, W - 1]), 1 + rng.permutation(W - 2)[:L]])
        sl[:, g] = c[np.argsort(rng.random((N, S, L + 2)), axis=-1)[..., :L]]
    pr[:, 1] = rng.choice(np.array([0, L - 1, L, S * L - 1]), (N, V)); pr[:, 5] = S * L - 1
    sl[1:, 5] = sl[0, 5]
    sl[:, 2] = mix(rng, some(rng, o[0] * V + rng.permutation(V), (N, S), L))
    sl[:, 6] = mix(rng, some(rng, o[1] * V + 1024 * rng.integers(0, V // 1024) + rng.permutation(1024), (N, S), L))
    for g in (3, 7): sl[:, g] = mix(rng, np.zeros((N, S, 1), np.int64) + rng.permutation(W)[:L])
    return pack(x, sl, pr)
def setup_inputs_ends(rng):
    x, sl, pr = parts(rng); x = 255 * rng.integers(0, 2, x.shape)
    for g in (0, 3, 6): x[:, g, :, 0::2] = 0; x[:, g, :, 1::2] = 255
    x[:, 1, :, 0::2] = rng.integers(0, 32, (N, 16, V // 2)); x[:, 1, :, 1::2] = rng.integers(224, 256, (N, 16, V // 2))
    c = np.arange(V); low = 255 * (L - 1) // (2 * L - 1); e = rng.integers(0, 4, (N, 16, V))
    x[:, 2] = np.where(np.arange(16)[:, None] % L == (c // 2) % L, 255 * (1 - c % 2), np.where(c % 2 == 1, 255 - low + e, low - e))
    for a in range(N):
        odd = int(a > (a ^ DS[0]))
        sl[a, 0] = some(rng, 2 * rng.permutation(W // 2) + odd, (S,), L); sl[a, 3] = some(rng, 2 * rng.permutation(W // 2) + 1 - odd, (S,), L)
        sl[a, 1] = some(rng, 2 * rng.permutation(W // 2) + odd, (S,), L)
        sl[a, 2] = mix(rng, 2 * (L * rng.integers(0, W // (2 * L), (S, L)) + np.arange(L)) + odd)
    t = np.arange(S)
    for a in range(N):
        b = a ^ DS[0]
        if a < b: sl[b, 0, t, rng.integers(0, L, S)] = sl[a, 0, t, rng.integers(0, L, S)]
    sl[:, 4] = np.concatenate([rng.permutation(W) for i in range((N * S * L + W - 1) // W)])[:N * S * L].reshape(N, S, L)
    one = rng.integers(0, N) * V + np.concatenate([rng.permutation(V) for i in range((S * L + V - 1) // V)])[:S * L].reshape(S, L)
    sl[:, 5] = mix(rng, np.zeros((N, 1, 1), np.int64) + one)
    sl[:, 7] = mix(rng, some(rng, 16 * rng.permutation(W // 16) + rng.integers(0, 16), (N, S), L))
    for g in (4, 5): pr[:, g] = mix(rng, np.zeros((N, 1), np.int64) + np.arange(max(V, S * L)) % (S * L))[:, :V]
    return pack(x, sl, pr)
def setup_inputs_spread(rng):
    x, sl, pr = parts(rng)
    x = (np.exp2(8 * rng.random((N, 8, 1, V))) * rng.random((N, 8, 16, V)) * (rng.random((N, 8, 1, V)) > 0.0625)).astype(np.int64)
    pr = np.minimum((S * L * rng.random((N, 8, V)) ** 3).astype(np.int64), S * L - 1)
    return pack(x, sl, pr)
def check_inputs(d):
    bad = []
    v = np.asarray(d["x"]).astype(np.float32)
    if not np.all((v >= 0) & (v <= 255) & (v == np.floor(v))): bad.append("range of x")
    for k, hi in (("sl", W - 1), ("prey", S * L - 1)):
        if np.min(d[k]) < 0 or np.max(d[k]) > hi: bad.append("range of " + k)
    e = np.sort(np.stack([gentries(a) for a in d["sl"]]).reshape(N, 8, S, L), axis=-1)
    if np.any(e[..., 1:] == e[..., :-1]): bad.append("different species in a site of sl")
    return bad
def reference(x, sl, prey):
    v = x.astype(np.float32).astype(np.int64).reshape(N, 8, 16, V)
    ls = np.stack([gentries(a) for a in sl]).astype(np.int64).reshape(N, 8, S, L); pl = np.stack([gentries(a) for a in prey]).astype(np.int64)
    j = np.arange(L)
    for d in DS:
        w = np.concatenate([v[a] for a in range(N)], axis=2)
        cs, od = [], []
        for a in range(N):
            c = np.add.reduce(np.take_along_axis(w, ls[a].reshape(8, 1, S * L), 2).reshape(8, 16, S, L), axis=3)
            cs.append(c); od.append(np.argsort(np.arange(S) - S * np.add.reduce(c, axis=1), axis=1))
        new = np.array(ls)
        for a in range(N):
            b = a ^ d
            if a < b:
                la = np.take_along_axis(ls[a], od[a][:, :, None], 1); lb = np.take_along_axis(ls[b], od[b][:, :, None], 1)
                ca = np.take_along_axis(cs[a], od[a][:, None, :], 2)[..., None]; cb = np.take_along_axis(cs[b], od[b][:, None, :], 2)[..., None]
                pool = np.concatenate([la, lb], axis=2)
                px = L * np.take_along_axis(w, pool.reshape(8, 1, -1), 2).reshape(8, 16, S, 2 * L)
                key = 2 * L * np.add.reduce(np.abs(px - ca) - np.abs(px - cb), axis=1) + np.arange(2 * L)
                eq = la[:, :, :, None] == lb[:, :, None, :]
                com = np.concatenate([np.any(eq, axis=3), np.any(eq, axis=2)], axis=2)
                m = np.add.reduce((~com[:, :, :L]).astype(np.int64), axis=2)[:, :, None]
                sp = np.take_along_axis(pool, np.argsort(np.where(com, 2 ** 40 + np.arange(2 * L), key), axis=2), 2)
                np.put_along_axis(new[a], od[a][:, :, None], np.take_along_axis(sp, np.where(j < m, j, m + j), 2), 1)
                np.put_along_axis(new[b], od[b][:, :, None], np.take_along_axis(sp, np.where(j < m, m + j, L + j), 2), 1)
        ls = new
        hx = [np.take_along_axis(w, np.take_along_axis(ls[a].reshape(8, S * L), pl[a], 1)[:, None, :], 2) for a in range(N)]
        v = (v + np.stack(hx) + 1) >> 1
    return {"yl": np.stack([gtable(a.reshape(8, -1)) for a in ls]).astype(np.float32), "yx": v.reshape(N, 128, V).astype(np.float32)}

@@ -1,0 +1,613 @@
+from concourse.bass import DstId, RemoteDMATransfer
+from concourse.mybir import AluOpType, ActivationFunctionType
+
+BF, FH, FF, I4, U2 = "bfloat16", "float16", "float32", "int32", "uint16"
+S6 = [128, 8, 2, 2, 2, 2]
+_SB = {
+    "SL": ([128, 128], I4), "PR": ([128, 256], I4), "XW": ([128, 4128], BF),
+    "LISTS": ([128, 512], U2), "OFF": ([128, 512], U2), "REP": ([128, 6144], BF),
+    "PREYL": ([128, 256], U2), "ILST": ([128, 128], U2),
+    "q0": ([128, 128], I4), "q1": ([128, 128], I4), "q2": ([128, 128], I4),
+    "w0": ([128, 256], I4), "w1": ([128, 256], I4), "w2": ([128, 256], I4), "w3": ([128, 256], I4), "w4": ([128, 256], I4),
+    "PT": ([128, 2048], BF), "IDT": ([128, 1280], BF), "PWIN": ([128, 16384], BF),
+    "ALLT0": ([128, 8192], BF), "ALLT1": ([128, 8192], BF), "POOL": ([128, 4096], BF),
+    "INF0": ([128, 4096], BF), "INF1": ([128, 4096], BF), "INF2": ([128, 4096], BF), "INF3": ([128, 2048], BF),
+    "V": ([128, 4096], FH), "VS": ([128, 2048], FH), "VT": ([128, 2048], FH),
+    "NH": ([128, 128], BF), "IBP": ([128, 128], BF), "IBN": ([128, 128], BF), "AMX": ([128, 128], FF),
+    "YXO": ([128, 4096], FF), "SU": ([128, 1024], FH), "V16": ([128, 2048], FH),
+    "E1O": ([128, 256], FH), "E1P": ([128, 768], FH), "C16": ([128, 128], FH), "E16": ([128, 2048], BF),
+    "CSM": ([128, 128], FH), "CBT": ([128, 128], FH),
+    "G": ([128, 1024], BF), "MA": ([128, 1024], BF), "MAF": ([128, 1024], FF),
+    "B8N": ([128, 8], BF), "B8P": ([128, 8], BF),
+    "IDSO": ([128, 256], BF), "IDSP": ([128, 768], BF), "IDO": ([128, 16, 16], FF), "PAF": ([128, 128], FF), "PAL": ([128, 128], U2),
+    "Y1": ([128, 2048], FH), "Y2": ([128, 2048], FH), "EQ": ([128, 2048], BF), "IDX": ([128, 32, 32], BF),
+    "K1": ([128, 128], FF),
+    "SRA": (S6, FF), "SRB": (S6, FF), "SRM": (S6, FF), "E2O": ([128, 128], FF), "E2P": ([128, 384], FF),
+    "SI": ([128, 128], I4), "QA": ([128, 128], I4), "BB": ([128, 128], I4), "M1": ([128, 128], BF), "QAB": ([128, 128], BF),
+    "ADJ": ([128, 128], BF), "LST": ([128, 128], U2), "YLO": ([128, 128], FF),
+    "ONE": ([128, 128], BF), "IB": ([128, 128], BF), "IF": ([128, 128], FF), "TC": ([128, 1024], BF),
+    "B8a": ([128, 8], BF), "B8": ([128, 8], BF), "BE": ([128, 1024], BF), "NBE": ([128, 1024], BF),
+    "GS": ([128, 1024], BF), "PCI": ([128, 1], I4), "P16I": ([128, 1], I4),
+    "P16": ([128, 1], FF), "CE": ([128, 1], FF), "T16": ([128, 128], BF), "TC16": ([128, 16], BF), "TCN": ([128, 16], BF),
+    "TDI": ([128, 128], BF), "TD": ([128, 128], BF), "TDN": ([128, 128], BF),
+    "QC": ([128, 128], BF), "QC2": ([128, 128], BF),
+    "BP": ([128, 8], FH), "BN": ([128, 8], FH), "BXP": ([128, 128], BF), "BXN": ([128, 128], BF),
+    "WC": ([128, 8], FF), "SEL": ([128, 32], BF), "N16": ([128, 256], I4),
+}
+SCRATCH = {k: ("sbuf", s, d) for k, (s, d) in _SB.items()}
+_PS = {"PS%d" % i: ([128, 16, 32] if i == 5 else [128, 512], FF) for i in range(8)}
+for _k, (_s, _d) in _PS.items():
+    SCRATCH[_k] = ("psum", _s, _d)
+SEMAPHORES = (["cv", "cs", "ct", "cg", "dsl", "dpr", "dx0", "dx1", "dpw0", "dpw1", "dyl"] + ["dyx%d" % i for i in range(6)]
+              + ["ali%d" % i for i in range(4)] + ["arep%d" % i for i in range(4)]
+              + ["apt", "lli", "lpt", "lrep", "linf", "lids", "lst", "le1", "le2", "le3"]
+              + ["ad3%d%d" % (k, h) for k in (0, 1) for h in (0, 1)]
+              + [n + str(k) for n in ("ainf", "aids", "ast", "ae1", "ae2", "ae3") for k in range(3)])
+
+ADD, SUB, MUL = AluOpType.add, AluOpType.subtract, AluOpType.mult
+MAX, MIN = AluOpType.max, AluOpType.min
+GT, GE, LT, EQU = AluOpType.is_gt, AluOpType.is_ge, AluOpType.is_lt, AluOpType.is_equal
+SHR, AND = AluOpType.arith_shift_right, AluOpType.bitwise_and
+COPY = ActivationFunctionType.Copy
+ALL = slice(None)
+BIG = 4194304.0
+DS = (1, 2, 3)
+
+
+def rank_program(g, core, T, topo):
+    me = T.rank_of(core)
+    if me is None:
+        return
+    cores = list(T.cores)
+    nrank = len(cores)
+    Q = {"v": g.vector, "s": g.scalar, "t": g.tensor, "g": g, "y": g.sync}
+    know = {q: {} for q in Q}
+    tot = {}
+    log = {}
+
+    def V(name, *idx, ps=ALL, tag=None):
+        shape = SCRATCH[name][1][1:]
+        st = [1] * len(shape)
+        for i in range(len(shape) - 2, -1, -1):
+            st[i] = st[i + 1] * shape[i + 1]
+        full = list(idx) + [ALL] * (len(shape) - len(idx))
+        m = 1
+        for x, n, w in reversed(list(zip(full, shape, st))):
+            r = range(x, x + 1) if isinstance(x, int) else range(*x.indices(n))
+            if m == (1 << w) - 1 and r.step == 1:
+                m = ((1 << (w * len(r))) - 1) << (w * r[0])
+            else:
+                m = sum(m << (i * w) for i in r)
+        return {"ap": T[name][tuple([ps] + full)], "n": name, "m": m, "tag": tag}
+
+    def C(name, a, b, step=1, **kw):
+        return V(name, slice(a, b, step), **kw)
+
+    def need(q, evs):
+        for sem, cnt, sn in sorted(evs, key=lambda e: -len(e[2])):
+            if know[q].get(sem, 0) >= cnt:
+                continue
+            c = tot[sem] if sem[0] in "dl" else cnt
+            Q[q].wait_ge(T.sem[sem], c)
+            k = know[q]
+            for s_, c_ in list(sn.items()) + [(sem, c)]:
+                if k.get(s_, 0) < c_:
+                    k[s_] = c_
+
+    def touch(q, ins, outs):
+        evs = []
+        for kind, lst in (("r", ins), ("w", outs)):
+            for r in lst:
+                if r["n"] in _PS:
+                    d = log.setdefault(r["n"], {})
+                    for oq in list(d):
+                        if oq != q:
+                            evs.append(d[oq])
+                            del d[oq]
+                    continue
+                for e in log.get(r["n"], ()):
+                    if not e[0] & r["m"] or (kind == "r" and e[2] == "r"):
+                        continue
+                    if e[1] is not None and r["tag"] is not None and e[1] != r["tag"]:
+                        continue
+                    evs.append(e[3])
+        return evs
+
+    def note(q, ins, outs, ev):
+        for kind, lst in (("r", ins), ("w", outs)):
+            for r in lst:
+                if r["n"] in _PS:
+                    log.setdefault(r["n"], {})[q] = ev
+                    continue
+                old = log.get(r["n"], [])
+                if kind == "w":
+                    old = [e for e in old if e[0] & ~r["m"] or (r["tag"] is not None and r["tag"] != e[1])]
+                log[r["n"]] = old + [(r["m"], r["tag"], kind, ev)]
+
+    def done(q, sem, n):
+        tot[sem] = tot.get(sem, 0) + n
+        d = dict(know[q])
+        d[sem] = tot[sem]
+        return (sem, tot[sem], d)
+
+    def op(q, fn, ins, outs):
+        need(q, touch(q, ins, outs))
+        ev = done(q, "c" + q, 1)
+        fn().then_inc(T.sem["c" + q], 1)
+        note(q, ins, outs, ev)
+
+    def dma(q, sem, out, in_, ext_out=None, ext_in=None):
+        ins, outs = [in_] if in_ else [], [out] if out else []
+        need(q, touch(q, ins, outs))
+        ev = done(q, sem, 16)
+        Q[q].dma_start(out["ap"] if out else ext_out, in_["ap"] if in_ else ext_in).then_inc(T.sem[sem], 16)
+        note(q, ins, outs, ev)
+
+    def expect(sem, cnt, outs):
+        tot[sem] = tot.get(sem, 0) + cnt
+        note("net", [], outs, (sem, tot[sem], {sem: tot[sem]}))
+
+    others = [r for r in range(nrank) if r != me]
+    off = [r for r in others if topo.chip(cores[r]) != topo.chip(core)]
+    on = [r for r in others if r not in off]
+    e_off = list(topo.engines(core, cores[off[0]]))
+    e_on = [e for e in topo.engines(core, cores[on[0]]) if e not in e_off]
+    NB = len(e_off)
+    far = off[me % 2]
+    e_hand = [e_on, list(topo.engines(core, cores[on[0]]))]
+
+    def did(r):
+        rid, pid, _ = topo.addr(cores[r])
+        return DstId(rid=rid, pnc=pid)
+
+    def ecount(src):
+        return len(topo.engines(cores[src], core))
+
+    def send(r, sem, lsem, dst, src, es=None):
+        need("g", touch("g", [src], []))
+        rid, pid, _ = topo.addr(cores[r])
+        es = es or topo.engines(core, cores[r])
+        ev = done("g", lsem, len(es))
+        g.remote_dma(dst["ap"], src["ap"], T.sem[sem], T.sem[lsem], pid, rid, sum(1 << e for e in es))
+        note("g", [src], [], ev)
+
+    def send_parts(parts, lsem, x):
+        need("g", touch("g", [x], []))
+        tr = [RemoteDMATransfer(dst_ids=[did(r) for r in rs], dma_engine_mask=sum(1 << e for e in es), remote_sem=T.sem[sem],
+                                srcs=[x["ap"]], dsts=[x["ap"] for r in rs], alu_op=0) for sem, rs, es in parts]
+        ev = done("g", lsem, sum(len(es) for _, _, es in parts))
+        g.remote_dma_fused(tr, local_sem=T.sem[lsem])
+        note("g", [x], [], ev)
+
+    def send_all(sem, lsem, x):
+        send_parts([(sem, off, e_off), (sem, on, e_on)], lsem, x)
+
+    def ts(out, a, s1, s2, op0, op1=None):
+        ins = [a] + [s for s in (s1, s2) if isinstance(s, dict)]
+        x1 = s1["ap"] if isinstance(s1, dict) else s1
+        x2 = s2["ap"] if isinstance(s2, dict) else s2
+        if op1 is None:
+            op("v", lambda: g.vector.tensor_scalar(out["ap"], a["ap"], x1, None, op0), ins, [out])
+        else:
+            op("v", lambda: g.vector.tensor_scalar(out["ap"], a["ap"], x1, x2, op0, op1), ins, [out])
+
+    def tt(out, a, b, o):
+        op("v", lambda: g.vector.tensor_tensor(out["ap"], a["ap"], b["ap"], o), [a, b], [out])
+
+    def ttg(out, win, lst, b, o):
+        op("v", lambda: g.vector.tensor_tensor(out["ap"], win["ap"].indirect(lst["ap"]), b["ap"], o), [win, lst, b], [out])
+
+    def vcopy(out, a):
+        op("v", lambda: g.vector.tensor_copy(out["ap"], a["ap"]), [a], [out])
+
+    def vgather(out, win, lst):
+        op("v", lambda: g.vector.tensor_copy(out["ap"], win["ap"].indirect(lst["ap"])), [win, lst], [out])
+
+    def sgather(out, win, lst):
+        op("s", lambda: g.scalar.activation(out["ap"], win["ap"].indirect(lst["ap"]), COPY), [win, lst], [out])
+
+    def scopy(out, a, bias=0.0, scale=1.0):
+        op("s", lambda: g.scalar.activation(out["ap"], a["ap"], COPY, bias=bias, scale=scale), [a], [out])
+
+    def fill(out, c):
+        op("v", lambda: g.vector.memset(out["ap"], c), [], [out])
+
+    def mm(out, l, r, start, stop):
+        op("t", lambda: g.tensor.matmul(out["ap"], l["ap"], r["ap"], start, stop), [l, r], [out])
+
+    def iota(out, pattern, cm, small=True, base=0):
+        if small:
+            op("g", lambda: g.iota(out["ap"], pattern, base, cm, allow_small_or_imprecise_dtypes=True), [], [out])
+        else:
+            op("g", lambda: g.iota(out["ap"], pattern, base, cm), [], [out])
+
+    def afs(out, a, pattern, cmp, base, cm):
+        op("g", lambda: g.affine_select(out["ap"], a["ap"], pattern, cmp, 0.0, base, cm), [a], [out])
+
+    def blk(name, r):
+        return C(name, 2048 * r, 2048 * r + 2048)
+
+    def row(name, i, n=128):
+        return C(name, n * i, n * i + n)
+
+    dma("y", "dsl", V("SL"), None, ext_in=T.sl[:, :])
+    dma("s", "dpr", V("PR"), None, ext_in=T.prey[:, :])
+    dma("y", "dx0", C("XW", 16, 2064), None, ext_in=T.x[:, 0:2048])
+    dma("s", "dx1", C("XW", 2064, 4112), None, ext_in=T.x[:, 2048:4096])
+    fill(V("ONE"), 1.0)
+    fill(C("XW", 0, 16), 0.0)
+    fill(C("XW", 4112, 4128), 0.0)
+    fill(C("PWIN", 0, 2048), 0.0)
+    scopy(C("PWIN", 2048, 4096), C("PWIN", 0, 2048))
+    scopy(C("PWIN", 4096, 6144), C("PWIN", 0, 2048))
+    iota(V("PCI"), [[0, 1]], 1, False)
+    afs(V("B8a"), C("ONE", 0, 8), [[-16, 8]], GE, 0, 1)
+    afs(V("B8"), V("B8a"), [[16, 8]], GE, 15, -1)
+    afs(V("IB"), V("ONE"), [[-1, 128]], EQU, 0, 1)
+    iota(V("N16"), [[16, 256]], 0, False)
+    vcopy(row("LISTS", me), V("SL"))
+    send_all("ali%d" % me, "lli", row("LISTS", me))
+
+    def offsets(q):
+        ts(row("OFF", q), row("LISTS", q), 16.0 - 4096.0 * me, 4112.0, ADD, MIN)
+    offsets(me)
+    ts(V("w0"), V("PR"), 2048 * me, None, ADD)
+    ts(V("w1"), V("w0"), 7, None, SHR)
+    ts(V("w2"), V("w0"), 127, None, AND)
+    vcopy(C("PT", 512 * me, 512 * me + 256), V("w1"))
+    vcopy(C("PT", 512 * me + 256, 512 * me + 512), V("w2"))
+    send_all("apt", "lpt", row("PT", me, 512))
+    iota(V("QC"), [[0, 8], [1, 16]], 0)
+    iota(V("TC16"), [[0, 16]], 1)
+    iota(V("T16"), [[0, 128]], 16)
+    for r in others:
+        expect("ali%d" % r, NB, [row("LISTS", r)])
+    expect("apt", NB * (nrank - 1), [row("PT", r, 512) for r in others])
+    ts(V("P16I"), V("PCI"), 15, None, AND)
+    vcopy(V("P16"), V("P16I"))
+    ts(V("w3"), V("N16"), V("P16"), None, ADD)
+    ts(V("w4"), V("w3"), 127, None, AND)
+    vcopy(C("IDT", 1024, 1280), V("w4"))
+    ts(V("w4"), V("w3"), 7, None, SHR)
+    vcopy(row("IDT", 0, 256), V("w4"))
+    order = [far, off[1 - me % 2], on[0]]
+    for i, q in enumerate(order):
+        offsets(q)
+        vgather(row("REP", 2 * i, 1024), V("XW"), row("OFF", 2 * q, 64))
+        sgather(row("REP", 2 * i + 1, 1024), V("XW"), row("OFF", 2 * q + 1, 64))
+        send(q, "arep%d" % me, "lrep", blk("ALLT0", me), row("REP", i, 2048), e_on if q in on else e_off)
+    for r in others:
+        expect("arep%d" % r, NB, [blk("ALLT0", r)])
+    vgather(row("ALLT0", 2 * me, 1024), V("XW"), row("OFF", 2 * me, 64))
+    sgather(row("ALLT0", 2 * me + 1, 1024), V("XW"), row("OFF", 2 * me + 1, 64))
+    iota(V("TC"), [[0, 8], [1, 128]], -1)
+    iota(V("QC2"), [[0, 8], [1, 16]], 0, base=16)
+    iota(V("TDI"), [[-1, 128]], 0, base=128)
+    iota(V("CE"), [[0, 1]], 16)
+    fill(V("EQ"), 1.0 / 16)
+    afs(V("E16"), V("EQ"), [[-1, 128], [0, 16]], EQU, 0, 1)
+    fill(C("PWIN", 6144, 12288), 0.0)
+    for o in range(1, nrank):
+        scopy(row("IDT", o, 256), row("IDT", 0, 256), bias=32.0 * o)
+    scopy(C("PWIN", 12288, 16384), C("PWIN", 0, 4096))
+
+    for o in range(nrank):
+        for c in range(4):
+            src = row("IDT", o if c == 0 else 4, 256) if c < 2 else row("PT", 2 * o + c - 2, 256)
+            dma("y", "dpw%d" % (c // 2), C("PWIN", 4096 * o, 4096 * o + 4096, ps=slice(c, 128, 16), tag=c), src)
+    for i in range(8):
+        ts(row("BE", i), V("ONE"), C("B8", i, i + 1), 128.0, MUL, MUL)
+    ts(V("NBE"), V("BE"), -1.0, None, MUL)
+    ts(V("B8N"), V("B8"), -128.0, None, MUL)
+    ts(V("B8P"), V("B8"), 128.0, None, MUL)
+    fill(V("GS"), 0.0)
+    for i in range(8):
+        fill(C("GS", 144 * i, 144 * i + 16), 1.0)
+    ts(V("q0"), V("SL"), 4, None, SHR)
+    ts(V("q1"), V("SL"), 15, None, AND)
+    ts(V("q2"), V("SL"), 12, None, SHR)
+    ts(V("q1"), V("q1"), 256, None, MUL)
+    ts(V("q2"), V("q2"), 3840, None, MUL)
+    tt(V("q0"), V("q0"), V("q1"), ADD)
+    tt(V("q0"), V("q0"), V("q2"), ADD)
+    vcopy(V("ILST"), V("q0"))
+    for i in range(8):
+        ts(row("BXP", i, 16), C("ONE", 0, 16), C("B8", i, i + 1), 32.0, MUL, MUL)
+    ts(V("BXN"), V("BXP"), -1.0, None, MUL)
+    ts(V("BP"), V("B8"), 1024.0, None, MUL)
+    ts(V("BN"), V("B8"), -1024.0, None, MUL)
+    ts(V("TCN"), V("TC16"), -0.5, None, MUL)
+    ts(V("TC16"), V("TC16"), 0.5, None, MUL)
+    ts(V("TD"), V("TDI"), 0.125, None, MUL)
+    ts(V("TDN"), V("TDI"), -0.125, None, MUL)
+
+    banks = ("PS3", "PS4", "PS6", "PS7")
+    mychip = sorted(on + [me])
+    for n, r in enumerate([me] + on + sorted(off, key=lambda r: mychip[r % 2] != me)):
+        for i, b in enumerate(banks):
+            mm(V(b), V("IB"), row("ALLT0", 4 * r + i, 512), n == 0, n == 3)
+    for i, b in enumerate(banks):
+        if i % 2 == 0:
+            ts(row("POOL", i, 512), V(b), -128.0, None, ADD)
+        else:
+            scopy(row("POOL", i, 512), V(b), bias=-128.0)
+
+    def ranks_open():
+        for h in (0, 1):
+            mm(V("PS%d" % h), V("IB"), row("TC", h, 512), True, False)
+
+    inf = ["INF0", "INF1", "INF2", "INF3"]
+
+    def info_done(k, nxt):
+        for j in range(16):
+            mm(C("PS4", j, 512, 16), C(inf[k], j, 2048, 16), V("SEL"), True, True)
+        if nxt is not None:
+            scopy(V("IDSO"), C("PS4", 0, 256))
+            send(me ^ nxt, "aids%d" % k, "lids", row("IDSP", k, 256), V("IDSO"))
+        if nxt is not None and k > 0:
+            scopy(V("PAF"), C("PS4", 384, 512))
+            mm(C("PS7", 0, 128), V("PAF"), V("IF"), True, True)
+            vcopy(V("PAL"), C("PS7", 0, 128))
+        scopy(V("IDO", slice(0, 8)), C("PS4", 256, 384))
+        if nxt is not None:
+            scopy(V("IDO", slice(8, 16)), C("PS4", 256, 384))
+
+    def vgath(a, b, tab):
+        sgather(C("REP", a, b), blk(tab, me), C("PREYL", a // 16, b // 16))
+
+    def vsum(a, bank):
+        mm(V(bank), V("IB"), C("V", a, a + 512), True, False)
+        mm(V(bank), V("IB"), C("REP", a, a + 512), False, True)
+
+    def vround(a, bank):
+        scopy(C("V", a, a + 512), V(bank), scale=0.5, bias=768.25)
+
+    def vdve(a, b, tab):
+        ttg(C("VS", a, b), blk(tab, me), C("PREYL", a // 16, b // 16), C("V", a, b), ADD)
+        ts(C("VT", a, b), C("VS", a, b), 0.5, 768.25, MUL, ADD)
+        ts(C("YXO", a, b), C("VT", a, b), -1408.0, None, ADD)
+
+    bits = {1: 5, 2: 4, 4: 3, 8: 2}
+
+    def half(name, s, sv, k=None, kv=None):
+        ix = [ALL] * 6
+        ix[bits[s]] = sv
+        if k is not None:
+            ix[bits[k]] = kv
+        return V(name, *ix[1:])
+
+    def stage(src, dst, s, k=None, desc=False):
+        for kv in ((0, 1) if k else (None,)):
+            lo, hi = half(src, s, 0, k, kv), half(src, s, 1, k, kv)
+            if dst in ("E2O", "SI"):
+                dl, dh = C(dst, 0, 128, 2), C(dst, 1, 128, 2)
+            else:
+                dl, dh = half(dst, s, 0, k, kv), half(dst, s, 1, k, kv)
+            if desc != (kv == 1):
+                dl, dh = dh, dl
+            tt(dl, lo, hi, MIN)
+            tt(dh, lo, hi, MAX)
+
+    def merge(src, other, last, desc=False):
+        stage(src, other, 8, None, desc)
+        stage(other, src, 4, None, desc)
+        stage(src, other, 2, None, desc)
+        stage(other, last, 1, None, desc)
+
+    for k, d in enumerate(DS):
+        p = me ^ d
+        isA = me < p
+        npart = ecount(p)
+        expect("aids%d" % k, npart, [row("IDSP", k, 256)])
+        expect("ainf%d" % k, npart, [C(inf[k], 2048, 4096)])
+        expect("ast%d" % k, npart, [C("POOL", 2048, 4096)])
+        src, o16 = ("POOL", 0.0) if k == 0 else ("V16", 24576.0)
+        for h in (0, 1):
+            for j in range(16):
+                mm(row("PS2", h, 64), V("IB"), C(src, 1024 * h + j, 1024 * h + 1024, 16), j == 0, j == 15)
+        if k == 0:
+            ranks_open()
+            sgather(C("INF0", 0, 2048), V("PWIN"), V("ILST"))
+        C16 = V("C16")
+        ts(C16, C("PS2", 0, 128), -o16, None, ADD)
+        mm(C("PS6", 384, 392), C16, V("B8N"), True, True)
+        for gg in range(8):
+            mm(row("PS%d" % (gg // 4), gg % 4), row("NBE", gg), C16, False, gg % 4 == 3)
+        mm(C("PS7", 0, 128), C16, V("IB"), True, True)
+        if k == 0:
+            for c, (e, w) in enumerate(((0.0, 128.0), (1.0, 1.0), (2.0, 128.0), (3.0, 1.0))):
+                ts(C("WC", c, c + 1), V("P16"), e, w, EQU, MUL)
+            tt(C("WC", 4, 5), C("WC", 0, 1), C("WC", 1, 2), ADD)
+            tt(C("WC", 5, 6), C("WC", 2, 3), C("WC", 3, 4), ADD)
+            for c, w in enumerate((0, 1, 4, 5)):
+                ts(row("SEL", c, 8), V("B8"), C("WC", w, w + 1), None, MUL)
+        for gg in range(8):
+            ts(row("G", gg), row("PS%d" % (gg // 4), gg % 4), C("PS6", 384 + gg, 385 + gg), None, GT)
+        vcopy(C("E1O", 0, 128), C("PS7", 0, 128))
+        for gg in range(8):
+            mm(C("PS2", 128, 256), row("GS", gg), row("G", gg), gg == 0, gg == 7)
+        ts(C("E1O", 128, 256), C("PS2", 128, 256), 1.0 / 2048, None, MUL)
+        send(p, "ae1%d" % k, "le1", row("E1P", k, 256), V("E1O"))
+        if k == 0:
+            ts(V("IBP"), V("IB"), 2 * BIG, None, MUL)
+            ts(V("IBN"), V("IB"), -2 * BIG, None, MUL)
+            fill(V("NH"), -0.5)
+            info_done(0, d)
+        for i, b in enumerate(("PS5", "PS6", "PS7", "PS4")):
+            mm(V(b), C("E1O", 0, 128), row("E16", i, 512), True, True)
+            tt(row("Y1", i, 512), V(b), row("POOL", i, 512), MAX)
+        for h in (0, 1):
+            mm(V("PS%d" % h), V("ONE"), row("G", h, 512), True, True)
+        send(p, "ast%d" % k, "lst", C("POOL", 2048, 4096), C("POOL", 0, 2048))
+        send(p, "ainf%d" % k, "linf", C(inf[k], 2048, 4096), C(inf[k], 0, 2048))
+        expect("ae1%d" % k, npart, [row("E1P", k, 256)])
+        scopy(V("IDX", slice(0, 16), slice(0, 16)), row("IDSP", k, 256), scale=1.0 / 32)
+        scopy(V("IDX", slice(16, 32), slice(8, 24)), row("IDSP", k, 256), scale=1.0 / 32)
+        scopy(V("IDX", slice(0, 16), slice(16, 24)), V("IDX", slice(0, 16), slice(0, 8)))
+        scopy(V("IDX", slice(16, 32), slice(0, 8)), V("IDX", slice(0, 16), slice(8, 16)))
+        KEY = C("PS3", 0, 128)
+        mm(KEY, V("IB"), V("QC" if isA else "QC2"), True, False)
+        mm(KEY, C16, V("BXN" if isA else "BXP"), False, False)
+        mm(C("PS6", 392, 400), row("E1P", 2 * k + 1), V("B8P"), True, True)
+        for gg in range(8):
+            ts(row("MA", gg), row("PS%d" % (gg // 4), gg % 4), C("PS6", 392 + gg, 393 + gg), 32.0, EQU, MUL)
+        for j in range(16):
+            mm(C("PS3", j, 128, 16), C("Y1", j, 2048, 16), V("BP" if isA else "BN"), False, False)
+        for gg in range(8):
+            mm(C("PS2", 256 + 16 * gg, 272 + 16 * gg), row("MA", gg), row("E1P", 16 * k + gg, 16), True, True)
+        ts(V("CSM"), C("PS2", 256, 384), 1.0 / 32, None, MUL)
+        Y2B = ("PS0", "PS1", "PS4", "PS7")
+        for b in range(4):
+            mm(V(Y2B[b]), V("CSM"), row("E16", b, 512), True, True)
+        mm(C("PS6", 0, 128), V("CSM"), V("IB"), True, True)
+        scopy(V("CBT"), C("PS6", 0, 128))
+        scopy(V("MAF"), V("MA"), scale=1.0 / 32)
+        for gg in range(8):
+            for c in (0, 1):
+                mm(V("PS5", slice(gg, 16, 8), slice(0, 24)), row("MA", gg), V("IDX", slice(8 * c + gg, 32, 16), slice(0, 24)),
+                   c == 0, c == 1)
+        for b in range(4):
+            tt(row("Y2", b, 512), V(Y2B[b]), row("POOL", b, 512), MAX)
+        IW, KC = (V("IBN"), "QC") if isA else (V("IBP"), "QC2")
+        CM = C("PS6", 384, 512)
+        mm(KEY, V("CBT"), V("BXP" if isA else "BXN"), False, False)
+        mm(CM, V("IB"), V(KC), True, False)
+        mm(CM, IW, V("NH"), False, False)
+        for r in range(8):
+            tt(row("EQ", r, 256), V("PS5", ALL, slice(r, r + 16)), V("IDO"), EQU)
+            if r == 0:
+                for j in range(16):
+                    mm(C("PS3", j, 128, 16), C("Y2", j, 2048, 16), V("BN" if isA else "BP"), False, j == 15)
+            for h in (0, 1):
+                mm(CM, IW, row("EQ", 2 * r + h), False, r == 7 and h == 1)
+            if r == 6:
+                vcopy(V("K1"), KEY)
+        tt(V("SRA"), V("K1"), CM, MIN if isA else MAX)
+        if k == 0:
+            scopy(V("V"), C("XW", 16, 4112), bias=1408.0)
+            vcopy(V("IF"), V("IB"))
+        else:
+            for i, b in ((0, "PS4"), (1, "PS7"), (2, "PS0"), (3, "PS1"), (4, "PS3")):
+                vsum(512 * i, b)
+                vround(512 * i, b)
+        desc = not isA
+        stage("SRA", "SRB", 1, 2, desc)
+        stage("SRB", "SRA", 2, 4, desc)
+        stage("SRA", "SRB", 1, 4, desc)
+        stage("SRB", "SRA", 4, 8, desc)
+        stage("SRA", "SRB", 2, 8, desc)
+        stage("SRB", "SRA", 1, 8, desc)
+        merge("SRA", "SRB", "E2O", desc)
+        send(p, "ae2%d" % k, "le2", row("E2P", k), V("E2O"))
+        expect("ae2%d" % k, npart, [row("E2P", k)])
+        if k == 0:
+            vcopy(V("PREYL"), V("PR"))
+        DIF = C("PS6", 128, 256)
+        mm(DIF, V("TD" if isA else "TDN"), V("ONE"), True, False)
+        for gg in range(8):
+            mm(row("PS6", 8 + gg, 16), row("MA", gg), V("TC16" if isA else "TCN"), False, gg == 7)
+        adj = V("T16")
+        if not isA:
+            adj = V("ADJ")
+            ts(adj, DIF, -1.0, V("CE"), MUL, ADD)
+        mm(C("PS2", 384, 512), adj, V("IB"), True, False)
+        if isA:
+            ts(V("SRB"), V("E2O"), -3000000.0, 2 * BIG, LT, MUL)
+            tt(V("SRM"), V("E2O"), V("SRB"), ADD)
+            merge("SRM", "SRB", "SRM")
+            ts(V("SRB"), V("SRM"), 3000000.0, -2 * BIG, LT, MUL)
+            tt(V("AMX"), V("SRM"), V("SRB"), ADD)
+        for gg in range(8):
+            mm(row("PS7", 8 + gg, 16), row("MAF", gg), row("E2P", 8 * k + gg, 16), True, True)
+        if k == 2:
+            for i, b in ((5, "PS0"), (6, "PS1")):
+                vsum(512 * i, b)
+                vround(512 * i, b)
+        if isA:
+            tt(V("SRA"), V("SRM"), C("PS7", 128, 256), MIN)
+            merge("SRA", "SRB", "SRA")
+            tt(V("SI"), V("SRA"), V("AMX"), MAX)
+        else:
+            tt(V("SRA"), V("E2O"), C("PS7", 128, 256), MAX)
+            merge("SRA", "SRB", "SI")
+        ts(V("BB"), V("SI"), 4, 1, SHR, AND)
+        ts(V("QA"), V("SI"), 15, None, AND)
+        tt(V("M1"), V("BB"), DIF, MUL)
+        vcopy(V("QAB"), V("QA"))
+        mm(C("PS2", 384, 512), V("M1"), V("IB"), False, False)
+        mm(C("PS2", 384, 512), V("QAB"), V("IB"), False, True)
+        vcopy(V("LST"), C("PS2", 384, 512))
+        tab = "ALLT0" if k == 1 else "ALLT1"
+        m0 = 2048 * me
+        if k == 2:
+            vgather(C(tab, m0, m0 + 1024), V("POOL"), C("LST", 0, 64))
+            sgather(C(tab, m0 + 1024, m0 + 2048), V("POOL"), C("LST", 64, 128))
+        else:
+            for h in (0, 1):
+                a = m0 + 1024 * h
+                vgather(C(tab, a, a + 512), V("POOL"), C("LST", 64 * h, 64 * h + 32))
+                sgather(C(tab, a + 512, a + 1024), V("POOL"), C("LST", 64 * h + 32, 64 * h + 64))
+                send_parts([("ad3%d%d" % (k, h), [far], e_off), ("ae3%d" % k, on, e_on)], "le3", C(tab, a, a + 1024))
+            piece = [C(tab, 2048 * far + 1024 * h, 2048 * far + 1024 * h + 1024) for h in (0, 1)]
+            for h in (0, 1):
+                expect("ad3%d%d" % (k, h), NB, [piece[h]])
+            for h in (0, 1):
+                send(on[0], "ae3%d" % k, "le3", piece[h], piece[h], e_hand[h])
+            expect("ae3%d" % k, 2 * len(e_on) + len(e_hand[0]) + len(e_hand[1]), [blk(tab, r) for r in others if r != far])
+        if k < 2:
+            vcopy(C("V16", 0, 1024), C(tab, m0, m0 + 1024))
+            sgather(C(inf[k + 1], 0, 2048), V(inf[k]), V("LST"))
+            late = ((5, "PS0"), (6, "PS1"), (7, "PS3")) if k > 0 else ()
+            for i, b in late:
+                vsum(512 * i, b)
+            info_done(k + 1, DS[k + 1])
+            for i, b in late:
+                vround(512 * i, b)
+            ranks_open()
+            ttg(V("SU"), V(tab), C("PAL", 0, 64), C("V16", 0, 1024), ADD)
+            sgather(C("REP", 4096, 5120), V(tab), C("PAL", 64, 128))
+            for h in (0, 1):
+                mm(V("PS%d" % (6 + h)), V("IB"), C(tab, m0 + 1024 + 512 * h, m0 + 1536 + 512 * h), True, False)
+            for h in (0, 1):
+                mm(V("PS%d" % (6 + h)), V("IB"), row("REP", 8 + h, 512), False, True)
+            ts(C("V16", 0, 1024), V("SU"), 0.5, 1536.25, MUL, ADD)
+            ts(row("V16", 2, 512), V("PS6"), 0.5, 1536.25, MUL, ADD)
+            scopy(row("V16", 3, 512), V("PS7"), scale=0.5, bias=1536.25)
+            for a in (0, 1024, 2048, 3072):
+                vgath(a, a + 1024, tab)
+            ts(C("POOL", 0, 2048), V("V16"), -1536.0, None, ADD)
+        else:
+            def put(i, a, b):
+                dma("y", "dyx%d" % i, None, C("YXO", a, b), ext_out=T.yx[:, a:b])
+
+            def last(a):
+                vround(a, "PS%d" % (a // 512 % 4))
+                scopy(C("YXO", a, a + 512), C("V", a, a + 512), bias=-1408.0)
+            vsum(3584, "PS4")
+            vgath(2048, 3072, tab)
+            vround(3584, "PS4")
+            vgath(3072, 4096, tab)
+            sgather(C("INF3", 1536, 2048), V(inf[k]), C("LST", 96, 128))
+            for a in range(2048, 4096, 512):
+                vsum(a, "PS%d" % (a // 512 % 4))
+            vdve(0, 1024, tab)
+            put(0, 0, 1024)
+            vgather(C("INF3", 0, 1536), V(inf[k]), C("LST", 0, 96))
+            last(2048)
+            last(2560)
+            put(1, 2048, 3072)
+            vdve(1024, 1536, tab)
+            put(2, 1024, 1536)
+            info_done(3, None)
+            mm(C("PS7", 0, 128), V("IDO", slice(0, 8)), V("IF"), True, True)
+            scopy(V("YLO"), C("PS7", 0, 128))
+            dma("y", "dyl", None, V("YLO"), ext_out=T.yl[:, :])
+            vdve(1536, 2048, tab)
+            put(3, 1536, 2048)
+            last(3072)
+            put(4, 3072, 3584)
+            last(3584)
+            put(5, 3584, 4096)
+    for sem in sorted(tot):
+        if know["g"].get(sem, 0) < tot[sem]:
+            g.wait_ge(T.sem[sem], tot[sem])

@@ -3,52 +3,49 @@ from concourse.mybir import AluOpType, ActivationFunctionType
 
 BF, FH, FF, I4, U2 = "bfloat16", "float16", "float32", "int32", "uint16"
 S6 = [128, 8, 2, 2, 2, 2]
+CFG = {"NS1": 2, "NV": 576, "PV": 1152, "EQ0": 4}
+XZ = 13328
 _SB = {
-    "SL": ([128, 128], I4), "PR": ([128, 256], I4), "XW": ([128, 4128], BF),
-    "LISTS": ([128, 512], U2), "OFF": ([128, 512], U2), "REP": ([128, 6144], BF),
-    "PREYL": ([128, 256], U2), "ILST": ([128, 128], U2),
-    "q0": ([128, 128], I4), "q1": ([128, 128], I4), "q2": ([128, 128], I4),
-    "w0": ([128, 256], I4), "w1": ([128, 256], I4), "w2": ([128, 256], I4), "w3": ([128, 256], I4), "w4": ([128, 256], I4),
-    "PT": ([128, 2048], BF), "IDT": ([128, 1280], BF), "PWIN": ([128, 16384], BF),
-    "ALLT0": ([128, 8192], BF), "ALLT1": ([128, 8192], BF), "POOL": ([128, 4096], BF),
-    "INF0": ([128, 4096], BF), "INF1": ([128, 4096], BF), "INF2": ([128, 4096], BF), "INF3": ([128, 2048], BF),
-    "V": ([128, 4096], FH), "VS": ([128, 2048], FH), "VT": ([128, 2048], FH),
-    "NH": ([128, 128], BF), "IBP": ([128, 128], BF), "IBN": ([128, 128], BF), "AMX": ([128, 128], FF),
-    "YXO": ([128, 4096], FF), "SU": ([128, 1024], FH), "V16": ([128, 2048], FH),
-    "E1O": ([128, 256], FH), "E1P": ([128, 768], FH), "C16": ([128, 128], FH), "E16": ([128, 2048], BF),
-    "CSM": ([128, 128], FH), "CBT": ([128, 128], FH),
-    "G": ([128, 1024], BF), "MA": ([128, 1024], BF), "MAF": ([128, 1024], FF),
-    "B8N": ([128, 8], BF), "B8P": ([128, 8], BF),
-    "IDSO": ([128, 256], BF), "IDSP": ([128, 768], BF), "IDO": ([128, 16, 16], FF), "PAF": ([128, 128], FF), "PAL": ([128, 128], U2),
-    "Y1": ([128, 2048], FH), "Y2": ([128, 2048], FH), "EQ": ([128, 2048], BF), "IDX": ([128, 32, 32], BF),
-    "K1": ([128, 128], FF),
-    "SRA": (S6, FF), "SRB": (S6, FF), "SRM": (S6, FF), "E2O": ([128, 128], FF), "E2P": ([128, 384], FF),
-    "SI": ([128, 128], I4), "QA": ([128, 128], I4), "BB": ([128, 128], I4), "M1": ([128, 128], BF), "QAB": ([128, 128], BF),
-    "ADJ": ([128, 128], BF), "LST": ([128, 128], U2), "YLO": ([128, 128], FF),
-    "ONE": ([128, 128], BF), "IB": ([128, 128], BF), "IF": ([128, 128], FF), "TC": ([128, 1024], BF),
-    "B8a": ([128, 8], BF), "B8": ([128, 8], BF), "BE": ([128, 1024], BF), "NBE": ([128, 1024], BF),
-    "GS": ([128, 1024], BF), "PCI": ([128, 1], I4), "P16I": ([128, 1], I4),
-    "P16": ([128, 1], FF), "CE": ([128, 1], FF), "T16": ([128, 128], BF), "TC16": ([128, 16], BF), "TCN": ([128, 16], BF),
-    "TDI": ([128, 128], BF), "TD": ([128, 128], BF), "TDN": ([128, 128], BF),
-    "QC": ([128, 128], BF), "QC2": ([128, 128], BF),
-    "BP": ([128, 8], FH), "BN": ([128, 8], FH), "BXP": ([128, 128], BF), "BXN": ([128, 128], BF),
-    "WC": ([128, 8], FF), "SEL": ([128, 32], BF), "N16": ([128, 256], I4),
+    "SL": ([128, 128], I4), "PR": ([128, 256], I4), "LISTS": ([128, 512], U2), "LF": ([128, 512], FF), "OFF": ([128, 512], U2),
+    "XS": ([128, 3072], BF), "XW": ([128, 16384], BF), "X0": ([128, 4096], BF),
+    "PT": ([128, 2, 4, 256], BF), "IDT": ([128, 4, 4, 256], BF), "PREYX": ([128, 256], U2), "XOC": ([128, 256], BF),
+    "DI": ([128, 128], I4), "q0": ([128, 128], I4), "q1": ([128, 128], I4), "ILST": ([128, 128], U2),
+    "w1": ([128, 256], I4), "w2": ([128, 256], I4), "IDS": ([128, 8, 16], BF),
+    "TAB": ([128, 8192], BF), "POOL": ([128, 4096], BF), "INF0": ([128, 4096], BF), "INF1": ([128, 4096], BF),
+    "H0": ([128, 4096], BF), "H1": ([128, 4096], BF), "REP": ([128, 2048], BF), "PP": ([128, 4096], FH),
+    "SU": ([128, 2048], FH), "V16": ([128, 2048], FH), "OUT": ([128, 3072], FH), "RCV": ([128, 4096], FH),
+    "YXO": ([128, 4096], FF), "YL": ([128, 512], FF),
+    "C16": ([128, 128], FH), "CS": ([128, 128], FH), "CSM": ([128, 128], FH), "E4": ([128, 512], BF), "E4N": ([128, 512], BF),
+    "G": ([128, 1024], BF), "M": ([128, 1024], BF), "MAF": ([128, 512], FF),
+    "IDO": ([128, 8, 16], FF), "IDX": ([128, 2, 2, 4, 32], BF), "PAL": ([128, 128], U2),
+    "Y1": ([128, 1024], FF), "Y1H": ([128, 2048], FH), "Y2": ([128, 2048], FH), "EQ": ([128, 1024], BF),
+    "K1": ([128, 64], FF), "T1": ([128, 64], FF),
+    "SRA": (S6, FF), "SRB": (S6, FF), "SI": (S6, I4), "QA": ([128, 128], I4), "BB": ([128, 128], I4),
+    "ZA": ([128, 4, 4, 32], BF), "ZB": ([128, 8, 240], BF), "LST": ([128, 128], U2),
+    "ONE": ([128, 128], BF), "IB": ([128, 128], BF), "IF": ([128, 128], FF), "BCQ": ([128, 128], FF), "TC": ([128, 1024], BF),
+    "IBP": ([128, 128], BF), "IBN": ([128, 128], BF), "IBQ": ([128, 128], BF), "IBH": ([128, 128], BF),
+    "PX": ([128, 4, 128], BF), "ZS": ([128, 224], BF), "ZQ": ([128, 224], BF),
+    "B8a": ([128, 8], BF), "B8": ([128, 8], BF), "B8N": ([128, 8], BF), "NBE": ([128, 1024], BF),
+    "PCI": ([128, 1], I4), "pi": ([128, 4], I4), "P16": ([128, 1], FF), "COL": ([128, 8], FF), "WC": ([128, 16], FF),
+    "T16": ([128, 2, 128], BF), "DB": ([128, 128], BF), "TCC": ([128, 32], BF), "QK": ([128, 128], BF),
+    "FQ": ([128, 4, 32], BF), "FN": ([128, 4, 32], BF), "QBIG": ([128, 128], FF), "NEG": ([128, 2], FF),
+    "C32": ([128, 2, 64], BF), "bx": ([128, 64], BF), "BX": ([128, 3, 8, 16], BF),
+    "BP1": ([128, 3, 8], FF), "BP2": ([128, 3, 8], FH), "BP3": ([128, 3, 8], FH),
+    "B8K": ([128, 2, 8], BF), "SEL": ([128, 3, 12], BF), "WB": ([128, 144], BF), "WY": ([128, 144], BF),
 }
 SCRATCH = {k: ("sbuf", s, d) for k, (s, d) in _SB.items()}
-_PS = {"PS%d" % i: ([128, 16, 32] if i == 5 else [128, 512], FF) for i in range(8)}
+_PS = {"PS%d" % i: ([128, 16, 32] if i in (4, 5) else [128, 32, 16], FF) for i in range(8)}
 for _k, (_s, _d) in _PS.items():
     SCRATCH[_k] = ("psum", _s, _d)
-SEMAPHORES = (["cv", "cs", "ct", "cg", "dsl", "dpr", "dx0", "dx1", "dpw0", "dpw1", "dyl"] + ["dyx%d" % i for i in range(6)]
-              + ["ali%d" % i for i in range(4)] + ["arep%d" % i for i in range(4)]
-              + ["apt", "lli", "lpt", "lrep", "linf", "lids", "lst", "le1", "le2", "le3"]
-              + ["ad3%d%d" % (k, h) for k in (0, 1) for h in (0, 1)]
-              + [n + str(k) for n in ("ainf", "aids", "ast", "ae1", "ae2", "ae3") for k in range(3)])
+SEMAPHORES = (["cv", "cs", "ct", "cg", "dsl", "dpr", "dcp", "dpw", "dyl", "ali", "apt", "ayl", "lli", "lpt", "lx", "lout", "lyl"]
+              + [n + str(i) for n in ("dx", "ax", "aout", "dyx") for i in range(4)]
+              + [n + str(k) for n in ("dpool", "dinf", "dtab0", "dtab1") for k in range(3)])
 
 ADD, SUB, MUL = AluOpType.add, AluOpType.subtract, AluOpType.mult
 MAX, MIN = AluOpType.max, AluOpType.min
-GT, GE, LT, EQU = AluOpType.is_gt, AluOpType.is_ge, AluOpType.is_lt, AluOpType.is_equal
+GT, GE, LT, EQU, NE = AluOpType.is_gt, AluOpType.is_ge, AluOpType.is_lt, AluOpType.is_equal, AluOpType.not_equal
 SHR, AND = AluOpType.arith_shift_right, AluOpType.bitwise_and
-COPY = ActivationFunctionType.Copy
+COPY, RELU, ABS = ActivationFunctionType.Copy, ActivationFunctionType.Relu, ActivationFunctionType.Abs
 ALL = slice(None)
 BIG = 4194304.0
 DS = (1, 2, 3)
@@ -65,7 +62,7 @@ def rank_program(g, core, T, topo):
     tot = {}
     log = {}
 
-    def V(name, *idx, ps=ALL, tag=None):
+    def V(name, *idx, ps=ALL):
         shape = SCRATCH[name][1][1:]
         st = [1] * len(shape)
         for i in range(len(shape) - 2, -1, -1):
@@ -78,7 +75,7 @@ def rank_program(g, core, T, topo):
                 m = ((1 << (w * len(r))) - 1) << (w * r[0])
             else:
                 m = sum(m << (i * w) for i in r)
-        return {"ap": T[name][tuple([ps] + full)], "n": name, "m": m, "tag": tag}
+        return {"ap": T[name][tuple([ps] + full)], "n": name, "m": m, "p": sum(1 << i for i in range(*ps.indices(128)))}
 
     def C(name, a, b, step=1, **kw):
         return V(name, slice(a, b, step), **kw)
@@ -106,11 +103,8 @@ def rank_program(g, core, T, topo):
                             del d[oq]
                     continue
                 for e in log.get(r["n"], ()):
-                    if not e[0] & r["m"] or (kind == "r" and e[2] == "r"):
-                        continue
-                    if e[1] is not None and r["tag"] is not None and e[1] != r["tag"]:
-                        continue
-                    evs.append(e[3])
+                    if e[0] & r["m"] and e[1] & r["p"] and not (kind == "r" and e[2] == "r"):
+                        evs.append(e[3])
         return evs
 
     def note(q, ins, outs, ev):
@@ -121,8 +115,10 @@ def rank_program(g, core, T, topo):
                     continue
                 old = log.get(r["n"], [])
                 if kind == "w":
-                    old = [e for e in old if e[0] & ~r["m"] or (r["tag"] is not None and r["tag"] != e[1])]
-                log[r["n"]] = old + [(r["m"], r["tag"], kind, ev)]
+                    old = [e for e in old if e[0] & ~r["m"] or e[1] & ~r["p"]]
+                else:
+                    old = [e for e in old if e[:3] != (r["m"], r["p"], "r") or e[3][0] != ev[0]]
+                log[r["n"]] = old + [(r["m"], r["p"], kind, ev)]
 
     def done(q, sem, n):
         tot[sem] = tot.get(sem, 0) + n
@@ -149,38 +145,29 @@ def rank_program(g, core, T, topo):
 
     others = [r for r in range(nrank) if r != me]
     off = [r for r in others if topo.chip(cores[r]) != topo.chip(core)]
+    off.sort(key=lambda r: topo.die(cores[r]) != topo.die(core))
     on = [r for r in others if r not in off]
     e_off = list(topo.engines(core, cores[off[0]]))
     e_on = [e for e in topo.engines(core, cores[on[0]]) if e not in e_off]
     NB = len(e_off)
-    far = off[me % 2]
-    e_hand = [e_on, list(topo.engines(core, cores[on[0]]))]
 
     def did(r):
         rid, pid, _ = topo.addr(cores[r])
         return DstId(rid=rid, pnc=pid)
 
-    def ecount(src):
-        return len(topo.engines(cores[src], core))
-
-    def send(r, sem, lsem, dst, src, es=None):
-        need("g", touch("g", [src], []))
-        rid, pid, _ = topo.addr(cores[r])
-        es = es or topo.engines(core, cores[r])
-        ev = done("g", lsem, len(es))
-        g.remote_dma(dst["ap"], src["ap"], T.sem[sem], T.sem[lsem], pid, rid, sum(1 << e for e in es))
-        note("g", [src], [], ev)
-
-    def send_parts(parts, lsem, x):
-        need("g", touch("g", [x], []))
+    def send(parts, lsem):
+        need("g", touch("g", [p[3] for p in parts], []))
         tr = [RemoteDMATransfer(dst_ids=[did(r) for r in rs], dma_engine_mask=sum(1 << e for e in es), remote_sem=T.sem[sem],
-                                srcs=[x["ap"]], dsts=[x["ap"] for r in rs], alu_op=0) for sem, rs, es in parts]
-        ev = done("g", lsem, sum(len(es) for _, _, es in parts))
+                                srcs=[x["ap"]], dsts=[y["ap"] for r in rs], alu_op=0) for sem, rs, es, x, y in parts]
+        ev = done("g", lsem, sum(len(p[2]) for p in parts))
         g.remote_dma_fused(tr, local_sem=T.sem[lsem])
-        note("g", [x], [], ev)
+        note("g", [p[3] for p in parts], [], ev)
 
     def send_all(sem, lsem, x):
-        send_parts([(sem, off, e_off), (sem, on, e_on)], lsem, x)
+        send([(sem, off, e_off, x, x), (sem, on, e_on, x, x)], lsem)
+
+    def send_to(r, sem, lsem, x, y):
+        send([(sem, [r], e_on if r in on else e_off, x, y)], lsem)
 
     def ts(out, a, s1, s2, op0, op1=None):
         ins = [a] + [s for s in (s1, s2) if isinstance(s, dict)]
@@ -206,8 +193,11 @@ def rank_program(g, core, T, topo):
     def sgather(out, win, lst):
         op("s", lambda: g.scalar.activation(out["ap"], win["ap"].indirect(lst["ap"]), COPY), [win, lst], [out])
 
-    def scopy(out, a, bias=0.0, scale=1.0):
-        op("s", lambda: g.scalar.activation(out["ap"], a["ap"], COPY, bias=bias, scale=scale), [a], [out])
+    def act(out, a, fn=COPY, bias=0.0, scale=1.0):
+        ins = [a] + [s for s in (bias, scale) if isinstance(s, dict)]
+        b = bias["ap"] if isinstance(bias, dict) else bias
+        s = scale["ap"] if isinstance(scale, dict) else scale
+        op("s", lambda: g.scalar.activation(out["ap"], a["ap"], fn, bias=b, scale=s), ins, [out])
 
     def fill(out, c):
         op("v", lambda: g.vector.memset(out["ap"], c), [], [out])
@@ -224,390 +214,486 @@ def rank_program(g, core, T, topo):
     def afs(out, a, pattern, cmp, base, cm):
         op("g", lambda: g.affine_select(out["ap"], a["ap"], pattern, cmp, 0.0, base, cm), [a], [out])
 
-    def blk(name, r):
-        return C(name, 2048 * r, 2048 * r + 2048)
+    def row(name, i, n=128, **kw):
+        return C(name, n * i, n * i + n, **kw)
 
-    def row(name, i, n=128):
-        return C(name, n * i, n * i + n)
+    def pb(b, n=32):
+        return slice(n * b, n * b + n)
 
+    def bank(name, a=0, b=512, ps=ALL):
+        w = SCRATCH[name][1][2]
+        if b - a < w:
+            return V(name, a // w, slice(a % w, a % w + b - a), ps=ps)
+        return V(name, slice(a // w, b // w), ps=ps)
+
+    def grp(gg):
+        return bank("PS%d" % (gg // 4), 128 * (gg % 4), 128 * (gg % 4) + 128)
+
+    def xcol(o, ps=ALL):
+        return C("XW", 16 + 4096 * o, 1040 + 4096 * o, ps=ps)
+
+    def swap(sem, dst, src, e, n):
+        w = 64 if e == 2 else 32
+        for b in range(128 // w):
+            o = b ^ (e * 32 // w)
+            dma("y", sem, C(dst[0], dst[1], dst[1] + n, ps=pb(b, w)), C(src[0], src[1], src[1] + n, ps=pb(o, w)))
+
+    AS = [[r for r in range(nrank) if r < r ^ d] for d in DS]
+    BS = [[r ^ d for r in a] for a, d in zip(AS, DS)]
+    PI = [[2 * r + w for r in a + b for w in (0, 1)] for a, b in zip(AS, BS)]
+    NS1, NV, PV, EQ0 = CFG["NS1"], CFG["NV"], CFG["PV"], CFG["EQ0"]
+
+    order = off + on
     dma("y", "dsl", V("SL"), None, ext_in=T.sl[:, :])
-    dma("s", "dpr", V("PR"), None, ext_in=T.prey[:, :])
-    dma("y", "dx0", C("XW", 16, 2064), None, ext_in=T.x[:, 0:2048])
-    dma("s", "dx1", C("XW", 2064, 4112), None, ext_in=T.x[:, 2048:4096])
+    for n, q in enumerate(order + [me]):
+        for c in range(4):
+            dst = C("XS", 1024 * n, 1024 * n + 1024, ps=pb(c)) if q != me else xcol(me, pb(c))
+            dma("ys"[c % 2], "dx%d" % n, dst, None, ext_in=T.x[32 * q:32 * q + 32, 1024 * c:1024 * c + 1024])
+        if n == 1:
+            dma("s", "dpr", V("PR"), None, ext_in=T.prey[:, :])
     fill(V("ONE"), 1.0)
-    fill(C("XW", 0, 16), 0.0)
-    fill(C("XW", 4112, 4128), 0.0)
-    fill(C("PWIN", 0, 2048), 0.0)
-    scopy(C("PWIN", 2048, 4096), C("PWIN", 0, 2048))
-    scopy(C("PWIN", 4096, 6144), C("PWIN", 0, 2048))
+    fill(C("XW", 1040, 4112), 0.0)
     iota(V("PCI"), [[0, 1]], 1, False)
+    afs(V("IB"), V("ONE"), [[-1, 128]], EQU, 0, 1)
     afs(V("B8a"), C("ONE", 0, 8), [[-16, 8]], GE, 0, 1)
     afs(V("B8"), V("B8a"), [[16, 8]], GE, 15, -1)
-    afs(V("IB"), V("ONE"), [[-1, 128]], EQU, 0, 1)
-    iota(V("N16"), [[16, 256]], 0, False)
+    fill(V("E4N"), 1.0 / 16)
+    fill(V("C32", 0), 32.0)
+    fill(V("C32", 1), -32.0)
+    fill(C("XW", 0, 16), 0.0)
+    afs(V("E4"), V("E4N"), [[-1, 128], [0, 4]], EQU, 0, 1)
     vcopy(row("LISTS", me), V("SL"))
-    send_all("ali%d" % me, "lli", row("LISTS", me))
-
-    def offsets(q):
-        ts(row("OFF", q), row("LISTS", q), 16.0 - 4096.0 * me, 4112.0, ADD, MIN)
-    offsets(me)
-    ts(V("w0"), V("PR"), 2048 * me, None, ADD)
-    ts(V("w1"), V("w0"), 7, None, SHR)
-    ts(V("w2"), V("w0"), 127, None, AND)
-    vcopy(C("PT", 512 * me, 512 * me + 256), V("w1"))
-    vcopy(C("PT", 512 * me + 256, 512 * me + 512), V("w2"))
-    send_all("apt", "lpt", row("PT", me, 512))
-    iota(V("QC"), [[0, 8], [1, 16]], 0)
-    iota(V("TC16"), [[0, 16]], 1)
-    iota(V("T16"), [[0, 128]], 16)
+    send_all("ali", "lli", row("LISTS", me))
+    for n, q in enumerate(order):
+        send_to(q, "ax%d" % me, "lx", row("XS", n, 1024), xcol(me))
+    expect("ali", NB * (nrank - 1), [row("LISTS", r) for r in others])
     for r in others:
-        expect("ali%d" % r, NB, [row("LISTS", r)])
-    expect("apt", NB * (nrank - 1), [row("PT", r, 512) for r in others])
-    ts(V("P16I"), V("PCI"), 15, None, AND)
-    vcopy(V("P16"), V("P16I"))
-    ts(V("w3"), V("N16"), V("P16"), None, ADD)
-    ts(V("w4"), V("w3"), 127, None, AND)
-    vcopy(C("IDT", 1024, 1280), V("w4"))
-    ts(V("w4"), V("w3"), 7, None, SHR)
-    vcopy(row("IDT", 0, 256), V("w4"))
-    order = [far, off[1 - me % 2], on[0]]
-    for i, q in enumerate(order):
-        offsets(q)
-        vgather(row("REP", 2 * i, 1024), V("XW"), row("OFF", 2 * q, 64))
-        sgather(row("REP", 2 * i + 1, 1024), V("XW"), row("OFF", 2 * q + 1, 64))
-        send(q, "arep%d" % me, "lrep", blk("ALLT0", me), row("REP", i, 2048), e_on if q in on else e_off)
-    for r in others:
-        expect("arep%d" % r, NB, [blk("ALLT0", r)])
-    vgather(row("ALLT0", 2 * me, 1024), V("XW"), row("OFF", 2 * me, 64))
-    sgather(row("ALLT0", 2 * me + 1, 1024), V("XW"), row("OFF", 2 * me + 1, 64))
-    iota(V("TC"), [[0, 8], [1, 128]], -1)
-    iota(V("QC2"), [[0, 8], [1, 16]], 0, base=16)
-    iota(V("TDI"), [[-1, 128]], 0, base=128)
-    iota(V("CE"), [[0, 1]], 16)
-    fill(V("EQ"), 1.0 / 16)
-    afs(V("E16"), V("EQ"), [[-1, 128], [0, 16]], EQU, 0, 1)
-    fill(C("PWIN", 6144, 12288), 0.0)
-    for o in range(1, nrank):
-        scopy(row("IDT", o, 256), row("IDT", 0, 256), bias=32.0 * o)
-    scopy(C("PWIN", 12288, 16384), C("PWIN", 0, 4096))
-
-    for o in range(nrank):
-        for c in range(4):
-            src = row("IDT", o if c == 0 else 4, 256) if c < 2 else row("PT", 2 * o + c - 2, 256)
-            dma("y", "dpw%d" % (c // 2), C("PWIN", 4096 * o, 4096 * o + 4096, ps=slice(c, 128, 16), tag=c), src)
+        expect("ax%d" % r, NB, [xcol(r)])
+    act(C("XW", 5136, 8208), C("XW", 1040, 4112))
+    act(C("XW", 9232, 12304), C("XW", 1040, 4112))
+    act(C("XW", XZ, 16384), C("XW", 1040, 1040 + 16384 - XZ))
+    act(V("ZB"), C("XW", 1040, 1040 + 1920))
+    vcopy(V("IF"), V("IB"))
+    fill(V("ZS"), 0.0)
+    fill(V("ZQ"), 0.0)
+    for c in range(4):
+        vcopy(row("BCQ", c, 32), row("IF", me, 32))
+        vcopy(C("ZS", 96, 128, ps=pb(c)), row("IB", c, 32, ps=pb(c)))
+    vcopy(C("ZQ", 96, 128), row("IB", me, 32))
+    ts(C("pi", 0, 1), V("PCI"), 15, None, AND)
+    ts(C("pi", 1, 2), V("PCI"), 5, None, SHR)
+    ts(C("pi", 2, 3), V("PCI"), 6, None, SHR)
+    ts(C("pi", 3, 4), V("PCI"), 5, 1, SHR, AND)
+    vcopy(V("P16"), C("pi", 0, 1))
+    ts(C("COL", 0, 1), C("pi", 1, 2), -1024.0, 16.0, MUL, ADD)
+    ts(C("COL", 1, 2), C("pi", 1, 2), 2048.0, None, MUL)
+    ts(C("COL", 2, 3), C("pi", 2, 3), -8192.0, 4096.0, MUL, ADD)
+    ts(C("COL", 3, 4), C("pi", 3, 4), -4096.0, 2048.0, MUL, ADD)
     for i in range(8):
-        ts(row("BE", i), V("ONE"), C("B8", i, i + 1), 128.0, MUL, MUL)
-    ts(V("NBE"), V("BE"), -1.0, None, MUL)
+        ts(row("NBE", i), V("ONE"), C("B8", i, i + 1), -128.0, MUL, MUL)
     ts(V("B8N"), V("B8"), -128.0, None, MUL)
-    ts(V("B8P"), V("B8"), 128.0, None, MUL)
-    fill(V("GS"), 0.0)
-    for i in range(8):
-        fill(C("GS", 144 * i, 144 * i + 16), 1.0)
-    ts(V("q0"), V("SL"), 4, None, SHR)
-    ts(V("q1"), V("SL"), 15, None, AND)
-    ts(V("q2"), V("SL"), 12, None, SHR)
-    ts(V("q1"), V("q1"), 256, None, MUL)
-    ts(V("q2"), V("q2"), 3840, None, MUL)
-    tt(V("q0"), V("q0"), V("q1"), ADD)
-    tt(V("q0"), V("q0"), V("q2"), ADD)
-    vcopy(V("ILST"), V("q0"))
-    for i in range(8):
-        ts(row("BXP", i, 16), C("ONE", 0, 16), C("B8", i, i + 1), 32.0, MUL, MUL)
-    ts(V("BXN"), V("BXP"), -1.0, None, MUL)
-    ts(V("BP"), V("B8"), 1024.0, None, MUL)
-    ts(V("BN"), V("B8"), -1024.0, None, MUL)
-    ts(V("TCN"), V("TC16"), -0.5, None, MUL)
-    ts(V("TC16"), V("TC16"), 0.5, None, MUL)
-    ts(V("TD"), V("TDI"), 0.125, None, MUL)
-    ts(V("TDN"), V("TDI"), -0.125, None, MUL)
+    ts(V("w1"), V("PR"), 1920, None, AND)
+    ts(V("w2"), V("PR"), 127, None, AND)
+    vcopy(V("PT", 0, me), V("w1"))
+    vcopy(V("PT", 1, me), V("w2"))
+    for c in (0, 1):
+        send_all("apt", "lpt", V("PT", c, me))
+    expect("apt", 2 * NB * (nrank - 1), [V("PT", ALL, r) for r in others])
 
-    banks = ("PS3", "PS4", "PS6", "PS7")
-    mychip = sorted(on + [me])
-    for n, r in enumerate([me] + on + sorted(off, key=lambda r: mychip[r % 2] != me)):
-        for i, b in enumerate(banks):
-            mm(V(b), V("IB"), row("ALLT0", 4 * r + i, 512), n == 0, n == 3)
-    for i, b in enumerate(banks):
-        if i % 2 == 0:
-            ts(row("POOL", i, 512), V(b), -128.0, None, ADD)
-        else:
-            scopy(row("POOL", i, 512), V(b), bias=-128.0)
+    def weights(k):
+        for side, rs in enumerate((AS[k], BS[k])):
+            s = 32 * (rs[1] - rs[0])
+            afs(V("bx"), V("C32", side), [[-s, 2], [-16, 2], [0, 16]], GE, -32 * rs[0], 1)
+            afs(V("BX", k, slice(4 * side, 4 * side + 4)), V("bx"), [[s, 2], [16, 2], [0, 16]], GE, 32 * rs[0] + 15, -1)
+    iota(V("QK"), [[16, 2], [0, 4], [1, 16]], 0)
+    weights(0)
+    iota(V("TC"), [[0, 8], [1, 128]], -1)
+    iota(V("IDT", 0), [[0, 4], [1, 256]], 0)
+    for c in range(6):
+        ts(C("WC", c, c + 1), V("P16"), float(c), None, EQU)
+    for a in (0, 1):
+        fill(V("IDT", 1, slice(2 * a, 2 * a + 2)), float(a))
+        fill(V("IDT", 2, slice(a, 4, 2)), float(a))
+    ts(C("WC", 6, 7), C("WC", 1, 2), C("COL", 2, 3), C("WC", 3, 4), MUL, ADD)
+    ts(C("WC", 7, 8), C("WC", 2, 3), C("COL", 3, 4), C("WC", 4, 5), MUL, ADD)
+    ts(C("WC", 8, 9), C("WC", 1, 2), 8192.0, C("WC", 5, 6), MUL, ADD)
+    ts(C("WC", 11, 12), C("WC", 1, 2), 2.0, C("WC", 2, 3), MUL, ADD)
+    ts(V("IDT", 3), V("IDT", 1), 0.0, V("P16"), MUL, ADD)
+    ts(C("WC", 9, 10), C("WC", 2, 3), 4096.0, C("WC", 8, 9), MUL, ADD)
+    ts(C("WC", 12, 13), C("WC", 5, 6), 4.0, C("WC", 11, 12), MUL, ADD)
+    ts(C("WC", 13, 14), C("WC", 6, 7), C("WC", 7, 8), None, ADD)
+    fill(V("WB"), 0.0)
+    fill(V("WY"), 0.0)
+    ts(C("WC", 10, 11), C("WC", 0, 1), 16.0, C("WC", 9, 10), MUL, ADD)
+    ts(C("WC", 14, 15), C("WC", 12, 13), 256.0, None, MUL)
+    ts(C("WC", 15, 16), C("WC", 12, 13), 256.0, C("WC", 0, 1), MUL, ADD)
+    fill(V("ZA"), 0.0)
+    ts(C("WB", 15, 128, 16), V("B8"), C("WC", 13, 14), None, MUL)
+    ts(C("WY", 15, 128, 16), V("B8"), C("WC", 10, 11), None, MUL)
+    ts(V("E4N"), V("E4"), -1.0, None, MUL)
+    ts(V("IBP"), V("IB"), 2 * BIG, None, MUL)
+    ts(V("IBN"), V("IB"), -2 * BIG, None, MUL)
+    fill(C("NEG", 0, 1), 0.0)
+    fill(C("NEG", 1, 2), -1536.0)
+    fill(V("FQ"), 0.0)
+    fill(V("FN"), 0.0)
+    vcopy(V("LF"), V("LISTS"))
+    mm(V("PS0"), V("BCQ"), V("LF"), True, True)
+    for n, r in enumerate(AS[0] + BS[0]):
+        mm(bank("PS2", 32 * n, 32 * n + 32), row("LF", r), row("IF", me, 32), True, True)
+    fill(V("FN", ALL, slice(16, 32)), -0.5)
+    vcopy(V("FQ", ALL, slice(16, 32)), C("QK", 64, 128))
+    ts(C("QBIG", 0, 64), C("QK", 0, 64), -BIG, None, ADD)
+    ts(C("QBIG", 64, 128), C("QK", 64, 128), BIG, None, ADD)
+    ts(V("BP1", 0), V("BX", 0, ALL, 0), 16.0, None, MUL)
+    ts(V("BP2", 0), V("BX", 0, ALL, 0), -16.0, None, MUL)
+    ts(V("BP3", 0), V("BX", 0, ALL, 0), 16.0, None, MUL)
+    ts(V("OFF"), V("PS0"), C("COL", 0, 1), float(XZ), ADD, MIN)
+    for r in range(nrank):
+        vcopy(V("DI", ps=pb(r)), bank("PS0", 128 * r, 128 * r + 128, ps=pb(r)))
+    vcopy(C("q0", 0, 64), bank("PS2", 64, 128))
+    ts(C("q1", 0, 64), C("q0", 0, 64), 16256, None, AND)
+    ts(C("q1", 64, 128), C("q0", 0, 64), 127, None, AND)
+    vcopy(V("IDS"), V("q1"))
+    ts(V("q0"), V("DI"), 4, None, SHR)
+    ts(V("q1"), V("DI"), 15, None, AND)
+    ts(V("q1"), V("q1"), 1024, None, MUL)
+    tt(V("q0"), V("q0"), V("q1"), ADD)
+    vcopy(V("ILST"), V("q0"))
+
+    def ids_out(src, full):
+        act(V("IDX", ALL, 0, ALL, slice(0, 16)), src(0, 16))
+        act(V("IDX", ALL, 1, ALL, slice(8, 24)), src(0, 16))
+        act(V("IDX", ALL, 0, ALL, slice(16, 24)), src(0, 8))
+        act(V("IDX", ALL, 1, ALL, slice(0, 8)), src(8, 16))
+        for h in (0, 1):
+            act(V("IDO", slice(4 * h, 4 * h + 4)), full)
+    ids_out(lambda a, b: V("IDS", ALL, slice(a, b)), bank("PS2", 0, 64))
 
     def ranks_open():
         for h in (0, 1):
             mm(V("PS%d" % h), V("IB"), row("TC", h, 512), True, False)
+    ranks_open()
+    for o in [me] + order[::-1]:
+        dma("y", "dcp", row("X0", o, 1024), xcol(o))
+    YB = ("PS4", "PS5", "PS6", "PS7")
+    for r in range(nrank):
+        vgather(row("TAB", 2 * r, 1024), C("XW", 0, XZ + 16), row("OFF", 2 * r, 64))
+        sgather(row("TAB", 2 * r + 1, 1024), C("XW", 0, XZ + 16), row("OFF", 2 * r + 1, 64))
+        for i, b in enumerate(YB):
+            mm(V(b), C("ZS", 96 - 32 * r, 224 - 32 * r), row("TAB", 4 * r + i, 512), r == 0, r == nrank - 1)
+    for i, b in enumerate(YB):
+        if i < 2:
+            ts(row("POOL", i, 512), V(b), -128.0, None, ADD)
+        else:
+            act(row("POOL", i, 512), V(b), bias=-128.0)
+    for c in range(4):
+        dma("y", "dpw", V("XW", ps=slice(c + 2 * (c // 3), 128, 16)), V("IDT", c))
+        for h in (0, 1):
+            dma("y", "dpw", V("XW", ps=slice(32 * c + 3 + h, 32 * c + 32, 16)), V("PT", h, ps=pb(me)))
+    for side, base in enumerate((2032, 2064)):
+        iota(row("DB", side, 64), [[0, 64]], 32 * side - 16, base=base)
+        iota(row("TCC", side, 16), [[0, 16]], 16 - 32 * side)
+    iota(V("T16", 0), [[0, 2], [-16, 2], [0, 32]], 16)
+    iota(V("T16", 1), [[-16, 2], [0, 64]], 16)
+    weights(1)
+    weights(2)
+    for c in range(4):
+        need("g", [("cg", tot["cg"], {})])
+        iota(V("XOC", ps=pb(c)), [[4096 - 8192 * (c // 2), 2], [2048 - 4096 * (c % 2), 2], [0, 64]], 0, base=2048 * c)
 
-    inf = ["INF0", "INF1", "INF2", "INF3"]
+    def late_constants():
+        for e in (1, 3):
+            for b in range(4):
+                act(V("PX", e, pb(b)), row("IB", b ^ e, 32))
+        for k in (1, 2):
+            act(V("BP1", k), V("BX", k, ALL, 0), scale=16.0)
+            act(V("BP2", k), V("BX", k, ALL, 0), scale=-16.0)
+            act(V("BP3", k), V("BX", k, ALL, 0), scale=16.0)
+            act(V("B8K", k - 1), V("BX", k, ALL, 0), ABS, scale=1.0 / 32)
+        for k in (1, 2):
+            for c, (w, side) in enumerate(((0, 1), (14, 1), (15, 0))):
+                act(V("SEL", k, slice(4 * c, 4 * c + 4)), V("B8K", k - 1, slice(4 * side, 4 * side + 4)), scale=C("WC", w, w + 1))
+        act(V("IBQ"), V("IB"), scale=0.25)
+        act(V("IBH"), V("IB"), scale=0.5)
 
-    def info_done(k, nxt):
+    def as_list(name, w, out):
         for j in range(16):
-            mm(C("PS4", j, 512, 16), C(inf[k], j, 2048, 16), V("SEL"), True, True)
-        if nxt is not None:
-            scopy(V("IDSO"), C("PS4", 0, 256))
-            send(me ^ nxt, "aids%d" % k, "lids", row("IDSP", k, 256), V("IDSO"))
-        if nxt is not None and k > 0:
-            scopy(V("PAF"), C("PS4", 384, 512))
-            mm(C("PS7", 0, 128), V("PAF"), V("IF"), True, True)
-            vcopy(V("PAL"), C("PS7", 0, 128))
-        scopy(V("IDO", slice(0, 8)), C("PS4", 256, 384))
-        if nxt is not None:
-            scopy(V("IDO", slice(8, 16)), C("PS4", 256, 384))
-
-    def vgath(a, b, tab):
-        sgather(C("REP", a, b), blk(tab, me), C("PREYL", a // 16, b // 16))
-
-    def vsum(a, bank):
-        mm(V(bank), V("IB"), C("V", a, a + 512), True, False)
-        mm(V(bank), V("IB"), C("REP", a, a + 512), False, True)
-
-    def vround(a, bank):
-        scopy(C("V", a, a + 512), V(bank), scale=0.5, bias=768.25)
-
-    def vdve(a, b, tab):
-        ttg(C("VS", a, b), blk(tab, me), C("PREYL", a // 16, b // 16), C("V", a, b), ADD)
-        ts(C("VT", a, b), C("VS", a, b), 0.5, 768.25, MUL, ADD)
-        ts(C("YXO", a, b), C("VT", a, b), -1408.0, None, ADD)
+            mm(out, C(w, 15 - j, 143 - j), C(name, j, 2048, 16), j == 0, j == 15)
 
     bits = {1: 5, 2: 4, 4: 3, 8: 2}
 
-    def half(name, s, sv, k=None, kv=None):
+    def half(name, s, sv, k=None, kv=None, side=None):
         ix = [ALL] * 6
         ix[bits[s]] = sv
         if k is not None:
             ix[bits[k]] = kv
+        if side is not None:
+            ix[1] = slice(4 * side, 4 * side + 4)
         return V(name, *ix[1:])
 
-    def stage(src, dst, s, k=None, desc=False):
-        for kv in ((0, 1) if k else (None,)):
-            lo, hi = half(src, s, 0, k, kv), half(src, s, 1, k, kv)
-            if dst in ("E2O", "SI"):
-                dl, dh = C(dst, 0, 128, 2), C(dst, 1, 128, 2)
-            else:
-                dl, dh = half(dst, s, 0, k, kv), half(dst, s, 1, k, kv)
-            if desc != (kv == 1):
-                dl, dh = dh, dl
-            tt(dl, lo, hi, MIN)
-            tt(dh, lo, hi, MAX)
+    def step(src, dst, s, k=None, kv=None, side=None, desc=False):
+        lo, hi = half(src, s, 0, k, kv, side), half(src, s, 1, k, kv, side)
+        dl, dh = half(dst, s, 0, k, kv, side), half(dst, s, 1, k, kv, side)
+        if desc:
+            dl, dh = dh, dl
+        tt(dl, lo, hi, MIN)
+        tt(dh, lo, hi, MAX)
 
-    def merge(src, other, last, desc=False):
-        stage(src, other, 8, None, desc)
-        stage(other, src, 4, None, desc)
-        stage(src, other, 2, None, desc)
-        stage(other, last, 1, None, desc)
+    def side_of(name, side):
+        return V(name, slice(4 * side, 4 * side + 4))
+
+    inf = ["INF0", "INF1", "INF0", "INF1"]
+    NS = 1024 - NV
+    SB = list(range(4 - NS1, 4))
+    VB = list(range(4 - NS1))
 
     for k, d in enumerate(DS):
-        p = me ^ d
-        isA = me < p
-        npart = ecount(p)
-        expect("aids%d" % k, npart, [row("IDSP", k, 256)])
-        expect("ainf%d" % k, npart, [C(inf[k], 2048, 4096)])
-        expect("ast%d" % k, npart, [C("POOL", 2048, 4096)])
-        src, o16 = ("POOL", 0.0) if k == 0 else ("V16", 24576.0)
-        for h in (0, 1):
+        src = "POOL" if k == 0 else "V16"
+        cut = 64 if k == 0 else PV // 16
+        for a, b in ((0, cut), (cut, 128)):
             for j in range(16):
-                mm(row("PS2", h, 64), V("IB"), C(src, 1024 * h + j, 1024 * h + 1024, 16), j == 0, j == 15)
-        if k == 0:
-            ranks_open()
-            sgather(C("INF0", 0, 2048), V("PWIN"), V("ILST"))
+                mm(V("PS2", slice(a // 8, b // 8), slice(0, 8)), V("IB"), C(src, 16 * a + j, 16 * b, 16), j == 0, j == 15)
         C16 = V("C16")
-        ts(C16, C("PS2", 0, 128), -o16, None, ADD)
-        mm(C("PS6", 384, 392), C16, V("B8N"), True, True)
+        if k > 0:
+            ts(C("POOL", 0, PV), C("V16", 0, PV), -1536.0, None, ADD)
+        for b in SB[:1]:
+            mm(V(YB[b]), V("IB"), C(src, b, 2048, 4), True, False)
+        ts(C16, V("PS2", slice(0, 16), slice(0, 8)), 0.0 if k == 0 else -24576.0, None, ADD)
+        mm(V("PS2", 0, slice(8, 16)), C16, V("B8N"), True, True)
+        mm(bank("PS3", 128, 256), C16, V("IB"), True, True)
+        act(V("CS"), bank("PS3", 128, 256))
         for gg in range(8):
-            mm(row("PS%d" % (gg // 4), gg % 4), row("NBE", gg), C16, False, gg % 4 == 3)
-        mm(C("PS7", 0, 128), C16, V("IB"), True, True)
-        if k == 0:
-            for c, (e, w) in enumerate(((0.0, 128.0), (1.0, 1.0), (2.0, 128.0), (3.0, 1.0))):
-                ts(C("WC", c, c + 1), V("P16"), e, w, EQU, MUL)
-            tt(C("WC", 4, 5), C("WC", 0, 1), C("WC", 1, 2), ADD)
-            tt(C("WC", 5, 6), C("WC", 2, 3), C("WC", 3, 4), ADD)
-            for c, w in enumerate((0, 1, 4, 5)):
-                ts(row("SEL", c, 8), V("B8"), C("WC", w, w + 1), None, MUL)
+            mm(grp(gg), row("NBE", gg), C16, False, gg % 4 == 3)
+        if VB:
+            mm(V("PS5"), V("CS"), V("E4"), True, True)
+        for b in SB[1:]:
+            mm(V(YB[b]), V("IB"), C(src, b, 2048, 4), True, False)
+        for n, b in enumerate(SB):
+            mm(V(YB[b]), V("CS"), V("E4N"), False, True)
+            act(row("Y1", n, 512), V(YB[b]), RELU, bias=C("NEG", min(k, 1), min(k, 1) + 1))
         for gg in range(8):
-            ts(row("G", gg), row("PS%d" % (gg // 4), gg % 4), C("PS6", 384 + gg, 385 + gg), None, GT)
-        vcopy(C("E1O", 0, 128), C("PS7", 0, 128))
+            ts(row("G", gg), grp(gg), V("PS2", 0, slice(8 + gg, 9 + gg)), None, GT)
+        if k > 0:
+            ts(C("POOL", PV, 2048), C("V16", PV, 2048), -1536.0, None, ADD)
+        swap("dpool%d" % k, ("POOL", 2048), ("POOL", 0), d, 2048)
         for gg in range(8):
-            mm(C("PS2", 128, 256), row("GS", gg), row("G", gg), gg == 0, gg == 7)
-        ts(C("E1O", 128, 256), C("PS2", 128, 256), 1.0 / 2048, None, MUL)
-        send(p, "ae1%d" % k, "le1", row("E1P", k, 256), V("E1O"))
-        if k == 0:
-            ts(V("IBP"), V("IB"), 2 * BIG, None, MUL)
-            ts(V("IBN"), V("IB"), -2 * BIG, None, MUL)
-            fill(V("NH"), -0.5)
-            info_done(0, d)
-        for i, b in enumerate(("PS5", "PS6", "PS7", "PS4")):
-            mm(V(b), C("E1O", 0, 128), row("E16", i, 512), True, True)
-            tt(row("Y1", i, 512), V(b), row("POOL", i, 512), MAX)
+            mm(V("PS2", 1, slice(8 + gg, 9 + gg)), row("G", gg), C("ONE", 0, 1), True, True)
         for h in (0, 1):
             mm(V("PS%d" % h), V("ONE"), row("G", h, 512), True, True)
-        send(p, "ast%d" % k, "lst", C("POOL", 2048, 4096), C("POOL", 0, 2048))
-        send(p, "ainf%d" % k, "linf", C(inf[k], 2048, 4096), C(inf[k], 0, 2048))
-        expect("ae1%d" % k, npart, [row("E1P", k, 256)])
-        scopy(V("IDX", slice(0, 16), slice(0, 16)), row("IDSP", k, 256), scale=1.0 / 32)
-        scopy(V("IDX", slice(16, 32), slice(8, 24)), row("IDSP", k, 256), scale=1.0 / 32)
-        scopy(V("IDX", slice(0, 16), slice(16, 24)), V("IDX", slice(0, 16), slice(0, 8)))
-        scopy(V("IDX", slice(16, 32), slice(0, 8)), V("IDX", slice(0, 16), slice(8, 16)))
-        KEY = C("PS3", 0, 128)
-        mm(KEY, V("IB"), V("QC" if isA else "QC2"), True, False)
-        mm(KEY, C16, V("BXN" if isA else "BXP"), False, False)
-        mm(C("PS6", 392, 400), row("E1P", 2 * k + 1), V("B8P"), True, True)
-        for gg in range(8):
-            ts(row("MA", gg), row("PS%d" % (gg // 4), gg % 4), C("PS6", 392 + gg, 393 + gg), 32.0, EQU, MUL)
-        for j in range(16):
-            mm(C("PS3", j, 128, 16), C("Y1", j, 2048, 16), V("BP" if isA else "BN"), False, False)
-        for gg in range(8):
-            mm(C("PS2", 256 + 16 * gg, 272 + 16 * gg), row("MA", gg), row("E1P", 16 * k + gg, 16), True, True)
-        ts(V("CSM"), C("PS2", 256, 384), 1.0 / 32, None, MUL)
-        Y2B = ("PS0", "PS1", "PS4", "PS7")
-        for b in range(4):
-            mm(V(Y2B[b]), V("CSM"), row("E16", b, 512), True, True)
-        mm(C("PS6", 0, 128), V("CSM"), V("IB"), True, True)
-        scopy(V("CBT"), C("PS6", 0, 128))
-        scopy(V("MAF"), V("MA"), scale=1.0 / 32)
-        for gg in range(8):
-            for c in (0, 1):
-                mm(V("PS5", slice(gg, 16, 8), slice(0, 24)), row("MA", gg), V("IDX", slice(8 * c + gg, 32, 16), slice(0, 24)),
-                   c == 0, c == 1)
-        for b in range(4):
-            tt(row("Y2", b, 512), V(Y2B[b]), row("POOL", b, 512), MAX)
-        IW, KC = (V("IBN"), "QC") if isA else (V("IBP"), "QC2")
-        CM = C("PS6", 384, 512)
-        mm(KEY, V("CBT"), V("BXP" if isA else "BXN"), False, False)
-        mm(CM, V("IB"), V(KC), True, False)
-        mm(CM, IW, V("NH"), False, False)
-        for r in range(8):
-            tt(row("EQ", r, 256), V("PS5", ALL, slice(r, r + 16)), V("IDO"), EQU)
-            if r == 0:
-                for j in range(16):
-                    mm(C("PS3", j, 128, 16), C("Y2", j, 2048, 16), V("BN" if isA else "BP"), False, j == 15)
-            for h in (0, 1):
-                mm(CM, IW, row("EQ", 2 * r + h), False, r == 7 and h == 1)
-            if r == 6:
-                vcopy(V("K1"), KEY)
-        tt(V("SRA"), V("K1"), CM, MIN if isA else MAX)
-        if k == 0:
-            scopy(V("V"), C("XW", 16, 4112), bias=1408.0)
-            vcopy(V("IF"), V("IB"))
-        else:
-            for i, b in ((0, "PS4"), (1, "PS7"), (2, "PS0"), (3, "PS1"), (4, "PS3")):
-                vsum(512 * i, b)
-                vround(512 * i, b)
-        desc = not isA
-        stage("SRA", "SRB", 1, 2, desc)
-        stage("SRB", "SRA", 2, 4, desc)
-        stage("SRA", "SRB", 1, 4, desc)
-        stage("SRB", "SRA", 4, 8, desc)
-        stage("SRA", "SRB", 2, 8, desc)
-        stage("SRB", "SRA", 1, 8, desc)
-        merge("SRA", "SRB", "E2O", desc)
-        send(p, "ae2%d" % k, "le2", row("E2P", k), V("E2O"))
-        expect("ae2%d" % k, npart, [row("E2P", k)])
-        if k == 0:
-            vcopy(V("PREYL"), V("PR"))
-        DIF = C("PS6", 128, 256)
-        mm(DIF, V("TD" if isA else "TDN"), V("ONE"), True, False)
-        for gg in range(8):
-            mm(row("PS6", 8 + gg, 16), row("MA", gg), V("TC16" if isA else "TCN"), False, gg == 7)
-        adj = V("T16")
-        if not isA:
-            adj = V("ADJ")
-            ts(adj, DIF, -1.0, V("CE"), MUL, ADD)
-        mm(C("PS2", 384, 512), adj, V("IB"), True, False)
-        if isA:
-            ts(V("SRB"), V("E2O"), -3000000.0, 2 * BIG, LT, MUL)
-            tt(V("SRM"), V("E2O"), V("SRB"), ADD)
-            merge("SRM", "SRB", "SRM")
-            ts(V("SRB"), V("SRM"), 3000000.0, -2 * BIG, LT, MUL)
-            tt(V("AMX"), V("SRM"), V("SRB"), ADD)
-        for gg in range(8):
-            mm(row("PS7", 8 + gg, 16), row("MAF", gg), row("E2P", 8 * k + gg, 16), True, True)
-        if k == 2:
-            for i, b in ((5, "PS0"), (6, "PS1")):
-                vsum(512 * i, b)
-                vround(512 * i, b)
-        if isA:
-            tt(V("SRA"), V("SRM"), C("PS7", 128, 256), MIN)
-            merge("SRA", "SRB", "SRA")
-            tt(V("SI"), V("SRA"), V("AMX"), MAX)
-        else:
-            tt(V("SRA"), V("E2O"), C("PS7", 128, 256), MAX)
-            merge("SRA", "SRB", "SI")
-        ts(V("BB"), V("SI"), 4, 1, SHR, AND)
-        ts(V("QA"), V("SI"), 15, None, AND)
-        tt(V("M1"), V("BB"), DIF, MUL)
-        vcopy(V("QAB"), V("QA"))
-        mm(C("PS2", 384, 512), V("M1"), V("IB"), False, False)
-        mm(C("PS2", 384, 512), V("QAB"), V("IB"), False, True)
-        vcopy(V("LST"), C("PS2", 384, 512))
-        tab = "ALLT0" if k == 1 else "ALLT1"
-        m0 = 2048 * me
-        if k == 2:
-            vgather(C(tab, m0, m0 + 1024), V("POOL"), C("LST", 0, 64))
-            sgather(C(tab, m0 + 1024, m0 + 2048), V("POOL"), C("LST", 64, 128))
-        else:
-            for h in (0, 1):
-                a = m0 + 1024 * h
-                vgather(C(tab, a, a + 512), V("POOL"), C("LST", 64 * h, 64 * h + 32))
-                sgather(C(tab, a + 512, a + 1024), V("POOL"), C("LST", 64 * h + 32, 64 * h + 64))
-                send_parts([("ad3%d%d" % (k, h), [far], e_off), ("ae3%d" % k, on, e_on)], "le3", C(tab, a, a + 1024))
-            piece = [C(tab, 2048 * far + 1024 * h, 2048 * far + 1024 * h + 1024) for h in (0, 1)]
-            for h in (0, 1):
-                expect("ad3%d%d" % (k, h), NB, [piece[h]])
-            for h in (0, 1):
-                send(on[0], "ae3%d" % k, "le3", piece[h], piece[h], e_hand[h])
-            expect("ae3%d" % k, 2 * len(e_on) + len(e_hand[0]) + len(e_hand[1]), [blk(tab, r) for r in others if r != far])
-        if k < 2:
-            vcopy(C("V16", 0, 1024), C(tab, m0, m0 + 1024))
-            sgather(C(inf[k + 1], 0, 2048), V(inf[k]), V("LST"))
-            late = ((5, "PS0"), (6, "PS1"), (7, "PS3")) if k > 0 else ()
-            for i, b in late:
-                vsum(512 * i, b)
-            info_done(k + 1, DS[k + 1])
-            for i, b in late:
-                vround(512 * i, b)
-            ranks_open()
-            ttg(V("SU"), V(tab), C("PAL", 0, 64), C("V16", 0, 1024), ADD)
-            sgather(C("REP", 4096, 5120), V(tab), C("PAL", 64, 128))
-            for h in (0, 1):
-                mm(V("PS%d" % (6 + h)), V("IB"), C(tab, m0 + 1024 + 512 * h, m0 + 1536 + 512 * h), True, False)
-            for h in (0, 1):
-                mm(V("PS%d" % (6 + h)), V("IB"), row("REP", 8 + h, 512), False, True)
-            ts(C("V16", 0, 1024), V("SU"), 0.5, 1536.25, MUL, ADD)
-            ts(row("V16", 2, 512), V("PS6"), 0.5, 1536.25, MUL, ADD)
-            scopy(row("V16", 3, 512), V("PS7"), scale=0.5, bias=1536.25)
-            for a in (0, 1024, 2048, 3072):
-                vgath(a, a + 1024, tab)
-            ts(C("POOL", 0, 2048), V("V16"), -1536.0, None, ADD)
-        else:
-            def put(i, a, b):
-                dma("y", "dyx%d" % i, None, C("YXO", a, b), ext_out=T.yx[:, a:b])
 
-            def last(a):
-                vround(a, "PS%d" % (a // 512 % 4))
-                scopy(C("YXO", a, a + 512), C("V", a, a + 512), bias=-1408.0)
-            vsum(3584, "PS4")
-            vgath(2048, 3072, tab)
-            vround(3584, "PS4")
-            vgath(3072, 4096, tab)
-            sgather(C("INF3", 1536, 2048), V(inf[k]), C("LST", 96, 128))
-            for a in range(2048, 4096, 512):
-                vsum(a, "PS%d" % (a // 512 % 4))
-            vdve(0, 1024, tab)
-            put(0, 0, 1024)
-            vgather(C("INF3", 0, 1536), V(inf[k]), C("LST", 0, 96))
-            last(2048)
-            last(2560)
-            put(1, 2048, 3072)
-            vdve(1024, 1536, tab)
-            put(2, 1024, 1536)
-            info_done(3, None)
-            mm(C("PS7", 0, 128), V("IDO", slice(0, 8)), V("IF"), True, True)
-            scopy(V("YLO"), C("PS7", 0, 128))
-            dma("y", "dyl", None, V("YLO"), ext_out=T.yl[:, :])
-            vdve(1536, 2048, tab)
-            put(3, 1536, 2048)
-            last(3072)
-            put(4, 3072, 3584)
-            last(3584)
-            put(5, 3584, 4096)
+        def own(b):
+            tt(row("Y1H", b, 512), V("PS5"), C("POOL", b, 2048, 4), MAX)
+        n1 = len(VB) // 2
+        for b in VB[:n1]:
+            own(b)
+        for gg in PI[k]:
+            ts(row("M", gg), grp(gg), V("PS2", 1, slice(8 + (gg ^ 2 * d), 9 + (gg ^ 2 * d))), None, EQU)
+        for i in range(4):
+            act(row("MAF", i), row("M", PI[k][i]))
+        for i in range(4):
+            for c in (0, 1):
+                mm(V("PS4", slice(i, 8, 4), slice(0, 24)), row("M", PI[k][i]), V("IDX", c, ALL, i, slice(0, 24)), c == 0, c == 1)
+        for gg in PI[k]:
+            mm(bank("PS3", 256 + 16 * gg, 272 + 16 * gg), row("M", gg), row("CS", gg ^ 2 * d, 16), True, True)
+        for b in VB[n1:]:
+            own(b)
+        vcopy(V("CSM"), bank("PS3", 256, 384))
+        mm(V("PS0"), V("CSM"), V("E4"), True, True)
+        KEY = bank("PS3", 0, 128)
+        mm(KEY, V("IB"), V("QK"), True, False)
+        for b in SB:
+            mm(V("PS3", slice(0, 8), slice(b, 16, 4)), C16, V("BX", k, ALL, slice(b, 16, 4)), False, False)
+        RB = V("PS5", slice(0, 4))
+        mm(RB, V("IB"), V("FQ"), True, False)
+        mm(RB, V("IBP"), V("FN"), False, False)
+
+        def keys(name, w, n, b, last=False):
+            for j in range(4):
+                mm(V("PS3", slice(0, 8), 4 * j + b), C(name, 512 * n + j, 512 * n + 512, 4), V(w, k), False, last and j == 3)
+
+        def same(r):
+            tt(row("EQ", r), V("PS4", slice(0, 8), slice(r, r + 16)), V("IDO"), EQU)
+            for h in (0, 1):
+                e = row("EQ", 2 * r + h, 64)
+                mm(bank("PS3", 0, 64), V("IBN"), e, False, False)
+                mm(V("PS5", slice(0, 4), slice(r + 8 * h, r + 8 * h + 16)), V("IBP"), e, False, False)
+        for b in VB:
+            keys("Y1H", "BP3", b, b)
+        for r in range(EQ0):
+            same(r)
+        for b in range(4):
+            if b == 3:
+                for r in range(EQ0, 8):
+                    same(r)
+            tt(row("Y2", b, 512), V("PS0"), C("POOL", b, 2048, 4), MAX)
+            if b < len(SB):
+                keys("Y1", "BP1", b, SB[b])
+            keys("Y2", "BP2", b, b, b == 3)
+        vcopy(V("K1"), bank("PS3", 64, 128))
+        tt(side_of("SRA", 0), bank("PS3", 0, 64), C("QBIG", 0, 64), MAX)
+        for i in range(4):
+            mm(V("PS5", i, slice(0, 16)), row("MAF", i), row("K1", i, 16), False, i == 3)
+        tt(V("T1"), V("PS5", slice(0, 4), slice(0, 16)), C("QBIG", 64, 128), MIN)
+        tt(side_of("SRA", 1), V("PS5", slice(0, 4), slice(16, 32)), V("T1"), MAX)
+        mm(bank("PS3", 256, 384), V("IB"), V("DB"), True, False)
+        for i in range(4):
+            mm(V("PS3", slice(16 + i, 24, 4)), row("M", PI[k][i]), V("TCC"), False, i == 3)
+        LP = bank("PS2", 384, 512)
+        mm(LP, V("T16", min(k, 1)), V("IB"), True, False)
+        if k == 0:
+            late_constants()
+            sgather(C("INF0", 0, 2048), V("XW"), V("ILST"))
+            swap("dinf0", ("INF0", 2048), ("INF0", 0), d, 2048)
+            mm(bank("PS7", 0, 256), V("IB"), V("XOC"), True, False)
+            for n in range(8):
+                c = n % 4
+                mm(bank("PS7", 0, 256), C("ZQ", 96 - 32 * c, 224 - 32 * c), V("PT", n // 4, ALL, slice(64 * c, 64 * c + 64)),
+                   False, n == 7)
+        else:
+            def part(o):
+                for a, b, bk in ((0, 512, "PS0"), (512, NV, "PS1"), (NV, 1024, YB[o])):
+                    if b > a:
+                        out = bank(bk, 0, b - a)
+                        for n, (w, nm) in enumerate((("IBQ", "X0"), ("IBQ", "H0"), ("IBH", "H1"))):
+                            mm(out, V(w), C(nm, 1024 * o + a, 1024 * o + b), n == 0, n == 2 and b <= NV)
+                        if b <= NV:
+                            act(C("PP", 1024 * o + a, 1024 * o + b), out)
+            for o in range(nrank):
+                sgather(row("H%d" % (k - 1), o, 1024), V("TAB"), row("PREYX", o, 64))
+                if k == 2 and o > 0:
+                    part(o - 1)
+            if k == 2:
+                part(nrank - 1)
+        for s, kk, a, b in ((1, 2, "SRA", "SRB"), (2, 4, "SRB", "SRA"), (1, 4, "SRA", "SRB"),
+                            (4, 8, "SRB", "SRA"), (2, 8, "SRA", "SRB"), (1, 8, "SRB", "SRA")):
+            for kv in (0, 1):
+                step(a, b, s, kk, kv, desc=kv == 1)
+        for s, a, b in ((8, "SRA", "SRB"), (4, "SRB", "SRA"), (2, "SRA", "SRB"), (1, "SRB", "SRA")):
+            for side in (0, 1):
+                step(a, b, s, side=side, desc=side == 1)
+        tt(side_of("SRB", 0), side_of("SRA", 0), side_of("SRA", 1), MIN)
+        tt(side_of("SRB", 1), side_of("SRA", 0), side_of("SRA", 1), MAX)
+        for s, a, b in ((8, "SRB", "SRA"), (4, "SRA", "SRB"), (2, "SRB", "SRA"), (1, "SRA", "SRB")):
+            step(a, b, s, side=0)
+            step(a, "SI" if s == 1 else b, s, side=1)
+        za = slice(0, 4, 2) if k == 0 else slice(0, 2)
+        zv = 2 * min(k, 1)
+        ts(V("T1"), side_of("SRB", 0), -3000000.0, 2 * BIG, LT, MUL)
+        ts(C("QA", 64, 128), side_of("SI", 1), 31, None, AND)
+        tt(side_of("SRA", 0), side_of("SRB", 0), V("T1"), ADD)
+        ts(C("BB", 64, 128), C("QA", 64, 128), 16.0, None, LT)
+        step("SRA", "SRB", 8, side=0)
+        vcopy(V("ZB", slice(4, 8), slice(112, 128)), C("QA", 64, 128))
+        step("SRB", "SRA", 4, side=0)
+        tt(V("ZB", slice(0, 4), slice(112, 128)), C("BB", 64, 128), bank("PS3", 320, 384), MUL)
+        step("SRA", "SRB", 2, side=0)
+        if k == 0:
+            vcopy(V("PREYX"), bank("PS7", 0, 256))
+        step("SRB", "SI", 1, side=0)
+        for c in (1, 0):
+            for i in range(4):
+                o = 16 * PI[k][4 + i]
+                mm(LP, V("ZB", 4 * c + i, slice(112 - o, 240 - o)), row("M", PI[k][4 + i]), False, False)
+        ts(C("BB", 0, 64), side_of("SI", 0), 4, 1, SHR, AND)
+        ts(C("QA", 0, 64), side_of("SI", 0), 31, None, AND)
+        tt(V("ZA", zv, za), C("BB", 0, 64), bank("PS3", 256, 320), MUL)
+        vcopy(V("ZA", zv + 1, za), C("QA", 0, 64))
+        for c in (0, 1):
+            mm(LP, V("ZA", zv + c), V("IB"), False, c == 1)
+        vcopy(V("LST"), LP)
+        for h in (0, 1):
+            vgather(row("TAB", 2 * h, 512), V("POOL"), row("LST", 2 * h, 32))
+            sgather(row("TAB", 2 * h + 1, 512), V("POOL"), row("LST", 2 * h + 1, 32))
+            swap("dtab%d%d" % (h, k), ("TAB", 4096 + 1024 * h), ("TAB", 1024 * h), 2, 1024)
+        pbk = ("PS0", "PS1", "PS4", "PS5", "PS6", "PS7", "PS3", "PS2") if k < 2 else ("PS0", "PS1", "PS3", "PS2") * 2
+        jobs = [(e, i) for i in range(4) for e in (1, 3)]
+
+        def turn(n):
+            mm(V(pbk[n]), V("PX", jobs[n][0]), row("TAB", jobs[n][1], 512), True, True)
+
+        def land(n, scalar=False):
+            dst = row("TAB", 4 * jobs[n][0] + jobs[n][1], 512)
+            if n % 2 or scalar:
+                act(dst, V(pbk[n]))
+            else:
+                vcopy(dst, V(pbk[n]))
+        if k < 2:
+            for n in range(8):
+                turn(n)
+            vgather(C(inf[k + 1], 0, 1024), V(inf[k]), C("LST", 0, 64))
+            sgather(C(inf[k + 1], 1024, 2048), V(inf[k]), C("LST", 64, 128))
+            swap("dinf%d" % (k + 1), (inf[k + 1], 2048), (inf[k + 1], 0), DS[k + 1], 2048)
+            land(0)
+            land(7)
+            as_list(inf[k + 1], "WB", bank("PS2", 0, 128))
+            for n in (1, 6, 2, 3, 5):
+                land(n)
+            vcopy(C("V16", 0, PV), C("TAB", 0, PV))
+            ts(V("PAL"), bank("PS2", 0, 128), C("COL", 1, 2), None, ADD)
+            land(4, True)
+            for j in range(16):
+                mm(V("PS3", slice(16, 28), j), C(inf[k + 1], j, 2048, 16), V("SEL", k + 1), True, True)
+            ranks_open()
+            w = (2048 - PV) // 2
+            ttg(C("SU", 0, PV), V("TAB"), C("PAL", 0, PV // 16), C("V16", 0, PV), ADD)
+            for h in (0, 1):
+                a = PV + w * h
+                sgather(row("REP", h, w), V("TAB"), C("PAL", a // 16, (a + w) // 16))
+                mm(bank("PS%d" % (6 + h), 0, w), V("IB"), C("TAB", a, a + w), True, False)
+            for h in (0, 1):
+                mm(bank("PS%d" % (6 + h), 0, w), V("IB"), row("REP", h, w), False, True)
+            ts(C("V16", 0, PV), C("SU", 0, PV), 0.5, 1536.25, MUL, ADD)
+            for h in (0, 1):
+                a = PV + w * h
+                act(C("V16", a, a + w), bank("PS%d" % (6 + h), 0, w), scale=0.5, bias=1536.25)
+            ids_out(lambda a, b: V("PS3", slice(16, 24), slice(a, b)), V("PS3", slice(24, 28)))
+        else:
+            for n in range(8):
+                turn(n)
+                land(n)
+            HALF = 1520.4375
+
+            def place(o, a, b):
+                if o == me:
+                    return C("RCV", 1024 * me + a, 1024 * me + b)
+                return C("OUT", 1024 * order.index(o) + a, 1024 * order.index(o) + b)
+
+            def store(q, n):
+                ts(C("YXO", 1024 * q, 1024 * q + 512), C("RCV", 1024 * q, 1024 * q + 512), -1408.0, None, ADD)
+                act(C("YXO", 1024 * q + 512, 1024 * q + 1024), C("RCV", 1024 * q + 512, 1024 * q + 1024), bias=-1408.0)
+                for c in range(4):
+                    dma("y", "dyx%d" % n, None, row("YXO", q, 1024, ps=pb(c)), ext_out=T.yx[32 * q:32 * q + 32, 1024 * c:1024 * c + 1024])
+
+            def shut(o):
+                act(place(o, NV, 1024), bank(YB[o], 0, NS), scale=0.5, bias=HALF)
+                if o != me:
+                    send_to(o, "aout%d" % me, "lout", row("OUT", order.index(o), 1024), row("RCV", me, 1024))
+                else:
+                    store(me, 0)
+            last = [off[0], off[1], me] + on
+            for n, o in enumerate(last):
+                ttg(C("SU", 1024 * (n % 2), 1024 * (n % 2) + NV), V("TAB"), C("PREYX", 64 * o, 64 * o + NV // 16),
+                    C("PP", 1024 * o, 1024 * o + NV), ADD)
+                sgather(row("REP", n, NS), V("TAB"), C("PREYX", 64 * o + NV // 16, 64 * o + 64))
+                mm(bank(YB[o], 0, NS), V("IB"), row("REP", n, NS), False, True)
+                ts(place(o, 0, NV), C("SU", 1024 * (n % 2), 1024 * (n % 2) + NV), 0.5, HALF, MUL, ADD)
+                if n > 0:
+                    shut(last[n - 1])
+            shut(last[-1])
+            vgather(C(inf[3], 0, 1024), V(inf[2]), C("LST", 0, 64))
+            sgather(C(inf[3], 1024, 2048), V(inf[2]), C("LST", 64, 128))
+            as_list(inf[3], "WY", bank("PS2", 0, 128))
+            for r in others:
+                expect("aout%d" % r, NB, [row("RCV", r, 1024)])
+            expect("ayl", NB * (nrank - 1), [row("YL", r) for r in others])
+            store(off[0], 1)
+            vcopy(row("YL", me), bank("PS2", 0, 128))
+            send_all("ayl", "lyl", row("YL", me))
+            store(off[1], 2)
+            store(on[0], 3)
+            for q in range(nrank):
+                dma("s", "dyl", None, row("YL", q, ps=pb(me)), ext_out=T.yl[32 * q:32 * q + 32, :])
     for sem in sorted(tot):
         if know["g"].get(sem, 0) < tot[sem]:
             g.wait_ge(T.sem[sem], tot[sem])

@@ -3,16 +3,17 @@ from concourse.mybir import AluOpType, ActivationFunctionType
 
 BF, FH, FF, I4, U2 = "bfloat16", "float16", "float32", "int32", "uint16"
 S6 = [128, 8, 2, 2, 2, 2]
-CFG = {"NS1": 2, "NV": 576, "PV": 1152, "EQ0": 4}
+CFG = {"NS1": 2, "PV": 1152, "PA": 896, "PC": 1152, "EQ0": 5, "EQ1": 8, "MT": 1, "DE": (2,), "CPD": 0, "LV": 3,
+       "CV": 640, "IV": 1280, "IA": 1152, "NPE": 1, "END": "w0 f0 s0 f1 f2 s1 s2 L c0 f3 O c2 s3 c1 c3 Y"}
 XZ = 13328
 _SB = {
     "SL": ([128, 128], I4), "PR": ([128, 256], I4), "LISTS": ([128, 512], U2), "LF": ([128, 512], FF), "OFF": ([128, 512], U2),
-    "XS": ([128, 3072], BF), "XW": ([128, 16384], BF), "X0": ([128, 4096], BF),
-    "PT": ([128, 2, 4, 256], BF), "IDT": ([128, 4, 4, 256], BF), "PREYX": ([128, 256], U2), "XOC": ([128, 256], BF),
+    "XW": ([128, XZ + 16 + 3072], BF), "X0": ([128, 4096], BF),
+    "PT": ([128, 2, 4, 256], BF), "IDT": ([128, 4, 4, 256], BF), "PREYX": ([128, 256], U2), "PREYL": ([128, 256], U2), "XOC": ([128, 256], BF),
     "DI": ([128, 128], I4), "q0": ([128, 128], I4), "q1": ([128, 128], I4), "ILST": ([128, 128], U2),
     "w1": ([128, 256], I4), "w2": ([128, 256], I4), "IDS": ([128, 8, 16], BF),
     "TAB": ([128, 8192], BF), "POOL": ([128, 4096], BF), "INF0": ([128, 4096], BF), "INF1": ([128, 4096], BF),
-    "H0": ([128, 4096], BF), "H1": ([128, 4096], BF), "REP": ([128, 2048], BF), "PP": ([128, 4096], FH),
+    "H0": ([128, 4096], BF), "H1": ([128, 4096], BF), "REP": ([128, 2048], BF), "PP": ([128, 2048], FH), "OWN": ([128, 2048], BF),
     "SU": ([128, 2048], FH), "V16": ([128, 2048], FH), "OUT": ([128, 3072], FH), "RCV": ([128, 4096], FH),
     "YXO": ([128, 4096], FF), "YL": ([128, 512], FF),
     "C16": ([128, 128], FH), "CS": ([128, 128], FH), "CSM": ([128, 128], FH), "E4": ([128, 512], BF), "E4N": ([128, 512], BF),
@@ -24,7 +25,7 @@ _SB = {
     "ZA": ([128, 4, 4, 32], BF), "ZB": ([128, 8, 240], BF), "LST": ([128, 128], U2),
     "ONE": ([128, 128], BF), "IB": ([128, 128], BF), "IF": ([128, 128], FF), "BCQ": ([128, 128], FF), "TC": ([128, 1024], BF),
     "IBP": ([128, 128], BF), "IBN": ([128, 128], BF), "IBQ": ([128, 128], BF), "IBH": ([128, 128], BF),
-    "PX": ([128, 4, 128], BF), "ZS": ([128, 224], BF), "ZQ": ([128, 224], BF),
+    "PX": ([128, 4, 128], BF), "ZS": ([128, 224], BF), "ZQ": ([128, 224], BF), "ZF": ([128, 224], FF),
     "B8a": ([128, 8], BF), "B8": ([128, 8], BF), "B8N": ([128, 8], BF), "NBE": ([128, 1024], BF),
     "PCI": ([128, 1], I4), "pi": ([128, 4], I4), "P16": ([128, 1], FF), "COL": ([128, 8], FF), "WC": ([128, 16], FF),
     "T16": ([128, 2, 128], BF), "DB": ([128, 128], BF), "TCC": ([128, 32], BF), "QK": ([128, 128], BF),
@@ -38,7 +39,7 @@ _PS = {"PS%d" % i: ([128, 16, 32] if i in (4, 5) else [128, 32, 16], FF) for i i
 for _k, (_s, _d) in _PS.items():
     SCRATCH[_k] = ("psum", _s, _d)
 SEMAPHORES = (["cv", "cs", "ct", "cg", "dsl", "dpr", "dcp", "dpw", "dyl", "ali", "apt", "ayl", "lli", "lpt", "lx", "lout", "lyl"]
-              + [n + str(i) for n in ("dx", "ax", "aout", "dyx") for i in range(4)]
+              + [n + str(i) for n in ("dx", "ax", "aout", "dyx", "dwin") for i in range(4)]
               + [n + str(k) for n in ("dpool", "dinf", "dtab0", "dtab1") for k in range(3)])
 
 ADD, SUB, MUL = AluOpType.add, AluOpType.subtract, AluOpType.mult
@@ -46,6 +47,7 @@ MAX, MIN = AluOpType.max, AluOpType.min
 GT, GE, LT, EQU, NE = AluOpType.is_gt, AluOpType.is_ge, AluOpType.is_lt, AluOpType.is_equal, AluOpType.not_equal
 SHR, AND = AluOpType.arith_shift_right, AluOpType.bitwise_and
 COPY, RELU, ABS = ActivationFunctionType.Copy, ActivationFunctionType.Relu, ActivationFunctionType.Abs
+IDENT = ActivationFunctionType.Identity
 ALL = slice(None)
 BIG = 4194304.0
 DS = (1, 2, 3)
@@ -232,6 +234,9 @@ def rank_program(g, core, T, topo):
     def xcol(o, ps=ALL):
         return C("XW", 16 + 4096 * o, 1040 + 4096 * o, ps=ps)
 
+    def leaving(n, ps=ALL):
+        return C("XW", XZ + 16 + 1024 * n, XZ + 1040 + 1024 * n, ps=ps)
+
     def swap(sem, dst, src, e, n):
         w = 64 if e == 2 else 32
         for b in range(128 // w):
@@ -241,13 +246,13 @@ def rank_program(g, core, T, topo):
     AS = [[r for r in range(nrank) if r < r ^ d] for d in DS]
     BS = [[r ^ d for r in a] for a, d in zip(AS, DS)]
     PI = [[2 * r + w for r in a + b for w in (0, 1)] for a, b in zip(AS, BS)]
-    NS1, NV, PV, EQ0 = CFG["NS1"], CFG["NV"], CFG["PV"], CFG["EQ0"]
+    NS1, PV, PA, PC, EQ0, EQ1, MT = (CFG[n] for n in ("NS1", "PV", "PA", "PC", "EQ0", "EQ1", "MT"))
 
     order = off + on
     dma("y", "dsl", V("SL"), None, ext_in=T.sl[:, :])
     for n, q in enumerate(order + [me]):
         for c in range(4):
-            dst = C("XS", 1024 * n, 1024 * n + 1024, ps=pb(c)) if q != me else xcol(me, pb(c))
+            dst = leaving(n, pb(c)) if q != me else xcol(me, pb(c))
             dma("ys"[c % 2], "dx%d" % n, dst, None, ext_in=T.x[32 * q:32 * q + 32, 1024 * c:1024 * c + 1024])
         if n == 1:
             dma("s", "dpr", V("PR"), None, ext_in=T.prey[:, :])
@@ -257,48 +262,69 @@ def rank_program(g, core, T, topo):
     afs(V("IB"), V("ONE"), [[-1, 128]], EQU, 0, 1)
     afs(V("B8a"), C("ONE", 0, 8), [[-16, 8]], GE, 0, 1)
     afs(V("B8"), V("B8a"), [[16, 8]], GE, 15, -1)
+    vcopy(row("LISTS", me), V("SL"))
+    send_all("ali", "lli", row("LISTS", me))
+    for n, q in enumerate(order):
+        send_to(q, "ax%d" % me, "lx", leaving(n), xcol(me))
+    expect("ali", NB * (nrank - 1), [row("LISTS", r) for r in others])
+    for r in others:
+        expect("ax%d" % r, NB, [xcol(r)])
+
+    def zeros(n):
+        return C("XW", 1040, 1040 + n)
+    act(C("XW", 5136, 8208), zeros(3072))
     fill(V("E4N"), 1.0 / 16)
     fill(V("C32", 0), 32.0)
     fill(V("C32", 1), -32.0)
     fill(C("XW", 0, 16), 0.0)
-    afs(V("E4"), V("E4N"), [[-1, 128], [0, 4]], EQU, 0, 1)
-    vcopy(row("LISTS", me), V("SL"))
-    send_all("ali", "lli", row("LISTS", me))
-    for n, q in enumerate(order):
-        send_to(q, "ax%d" % me, "lx", row("XS", n, 1024), xcol(me))
-    expect("ali", NB * (nrank - 1), [row("LISTS", r) for r in others])
-    for r in others:
-        expect("ax%d" % r, NB, [xcol(r)])
-    act(C("XW", 5136, 8208), C("XW", 1040, 4112))
-    act(C("XW", 9232, 12304), C("XW", 1040, 4112))
-    act(C("XW", XZ, 16384), C("XW", 1040, 1040 + 16384 - XZ))
-    act(V("ZB"), C("XW", 1040, 1040 + 1920))
-    vcopy(V("IF"), V("IB"))
-    fill(V("ZS"), 0.0)
-    fill(V("ZQ"), 0.0)
-    for c in range(4):
-        vcopy(row("BCQ", c, 32), row("IF", me, 32))
-        vcopy(C("ZS", 96, 128, ps=pb(c)), row("IB", c, 32, ps=pb(c)))
-    vcopy(C("ZQ", 96, 128), row("IB", me, 32))
+    fill(C("XW", XZ, XZ + 16), 0.0)
     ts(C("pi", 0, 1), V("PCI"), 15, None, AND)
     ts(C("pi", 1, 2), V("PCI"), 5, None, SHR)
     ts(C("pi", 2, 3), V("PCI"), 6, None, SHR)
     ts(C("pi", 3, 4), V("PCI"), 5, 1, SHR, AND)
+    vcopy(V("IF"), V("IB"))
+    vcopy(row("LF", me), V("SL"))
     vcopy(V("P16"), C("pi", 0, 1))
     ts(C("COL", 0, 1), C("pi", 1, 2), -1024.0, 16.0, MUL, ADD)
     ts(C("COL", 1, 2), C("pi", 1, 2), 2048.0, None, MUL)
     ts(C("COL", 2, 3), C("pi", 2, 3), -8192.0, 4096.0, MUL, ADD)
     ts(C("COL", 3, 4), C("pi", 3, 4), -4096.0, 2048.0, MUL, ADD)
-    for i in range(8):
-        ts(row("NBE", i), V("ONE"), C("B8", i, i + 1), -128.0, MUL, MUL)
-    ts(V("B8N"), V("B8"), -128.0, None, MUL)
+    for c in range(4):
+        vcopy(row("BCQ", c, 32), row("IB", me, 32))
+
+    def spread(r):
+        mm(grp(r), V("BCQ"), row("LF", r), True, True)
+
+    def columns(r):
+        ts(row("OFF", r), grp(r), C("COL", 0, 1), float(XZ), ADD, MIN)
+    spread(me)
+    fill(C("XW", 9232, 12304), 0.0)
+    columns(me)
     ts(V("w1"), V("PR"), 1920, None, AND)
     ts(V("w2"), V("PR"), 127, None, AND)
     vcopy(V("PT", 0, me), V("w1"))
     vcopy(V("PT", 1, me), V("w2"))
+    afs(V("E4"), V("E4N"), [[-1, 128], [0, 4]], EQU, 0, 1)
     for c in (0, 1):
         send_all("apt", "lpt", V("PT", c, me))
     expect("apt", 2 * NB * (nrank - 1), [V("PT", ALL, r) for r in others])
+    fill(V("ZS"), 0.0)
+    for c in range(4):
+        vcopy(C("ZS", 96, 128, ps=pb(c)), row("IB", c, 32, ps=pb(c)))
+    for i in range(8):
+        ts(row("NBE", i), V("ONE"), C("B8", i, i + 1), -128.0, MUL, MUL)
+    ts(V("B8N"), V("B8"), -128.0, None, MUL)
+    fill(C("NEG", 0, 1), 0.0)
+    fill(C("NEG", 1, 2), -1536.0)
+    for nm in ("ZF", "ZQ"):
+        act(V(nm), zeros(224))
+        act(C(nm, 96, 128), row("IB", me, 32))
+    act(V("IBP"), V("IB"), scale=2 * BIG)
+    act(V("IBN"), V("IB"), scale=-2 * BIG)
+    act(V("FQ"), zeros(128))
+    act(V("FN"), zeros(128))
+    act(V("FN", ALL, slice(16, 32)), zeros(64), bias=-0.5)
+    act(V("IDT", 3), zeros(1024), IDENT, bias=V("P16"))
 
     def weights(k):
         for side, rs in enumerate((AS[k], BS[k])):
@@ -309,57 +335,15 @@ def rank_program(g, core, T, topo):
     weights(0)
     iota(V("TC"), [[0, 8], [1, 128]], -1)
     iota(V("IDT", 0), [[0, 4], [1, 256]], 0)
-    for c in range(6):
-        ts(C("WC", c, c + 1), V("P16"), float(c), None, EQU)
-    for a in (0, 1):
-        fill(V("IDT", 1, slice(2 * a, 2 * a + 2)), float(a))
-        fill(V("IDT", 2, slice(a, 4, 2)), float(a))
-    ts(C("WC", 6, 7), C("WC", 1, 2), C("COL", 2, 3), C("WC", 3, 4), MUL, ADD)
-    ts(C("WC", 7, 8), C("WC", 2, 3), C("COL", 3, 4), C("WC", 4, 5), MUL, ADD)
-    ts(C("WC", 8, 9), C("WC", 1, 2), 8192.0, C("WC", 5, 6), MUL, ADD)
-    ts(C("WC", 11, 12), C("WC", 1, 2), 2.0, C("WC", 2, 3), MUL, ADD)
-    ts(V("IDT", 3), V("IDT", 1), 0.0, V("P16"), MUL, ADD)
-    ts(C("WC", 9, 10), C("WC", 2, 3), 4096.0, C("WC", 8, 9), MUL, ADD)
-    ts(C("WC", 12, 13), C("WC", 5, 6), 4.0, C("WC", 11, 12), MUL, ADD)
-    ts(C("WC", 13, 14), C("WC", 6, 7), C("WC", 7, 8), None, ADD)
-    fill(V("WB"), 0.0)
-    fill(V("WY"), 0.0)
-    ts(C("WC", 10, 11), C("WC", 0, 1), 16.0, C("WC", 9, 10), MUL, ADD)
-    ts(C("WC", 14, 15), C("WC", 12, 13), 256.0, None, MUL)
-    ts(C("WC", 15, 16), C("WC", 12, 13), 256.0, C("WC", 0, 1), MUL, ADD)
-    fill(V("ZA"), 0.0)
-    ts(C("WB", 15, 128, 16), V("B8"), C("WC", 13, 14), None, MUL)
-    ts(C("WY", 15, 128, 16), V("B8"), C("WC", 10, 11), None, MUL)
-    ts(V("E4N"), V("E4"), -1.0, None, MUL)
-    ts(V("IBP"), V("IB"), 2 * BIG, None, MUL)
-    ts(V("IBN"), V("IB"), -2 * BIG, None, MUL)
-    fill(C("NEG", 0, 1), 0.0)
-    fill(C("NEG", 1, 2), -1536.0)
-    fill(V("FQ"), 0.0)
-    fill(V("FN"), 0.0)
-    vcopy(V("LF"), V("LISTS"))
-    mm(V("PS0"), V("BCQ"), V("LF"), True, True)
+    iota(V("IDT", 1), [[1, 2], [0, 512]], 0)
+    iota(V("IDT", 2), [[0, 2], [1, 2], [0, 256]], 0)
+    for r in order[::-1]:
+        vcopy(row("LF", r), row("LISTS", r))
+        spread(r)
     for n, r in enumerate(AS[0] + BS[0]):
-        mm(bank("PS2", 32 * n, 32 * n + 32), row("LF", r), row("IF", me, 32), True, True)
-    fill(V("FN", ALL, slice(16, 32)), -0.5)
-    vcopy(V("FQ", ALL, slice(16, 32)), C("QK", 64, 128))
-    ts(C("QBIG", 0, 64), C("QK", 0, 64), -BIG, None, ADD)
-    ts(C("QBIG", 64, 128), C("QK", 64, 128), BIG, None, ADD)
-    ts(V("BP1", 0), V("BX", 0, ALL, 0), 16.0, None, MUL)
-    ts(V("BP2", 0), V("BX", 0, ALL, 0), -16.0, None, MUL)
-    ts(V("BP3", 0), V("BX", 0, ALL, 0), 16.0, None, MUL)
-    ts(V("OFF"), V("PS0"), C("COL", 0, 1), float(XZ), ADD, MIN)
+        mm(bank("PS3", 256 + 32 * n, 288 + 32 * n), row("LF", r), row("IF", me, 32), True, True)
     for r in range(nrank):
-        vcopy(V("DI", ps=pb(r)), bank("PS0", 128 * r, 128 * r + 128, ps=pb(r)))
-    vcopy(C("q0", 0, 64), bank("PS2", 64, 128))
-    ts(C("q1", 0, 64), C("q0", 0, 64), 16256, None, AND)
-    ts(C("q1", 64, 128), C("q0", 0, 64), 127, None, AND)
-    vcopy(V("IDS"), V("q1"))
-    ts(V("q0"), V("DI"), 4, None, SHR)
-    ts(V("q1"), V("DI"), 15, None, AND)
-    ts(V("q1"), V("q1"), 1024, None, MUL)
-    tt(V("q0"), V("q0"), V("q1"), ADD)
-    vcopy(V("ILST"), V("q0"))
+        mm(bank("PS3", 384, 512), C("ZF", 96 - 32 * r, 224 - 32 * r), row("LF", r), r == 0, r == nrank - 1)
 
     def ids_out(src, full):
         act(V("IDX", ALL, 0, ALL, slice(0, 16)), src(0, 16))
@@ -368,29 +352,53 @@ def rank_program(g, core, T, topo):
         act(V("IDX", ALL, 1, ALL, slice(0, 8)), src(8, 16))
         for h in (0, 1):
             act(V("IDO", slice(4 * h, 4 * h + 4)), full)
-    ids_out(lambda a, b: V("IDS", ALL, slice(a, b)), bank("PS2", 0, 64))
 
     def ranks_open():
         for h in (0, 1):
             mm(V("PS%d" % h), V("IB"), row("TC", h, 512), True, False)
-    ranks_open()
     for o in [me] + order[::-1]:
         dma("y", "dcp", row("X0", o, 1024), xcol(o))
     YB = ("PS4", "PS5", "PS6", "PS7")
-    for r in range(nrank):
-        vgather(row("TAB", 2 * r, 1024), C("XW", 0, XZ + 16), row("OFF", 2 * r, 64))
-        sgather(row("TAB", 2 * r + 1, 1024), C("XW", 0, XZ + 16), row("OFF", 2 * r + 1, 64))
-        for i, b in enumerate(YB):
-            mm(V(b), C("ZS", 96 - 32 * r, 224 - 32 * r), row("TAB", 4 * r + i, 512), r == 0, r == nrank - 1)
+    win = C("XW", 0, XZ + 16)
+    askers = [me] + order[::-1]
+    for n, r in enumerate(askers):
+        zs = C("ZS", 96 - 32 * r, 224 - 32 * r)
+        if n < nrank - 1:
+            columns(askers[n + 1])
+            vgather(row("TAB", 2 * r, 1024), win, row("OFF", 2 * r, 64))
+            sgather(row("TAB", 2 * r + 1, 1024), win, row("OFF", 2 * r + 1, 64))
+            for i, b in enumerate(YB):
+                mm(V(b), zs, row("TAB", 4 * r + i, 512), n == 0, False)
+            if n == nrank - 2:
+                ranks_open()
+        else:
+            for i, b in enumerate(YB):
+                (sgather if i % 2 else vgather)(row("TAB", 4 * r + i, 512), win, row("OFF", 4 * r + i, 32))
+                mm(V(b), zs, row("TAB", 4 * r + i, 512), False, True)
     for i, b in enumerate(YB):
-        if i < 2:
+        if i % 2 == 0:
             ts(row("POOL", i, 512), V(b), -128.0, None, ADD)
         else:
             act(row("POOL", i, 512), V(b), bias=-128.0)
+    act(V("E4N"), V("E4"), scale=-1.0)
+    act(V("BP1", 0), V("BX", 0, ALL, 0), scale=16.0)
+    act(V("BP2", 0), V("BX", 0, ALL, 0), scale=-16.0)
+    act(V("BP3", 0), V("BX", 0, ALL, 0), scale=16.0)
+    act(V("FQ", ALL, slice(16, 32)), C("QK", 64, 128))
+    act(C("QBIG", 0, 64), C("QK", 0, 64), bias=-BIG)
+    act(C("QBIG", 64, 128), C("QK", 64, 128), bias=BIG)
+    vcopy(C("q0", 0, 64), bank("PS3", 320, 384))
+    vcopy(V("DI"), bank("PS3", 384, 512))
+    ts(C("q1", 0, 64), C("q0", 0, 64), 16256, None, AND)
+    ts(C("q1", 64, 128), C("q0", 0, 64), 127, None, AND)
+    ts(C("WC", 0, 6), C("QK", 0, 6), V("P16"), None, EQU)
+    vcopy(V("IDS"), V("q1"))
+    ids_out(lambda a, b: V("IDS", ALL, slice(a, b)), bank("PS3", 256, 320))
     for c in range(4):
-        dma("y", "dpw", V("XW", ps=slice(c + 2 * (c // 3), 128, 16)), V("IDT", c))
         for h in (0, 1):
-            dma("y", "dpw", V("XW", ps=slice(32 * c + 3 + h, 32 * c + 32, 16)), V("PT", h, ps=pb(me)))
+            dma("y", "dpw", C("XW", 0, 16384, ps=slice(32 * c + 3 + h, 32 * c + 32, 16)), V("PT", h, ps=pb(me)))
+    for c in (3, 0, 1, 2):
+        dma("y", "dpw", C("XW", 0, 16384, ps=slice(c + 2 * (c // 3), 128, 16)), V("IDT", c))
     for side, base in enumerate((2032, 2064)):
         iota(row("DB", side, 64), [[0, 64]], 32 * side - 16, base=base)
         iota(row("TCC", side, 16), [[0, 16]], 16 - 32 * side)
@@ -403,6 +411,19 @@ def rank_program(g, core, T, topo):
         iota(V("XOC", ps=pb(c)), [[4096 - 8192 * (c // 2), 2], [2048 - 4096 * (c % 2), 2], [0, 64]], 0, base=2048 * c)
 
     def late_constants():
+        def w(i):
+            return C("WC", i, i + 1)
+        act(V("ZA"), V("IDT", 1, slice(0, 2)))
+        for n in range(4):
+            act(V("ZB", slice(2 * n, 2 * n + 2)), V("IDT", 1, slice(0, 2), slice(0, 240)))
+        act(V("WB"), V("IDT", 1, 0, slice(0, 144)))
+        act(V("WY"), V("IDT", 1, 0, slice(0, 144)))
+        for out, a, s, b in ((6, 1, C("COL", 2, 3), 3), (7, 2, C("COL", 3, 4), 4), (8, 1, 8192.0, 5), (11, 1, 2.0, 2),
+                             (9, 2, 4096.0, 8), (12, 5, 4.0, 11), (13, 6, 1.0, 7), (10, 0, 16.0, 9), (15, 12, 256.0, 0)):
+            act(w(out), w(a), IDENT, bias=w(b), scale=s)
+        act(w(14), w(12), scale=256.0)
+        act(C("WB", 15, 128, 16), V("B8"), scale=w(13))
+        act(C("WY", 15, 128, 16), V("B8"), scale=w(10))
         for e in (1, 3):
             for b in range(4):
                 act(V("PX", e, pb(b)), row("IB", b ^ e, 32))
@@ -414,6 +435,9 @@ def rank_program(g, core, T, topo):
         for k in (1, 2):
             for c, (w, side) in enumerate(((0, 1), (14, 1), (15, 0))):
                 act(V("SEL", k, slice(4 * c, 4 * c + 4)), V("B8K", k - 1, slice(4 * side, 4 * side + 4)), scale=C("WC", w, w + 1))
+        for n in range(CFG["NPE"]):
+            for b in range(4):
+                act(V("PX", 2 * n, pb(b)), row("IB", order[n], 32))
         act(V("IBQ"), V("IB"), scale=0.25)
         act(V("IBH"), V("IB"), scale=0.5)
 
@@ -444,101 +468,131 @@ def rank_program(g, core, T, topo):
         return V(name, slice(4 * side, 4 * side + 4))
 
     inf = ["INF0", "INF1", "INF0", "INF1"]
-    NS = 1024 - NV
+    def sums(src, a, b):
+        for j in range(16):
+            mm(V("PS2", slice(a // 8, b // 8), slice(0, 8)), V("IB"), C(src, 16 * a + j, 16 * b, 16), j == 0, j == 15)
+
     SB = list(range(4 - NS1, 4))
     VB = list(range(4 - NS1))
 
     for k, d in enumerate(DS):
         src = "POOL" if k == 0 else "V16"
-        cut = 64 if k == 0 else PV // 16
-        for a, b in ((0, cut), (cut, 128)):
-            for j in range(16):
-                mm(V("PS2", slice(a // 8, b // 8), slice(0, 8)), V("IB"), C(src, 16 * a + j, 16 * b, 16), j == 0, j == 15)
+        if k == 0:
+            sums(src, 0, 64)
+        sums(src, 64 if k == 0 else PA // 16, 128)
         C16 = V("C16")
         if k > 0:
-            ts(C("POOL", 0, PV), C("V16", 0, PV), -1536.0, None, ADD)
+            ts(C("POOL", 0, PC), C("V16", 0, PC), -1536.0, None, ADD)
         for b in SB[:1]:
             mm(V(YB[b]), V("IB"), C(src, b, 2048, 4), True, False)
         ts(C16, V("PS2", slice(0, 16), slice(0, 8)), 0.0 if k == 0 else -24576.0, None, ADD)
+        if k == 0:
+            ts(V("q1"), V("DI"), 15, None, AND)
+            ts(V("q0"), V("DI"), 4, None, SHR)
+            ts(V("q1"), V("q1"), 1024, None, MUL)
+        if k == 1:
+            for o in range(nrank):
+                ts(row("PREYL", o, 64), row("PREYX", o, 64), C("XOC", 64 * o, 64 * o + 1), None, SUB)
         mm(V("PS2", 0, slice(8, 16)), C16, V("B8N"), True, True)
+        for n, gg in enumerate(PI[k]):
+            mm(grp(n), row("NBE", gg), C16, False, n % 4 == 3)
         mm(bank("PS3", 128, 256), C16, V("IB"), True, True)
         act(V("CS"), bank("PS3", 128, 256))
-        for gg in range(8):
-            mm(grp(gg), row("NBE", gg), C16, False, gg % 4 == 3)
-        if VB:
-            mm(V("PS5"), V("CS"), V("E4"), True, True)
+        swap("dpool%d" % k, ("POOL", 2048), ("POOL", 0), d, 2048)
         for b in SB[1:]:
             mm(V(YB[b]), V("IB"), C(src, b, 2048, 4), True, False)
-        for n, b in enumerate(SB):
+        if VB:
+            mm(V("PS5"), V("CS"), V("E4"), True, True)
+        for n, gg in enumerate(PI[k]):
+            ts(row("G", n), grp(n), V("PS2", 0, slice(8 + gg, 9 + gg)), None, GT)
+        mm(V("PS0"), V("ONE"), row("G", 0, 512), True, True)
+        for n in (range(4, 8) if MT else range(8)):
+            mm(V("PS2", 1, slice(8 + n, 9 + n)), row("G", n), C("ONE", 0, 1), True, True)
+        if not MT:
+            mm(V("PS1"), V("ONE"), row("G", 1, 512), True, True)
+
+        def far(n):
+            act(row("Y1", n, 512), V(YB[SB[n]]), RELU, bias=C("NEG", min(k, 1), min(k, 1) + 1))
+        for b in SB:
             mm(V(YB[b]), V("CS"), V("E4N"), False, True)
-            act(row("Y1", n, 512), V(YB[b]), RELU, bias=C("NEG", min(k, 1), min(k, 1) + 1))
-        for gg in range(8):
-            ts(row("G", gg), grp(gg), V("PS2", 0, slice(8 + gg, 9 + gg)), None, GT)
-        if k > 0:
-            ts(C("POOL", PV, 2048), C("V16", PV, 2048), -1536.0, None, ADD)
-        swap("dpool%d" % k, ("POOL", 2048), ("POOL", 0), d, 2048)
-        for gg in range(8):
-            mm(V("PS2", 1, slice(8 + gg, 9 + gg)), row("G", gg), C("ONE", 0, 1), True, True)
-        for h in (0, 1):
-            mm(V("PS%d" % h), V("ONE"), row("G", h, 512), True, True)
+        for n in range(len(SB) - MT):
+            far(n)
 
         def own(b):
             tt(row("Y1H", b, 512), V("PS5"), C("POOL", b, 2048, 4), MAX)
-        n1 = len(VB) // 2
-        for b in VB[:n1]:
-            own(b)
-        for gg in PI[k]:
-            ts(row("M", gg), grp(gg), V("PS2", 1, slice(8 + (gg ^ 2 * d), 9 + (gg ^ 2 * d))), None, EQU)
-        for i in range(4):
-            act(row("MAF", i), row("M", PI[k][i]))
-        for i in range(4):
-            for c in (0, 1):
-                mm(V("PS4", slice(i, 8, 4), slice(0, 24)), row("M", PI[k][i]), V("IDX", c, ALL, i, slice(0, 24)), c == 0, c == 1)
-        for gg in PI[k]:
-            mm(bank("PS3", 256 + 16 * gg, 272 + 16 * gg), row("M", gg), row("CS", gg ^ 2 * d, 16), True, True)
-        for b in VB[n1:]:
-            own(b)
-        vcopy(V("CSM"), bank("PS3", 256, 384))
-        mm(V("PS0"), V("CSM"), V("E4"), True, True)
-        KEY = bank("PS3", 0, 128)
-        mm(KEY, V("IB"), V("QK"), True, False)
-        for b in SB:
-            mm(V("PS3", slice(0, 8), slice(b, 16, 4)), C16, V("BX", k, ALL, slice(b, 16, 4)), False, False)
-        RB = V("PS5", slice(0, 4))
-        mm(RB, V("IB"), V("FQ"), True, False)
-        mm(RB, V("IBP"), V("FN"), False, False)
 
         def keys(name, w, n, b, last=False):
             for j in range(4):
                 mm(V("PS3", slice(0, 8), 4 * j + b), C(name, 512 * n + j, 512 * n + 512, 4), V(w, k), False, last and j == 3)
+        n1 = len(VB) // 2
+        for b in VB[:n1]:
+            own(b)
+        mm(bank("PS3", 0, 128), V("IB"), V("QK"), True, False)
+        for b in SB:
+            mm(V("PS3", slice(0, 8), slice(b, 16, 4)), C16, V("BX", k, ALL, slice(b, 16, 4)), False, False)
+        for b in VB[:n1]:
+            keys("Y1H", "BP3", b, b)
+        for n in range(4 if MT else 8):
+            ts(row("M", n), grp(n), V("PS2", 1, slice(8 + (n ^ 4), 9 + (n ^ 4))), None, EQU)
+            if MT:
+                mm(grp(4 + n), row("M", n), V("IB"), True, True)
+        if MT:
+            act(row("M", 1, 512), V("PS1"))
+            far(len(SB) - 1)
+        act(V("MAF"), row("M", 0, 512))
+        for i in range(4):
+            for c in (0, 1):
+                mm(V("PS4", slice(i, 8, 4), slice(0, 24)), row("M", i), V("IDX", c, ALL, i, slice(0, 24)), c == 0, c == 1)
+        for n, gg in enumerate(PI[k]):
+            if n == 4 and MT and len(SB) > 1:
+                keys("Y1", "BP1", 0, SB[0])
+            mm(bank("PS2", 256 + 16 * gg, 272 + 16 * gg), row("M", n), row("CS", gg ^ 2 * d, 16), True, True)
+        for b in VB[n1:]:
+            own(b)
 
         def same(r):
             tt(row("EQ", r), V("PS4", slice(0, 8), slice(r, r + 16)), V("IDO"), EQU)
+
+        def flags(r):
             for h in (0, 1):
                 e = row("EQ", 2 * r + h, 64)
                 mm(bank("PS3", 0, 64), V("IBN"), e, False, False)
                 mm(V("PS5", slice(0, 4), slice(r + 8 * h, r + 8 * h + 16)), V("IBP"), e, False, False)
-        for b in VB:
-            keys("Y1H", "BP3", b, b)
         for r in range(EQ0):
             same(r)
+        vcopy(V("CSM"), bank("PS2", 256, 384))
+        mm(V("PS0"), V("CSM"), V("E4"), True, True)
+        RB = V("PS5", slice(0, 4))
+        mm(RB, V("IB"), V("FQ"), True, False)
+        mm(RB, V("IBP"), V("FN"), False, False)
+        for b in VB[n1:]:
+            keys("Y1H", "BP3", b, b)
+        for r in range(EQ0, EQ1):
+            same(r)
+        for r in range(EQ1):
+            flags(r)
+        todo = list(range(1 if MT and len(SB) > 1 else 0, len(SB)))
         for b in range(4):
             if b == 3:
-                for r in range(EQ0, 8):
+                for r in range(EQ1, 8):
                     same(r)
+                    flags(r)
             tt(row("Y2", b, 512), V("PS0"), C("POOL", b, 2048, 4), MAX)
-            if b < len(SB):
-                keys("Y1", "BP1", b, SB[b])
+            if b < len(todo):
+                keys("Y1", "BP1", todo[b], SB[todo[b]])
             keys("Y2", "BP2", b, b, b == 3)
         vcopy(V("K1"), bank("PS3", 64, 128))
         tt(side_of("SRA", 0), bank("PS3", 0, 64), C("QBIG", 0, 64), MAX)
         for i in range(4):
             mm(V("PS5", i, slice(0, 16)), row("MAF", i), row("K1", i, 16), False, i == 3)
+        if k == 0:
+            tt(V("q0"), V("q0"), V("q1"), ADD)
+            vcopy(V("ILST"), V("q0"))
         tt(V("T1"), V("PS5", slice(0, 4), slice(0, 16)), C("QBIG", 64, 128), MIN)
         tt(side_of("SRA", 1), V("PS5", slice(0, 4), slice(16, 32)), V("T1"), MAX)
         mm(bank("PS3", 256, 384), V("IB"), V("DB"), True, False)
         for i in range(4):
-            mm(V("PS3", slice(16 + i, 24, 4)), row("M", PI[k][i]), V("TCC"), False, i == 3)
+            mm(V("PS3", slice(16 + i, 24, 4)), row("M", i), V("TCC"), False, i == 3)
         LP = bank("PS2", 384, 512)
         mm(LP, V("T16", min(k, 1)), V("IB"), True, False)
         if k == 0:
@@ -551,20 +605,30 @@ def rank_program(g, core, T, topo):
                 mm(bank("PS7", 0, 256), C("ZQ", 96 - 32 * c, 224 - 32 * c), V("PT", n // 4, ALL, slice(64 * c, 64 * c + 64)),
                    False, n == 7)
         else:
-            def part(o):
-                for a, b, bk in ((0, 512, "PS0"), (512, NV, "PS1"), (NV, 1024, YB[o])):
-                    if b > a:
-                        out = bank(bk, 0, b - a)
-                        for n, (w, nm) in enumerate((("IBQ", "X0"), ("IBQ", "H0"), ("IBH", "H1"))):
-                            mm(out, V(w), C(nm, 1024 * o + a, 1024 * o + b), n == 0, n == 2 and b <= NV)
-                        if b <= NV:
-                            act(C("PP", 1024 * o + a, 1024 * o + b), out)
-            for o in range(nrank):
+            def part(o, h):
+                for n, (w, nm) in enumerate((("IBQ", "X0"), ("IBQ", "H0"), ("IBH", "H1"))):
+                    mm(V(YB[o] if h else "PS%d" % (o % 2)), V(w), row(nm, 2 * o + h, 512), n == 0, n == 2 and not h)
+
+            def prey(o):
                 sgather(row("H%d" % (k - 1), o, 1024), V("TAB"), row("PREYX", o, 64))
-                if k == 2 and o > 0:
-                    part(o - 1)
+
+            def keep(o):
+                act(row("PP", o, 512), V("PS%d" % (o % 2)))
+            for o in range(3):
+                prey(o)
             if k == 2:
-                part(nrank - 1)
+                part(0, 0)
+                part(1, 0)
+                keep(0)
+            prey(3)
+            if k == 2:
+                part(0, 1)
+                keep(1)
+                part(2, 0)
+                part(1, 1)
+                part(3, 0)
+                keep(2)
+                keep(3)
         for s, kk, a, b in ((1, 2, "SRA", "SRB"), (2, 4, "SRB", "SRA"), (1, 4, "SRA", "SRB"),
                             (4, 8, "SRB", "SRA"), (2, 8, "SRA", "SRB"), (1, 8, "SRB", "SRA")):
             for kv in (0, 1):
@@ -594,7 +658,7 @@ def rank_program(g, core, T, topo):
         for c in (1, 0):
             for i in range(4):
                 o = 16 * PI[k][4 + i]
-                mm(LP, V("ZB", 4 * c + i, slice(112 - o, 240 - o)), row("M", PI[k][4 + i]), False, False)
+                mm(LP, V("ZB", 4 * c + i, slice(112 - o, 240 - o)), row("M", 4 + i), False, False)
         ts(C("BB", 0, 64), side_of("SI", 0), 4, 1, SHR, AND)
         ts(C("QA", 0, 64), side_of("SI", 0), 31, None, AND)
         tt(V("ZA", zv, za), C("BB", 0, 64), bank("PS3", 256, 320), MUL)
@@ -602,98 +666,129 @@ def rank_program(g, core, T, topo):
         for c in (0, 1):
             mm(LP, V("ZA", zv + c), V("IB"), False, c == 1)
         vcopy(V("LST"), LP)
+        if k == 2:
+            part(2, 1)
+            part(3, 1)
         for h in (0, 1):
             vgather(row("TAB", 2 * h, 512), V("POOL"), row("LST", 2 * h, 32))
             sgather(row("TAB", 2 * h + 1, 512), V("POOL"), row("LST", 2 * h + 1, 32))
-            swap("dtab%d%d" % (h, k), ("TAB", 4096 + 1024 * h), ("TAB", 1024 * h), 2, 1024)
-        pbk = ("PS0", "PS1", "PS4", "PS5", "PS6", "PS7", "PS3", "PS2") if k < 2 else ("PS0", "PS1", "PS3", "PS2") * 2
-        jobs = [(e, i) for i in range(4) for e in (1, 3)]
+            for e in CFG["DE"] if k < 2 else ():
+                swap("dtab%d%d" % (h, k), ("TAB", 2048 * e + 1024 * h), ("TAB", 1024 * h), e, 1024)
+            if k < 2 and CFG["CPD"]:
+                a, b = 1024 * h, min(PV, 1024 * h + 1024)
+                dma("y", "dtab%d%d" % (h, k), C("OWN", a, b), C("TAB", a, b))
+        pbk = ("PS0", "PS1", "PS4", "PS5", "PS6", "PS7", "PS3", "PS2")
+        jobs = [(e, i) for i in range(4) for e in (1, 2, 3) if e not in CFG["DE"]]
 
         def turn(n):
             mm(V(pbk[n]), V("PX", jobs[n][0]), row("TAB", jobs[n][1], 512), True, True)
 
-        def land(n, scalar=False):
+        def land(n, scalar):
             dst = row("TAB", 4 * jobs[n][0] + jobs[n][1], 512)
-            if n % 2 or scalar:
+            if scalar:
                 act(dst, V(pbk[n]))
             else:
                 vcopy(dst, V(pbk[n]))
+
+        def info(a):
+            vgather(C(inf[k + 1], 0, a), V(inf[k]), C("LST", 0, a // 16))
+            sgather(C(inf[k + 1], a, 2048), V(inf[k]), C("LST", a // 16, 128))
         if k < 2:
-            for n in range(8):
+            for n in range(len(jobs)):
                 turn(n)
-            vgather(C(inf[k + 1], 0, 1024), V(inf[k]), C("LST", 0, 64))
-            sgather(C(inf[k + 1], 1024, 2048), V(inf[k]), C("LST", 64, 128))
+            info(CFG["IA"])
             swap("dinf%d" % (k + 1), (inf[k + 1], 2048), (inf[k + 1], 0), DS[k + 1], 2048)
-            land(0)
-            land(7)
+            if len(jobs) == 8:
+                land(7, True)
             as_list(inf[k + 1], "WB", bank("PS2", 0, 128))
-            for n in (1, 6, 2, 3, 5):
-                land(n)
-            vcopy(C("V16", 0, PV), C("TAB", 0, PV))
+            rest = list(range(min(len(jobs), 7)))
+            nv = CFG["LV"]
+            for n in rest[:nv]:
+                land(n, False)
+            for n in rest[:nv - 1:-1]:
+                land(n, True)
+            if not CFG["CPD"]:
+                vcopy(C("OWN", 0, PV), C("TAB", 0, PV))
             ts(V("PAL"), bank("PS2", 0, 128), C("COL", 1, 2), None, ADD)
-            land(4, True)
             for j in range(16):
                 mm(V("PS3", slice(16, 28), j), C(inf[k + 1], j, 2048, 16), V("SEL", k + 1), True, True)
-            ranks_open()
             w = (2048 - PV) // 2
-            ttg(C("SU", 0, PV), V("TAB"), C("PAL", 0, PV // 16), C("V16", 0, PV), ADD)
+            for h in (0, 1):
+                a = PV + w * h
+                mm(bank("PS%d" % (6 + h), 0, w), V("IB"), C("TAB", a, a + w), True, False)
+            ranks_open()
+            ttg(C("SU", 0, PA), V("TAB"), C("PAL", 0, PA // 16), C("OWN", 0, PA), ADD)
             for h in (0, 1):
                 a = PV + w * h
                 sgather(row("REP", h, w), V("TAB"), C("PAL", a // 16, (a + w) // 16))
-                mm(bank("PS%d" % (6 + h), 0, w), V("IB"), C("TAB", a, a + w), True, False)
-            for h in (0, 1):
                 mm(bank("PS%d" % (6 + h), 0, w), V("IB"), row("REP", h, w), False, True)
-            ts(C("V16", 0, PV), C("SU", 0, PV), 0.5, 1536.25, MUL, ADD)
+            ts(C("V16", 0, PA), C("SU", 0, PA), 0.5, 1536.25, MUL, ADD)
+            sums("V16", 0, PA // 16)
+            ttg(C("SU", PA, PV), V("TAB"), C("PAL", PA // 16, PV // 16), C("OWN", PA, PV), ADD)
+            ts(C("V16", PA, PV), C("SU", PA, PV), 0.5, 1536.25, MUL, ADD)
             for h in (0, 1):
                 a = PV + w * h
                 act(C("V16", a, a + w), bank("PS%d" % (6 + h), 0, w), scale=0.5, bias=1536.25)
+            act(C("POOL", PC, 2048), C("V16", PC, 2048), bias=-1536.0)
             ids_out(lambda a, b: V("PS3", slice(16, 24), slice(a, b)), V("PS3", slice(24, 28)))
         else:
-            for n in range(8):
-                turn(n)
-                land(n)
             HALF = 1520.4375
+            CV = CFG["CV"]
 
-            def place(o, a, b):
-                if o == me:
-                    return C("RCV", 1024 * me + a, 1024 * me + b)
-                return C("OUT", 1024 * order.index(o) + a, 1024 * order.index(o) + b)
-
-            def store(q, n):
-                ts(C("YXO", 1024 * q, 1024 * q + 512), C("RCV", 1024 * q, 1024 * q + 512), -1408.0, None, ADD)
-                act(C("YXO", 1024 * q + 512, 1024 * q + 1024), C("RCV", 1024 * q + 512, 1024 * q + 1024), bias=-1408.0)
-                for c in range(4):
-                    dma("y", "dyx%d" % n, None, row("YXO", q, 1024, ps=pb(c)), ext_out=T.yx[32 * q:32 * q + 32, 1024 * c:1024 * c + 1024])
-
-            def shut(o):
-                act(place(o, NV, 1024), bank(YB[o], 0, NS), scale=0.5, bias=HALF)
-                if o != me:
-                    send_to(o, "aout%d" % me, "lout", row("OUT", order.index(o), 1024), row("RCV", me, 1024))
-                else:
-                    store(me, 0)
-            last = [off[0], off[1], me] + on
-            for n, o in enumerate(last):
-                ttg(C("SU", 1024 * (n % 2), 1024 * (n % 2) + NV), V("TAB"), C("PREYX", 64 * o, 64 * o + NV // 16),
-                    C("PP", 1024 * o, 1024 * o + NV), ADD)
-                sgather(row("REP", n, NS), V("TAB"), C("PREYX", 64 * o + NV // 16, 64 * o + 64))
-                mm(bank(YB[o], 0, NS), V("IB"), row("REP", n, NS), False, True)
-                ts(place(o, 0, NV), C("SU", 1024 * (n % 2), 1024 * (n % 2) + NV), 0.5, HALF, MUL, ADD)
-                if n > 0:
-                    shut(last[n - 1])
-            shut(last[-1])
-            vgather(C(inf[3], 0, 1024), V(inf[2]), C("LST", 0, 64))
-            sgather(C(inf[3], 1024, 2048), V(inf[2]), C("LST", 64, 128))
-            as_list(inf[3], "WY", bank("PS2", 0, 128))
+            last = order + [me]
+            wins = [("TAB", 2048), ("TAB", 4096), ("TAB", 6144), ("OWN", 0)]
+            NPE = CFG["NPE"]
             for r in others:
                 expect("aout%d" % r, NB, [row("RCV", r, 1024)])
             expect("ayl", NB * (nrank - 1), [row("YL", r) for r in others])
-            store(off[0], 1)
-            vcopy(row("YL", me), bank("PS2", 0, 128))
-            send_all("ayl", "lyl", row("YL", me))
-            store(off[1], 2)
-            store(on[0], 3)
-            for q in range(nrank):
-                dma("s", "dyl", None, row("YL", q, ps=pb(me)), ext_out=T.yl[32 * q:32 * q + 32, :])
+
+            def spread_out(n):
+                for i in range(4):
+                    mm(V("PS%d" % i), V("PX", 2 * n), row("TAB", i, 512), True, True)
+                for i in range(4):
+                    (act if i % 2 else vcopy)(row("TAB", 4 * n + 4 + i, 512), V("PS%d" % i))
+            for n in range(NPE, nrank):
+                for c in range(4):
+                    dma("y", "dwin%d" % n, C(wins[n][0], wins[n][1], wins[n][1] + 2048, ps=pb(c)), C("TAB", 0, 2048, ps=pb(last[n])))
+
+            def lists():
+                info(CFG["IV"])
+                as_list(inf[3], "WY", bank("PS2", 0, 128))
+
+            def lists_out():
+                vcopy(row("YL", me), bank("PS2", 0, 128))
+                send_all("ayl", "lyl", row("YL", me))
+
+            def lists_store():
+                for q in range(nrank):
+                    dma("y", "dyl", None, row("YL", q, ps=pb(me)), ext_out=T.yl[32 * q:32 * q + 32, :])
+
+            def fetch(n):
+                o, w = last[n], C(wins[n][0], wins[n][1], wins[n][1] + 2048)
+                ttg(row("SU", n, 512), w, row("PREYL", 2 * o, 32), row("PP", o, 512), ADD)
+                sgather(row("REP", n, 512), w, row("PREYL", 2 * o + 1, 32))
+                mm(V(YB[o]), V("IB"), row("REP", n, 512), False, True)
+
+            def shut(n):
+                o = last[n]
+                nm, a = ("RCV", 2 * me) if o == me else ("OUT", 2 * n)
+                ts(row(nm, a, 512), row("SU", n, 512), 0.5, HALF, MUL, ADD)
+                act(row(nm, a + 1, 512), V(YB[o]), scale=0.5, bias=HALF)
+                if o != me:
+                    send_to(o, "aout%d" % me, "lout", row("OUT", n, 1024), row("RCV", me, 1024))
+
+            def store(n):
+                q = last[n]
+                ts(C("YXO", 1024 * q, 1024 * q + CV), C("RCV", 1024 * q, 1024 * q + CV), -1408.0, None, ADD)
+                act(C("YXO", 1024 * q + CV, 1024 * q + 1024), C("RCV", 1024 * q + CV, 1024 * q + 1024), bias=-1408.0)
+                for c in range(4):
+                    dma("y", "dyx%d" % n, None, row("YXO", q, 1024, ps=pb(c)), ext_out=T.yx[32 * q:32 * q + 32, 1024 * c:1024 * c + 1024])
+            steps = {"w": spread_out, "f": fetch, "s": shut, "c": store}
+            for word in CFG["END"].split():
+                if word[0] in steps:
+                    steps[word[0]](int(word[1]))
+                else:
+                    {"L": lists, "O": lists_out, "Y": lists_store}[word]()
     for sem in sorted(tot):
         if know["g"].get(sem, 0) < tot[sem]:
             g.wait_ge(T.sem[sem], tot[sem])

@@ -3,8 +3,9 @@ from concourse.mybir import AluOpType, ActivationFunctionType
 
 BF, FH, FF, I4, U2 = "bfloat16", "float16", "float32", "int32", "uint16"
 S6 = [128, 8, 2, 2, 2, 2]
-CFG = {"NS1": 2, "PV": 1152, "PA": 896, "PC": 1152, "EQ0": 5, "EQ1": 8, "MT": 1, "DE": (2,), "CPD": 0, "LV": 3,
-       "CV": 640, "IV": 1280, "IA": 1152, "NPE": 1, "END": "w0 f0 s0 f1 f2 s1 s2 L c0 f3 O c2 s3 c1 c3 Y"}
+CFG = {"PV": 1088, "PA": 896, "PC": 1088, "GS": 1, "N0": 4, "N1": 8, "NO": 12, "DE": ((2, 3, 1), ()), "CPD": 1, "LV": 3,
+       "CV": 640, "IV": 640, "IA": 1024, "LO": (0, 1, 2, 3), "NPE": 1, "HP": 0, "HO": 0, "OA": 0, "LEAD": 2,
+       "WH": 2, "LA": 1, "END": "w0 f0 l0 s0 f1 f2 s1 s2 l1 L c0 f3 O c2 s3 c1 c3 Y"}
 XZ = 13328
 _SB = {
     "SL": ([128, 128], I4), "PR": ([128, 256], I4), "LISTS": ([128, 512], U2), "LF": ([128, 512], FF), "OFF": ([128, 512], U2),
@@ -16,29 +17,30 @@ _SB = {
     "H0": ([128, 4096], BF), "H1": ([128, 4096], BF), "REP": ([128, 2048], BF), "PP": ([128, 2048], FH), "OWN": ([128, 2048], BF),
     "SU": ([128, 2048], FH), "V16": ([128, 2048], FH), "OUT": ([128, 3072], FH), "RCV": ([128, 4096], FH),
     "YXO": ([128, 4096], FF), "YL": ([128, 512], FF),
-    "C16": ([128, 128], FH), "CS": ([128, 128], FH), "CSM": ([128, 128], FH), "E4": ([128, 512], BF), "E4N": ([128, 512], BF),
-    "G": ([128, 1024], BF), "M": ([128, 1024], BF), "MAF": ([128, 512], FF),
-    "IDO": ([128, 8, 16], FF), "IDX": ([128, 2, 2, 4, 32], BF), "PAL": ([128, 128], U2),
-    "Y1": ([128, 1024], FF), "Y1H": ([128, 2048], FH), "Y2": ([128, 2048], FH), "EQ": ([128, 1024], BF),
-    "K1": ([128, 64], FF), "T1": ([128, 64], FF),
+    "C16": ([128, 128], FH), "CSZ": ([128, 8, 48], FH), "CB": ([128, 8], FF), "B8P": ([128, 8], BF),
+    "IBS": ([128, 128], BF), "IBM": ([128, 128], BF),
+    "G": ([128, 1024], BF), "M": ([128, 1024], BF), "M64": ([128, 512], BF), "QKS": ([128, 128], BF),
+    "IDO": ([128, 4, 2, 16], FF), "IDX": ([128, 8, 2, 16], BF), "PAL": ([128, 128], U2),
+    "Y1": ([128, 1024], FF), "Y1H": ([128, 2048], FH), "Y2": ([128, 2048], FH), "EQ": ([128, 32, 2, 2, 8], BF),
+    "K1": ([128, 128], FH),
     "SRA": (S6, FF), "SRB": (S6, FF), "SI": (S6, I4), "QA": ([128, 128], I4), "BB": ([128, 128], I4),
-    "ZA": ([128, 4, 4, 32], BF), "ZB": ([128, 8, 240], BF), "LST": ([128, 128], U2),
+    "ZA": ([128, 4, 4, 32], BF), "ZB": ([128, 8, 48], BF), "LST": ([128, 128], U2),
     "ONE": ([128, 128], BF), "IB": ([128, 128], BF), "IF": ([128, 128], FF), "BCQ": ([128, 128], FF), "TC": ([128, 1024], BF),
     "IBP": ([128, 128], BF), "IBN": ([128, 128], BF), "IBQ": ([128, 128], BF), "IBH": ([128, 128], BF),
     "PX": ([128, 4, 128], BF), "ZS": ([128, 224], BF), "ZQ": ([128, 224], BF), "ZF": ([128, 224], FF),
     "B8a": ([128, 8], BF), "B8": ([128, 8], BF), "B8N": ([128, 8], BF), "NBE": ([128, 1024], BF),
     "PCI": ([128, 1], I4), "pi": ([128, 4], I4), "P16": ([128, 1], FF), "COL": ([128, 8], FF), "WC": ([128, 16], FF),
     "T16": ([128, 2, 128], BF), "DB": ([128, 128], BF), "TCC": ([128, 32], BF), "QK": ([128, 128], BF),
-    "FQ": ([128, 4, 32], BF), "FN": ([128, 4, 32], BF), "QBIG": ([128, 128], FF), "NEG": ([128, 2], FF),
+    "QBIG": ([128, 128], FF), "NEG": ([128, 2], FF),
     "C32": ([128, 2, 64], BF), "bx": ([128, 64], BF), "BX": ([128, 3, 8, 16], BF),
     "BP1": ([128, 3, 8], FF), "BP2": ([128, 3, 8], FH), "BP3": ([128, 3, 8], FH),
-    "B8K": ([128, 2, 8], BF), "SEL": ([128, 3, 12], BF), "WB": ([128, 144], BF), "WY": ([128, 144], BF),
+    "B8K": ([128, 8], BF), "BC": ([128, 4, 128], BF), "SEL": ([128, 3, 12], BF), "WB": ([128, 144], BF), "WY": ([128, 144], BF),
 }
 SCRATCH = {k: ("sbuf", s, d) for k, (s, d) in _SB.items()}
-_PS = {"PS%d" % i: ([128, 16, 32] if i in (4, 5) else [128, 32, 16], FF) for i in range(8)}
+_PS = {"PS%d" % i: ([128, 64, 2, 2, 2] if i in (4, 5) else [128, 32, 16], FF) for i in range(8)}
 for _k, (_s, _d) in _PS.items():
     SCRATCH[_k] = ("psum", _s, _d)
-SEMAPHORES = (["cv", "cs", "ct", "cg", "dsl", "dpr", "dcp", "dpw", "dyl", "ali", "apt", "ayl", "lli", "lpt", "lx", "lout", "lyl"]
+SEMAPHORES = (["cv", "cs", "ct", "cg", "dsl", "dpr", "dcp", "dpw", "dyl", "ali", "apt", "ayl", "lli", "lpt", "lx", "lout", "lyl", "hpt0", "hpt1", "hout"]
               + [n + str(i) for n in ("dx", "ax", "aout", "dyx", "dwin") for i in range(4)]
               + [n + str(k) for n in ("dpool", "dinf", "dtab0", "dtab1") for k in range(3)])
 
@@ -47,18 +49,45 @@ MAX, MIN = AluOpType.max, AluOpType.min
 GT, GE, LT, EQU, NE = AluOpType.is_gt, AluOpType.is_ge, AluOpType.is_lt, AluOpType.is_equal, AluOpType.not_equal
 SHR, AND = AluOpType.arith_shift_right, AluOpType.bitwise_and
 COPY, RELU, ABS = ActivationFunctionType.Copy, ActivationFunctionType.Relu, ActivationFunctionType.Abs
-IDENT = ActivationFunctionType.Identity
+IDENT, SIGN = ActivationFunctionType.Identity, ActivationFunctionType.Sign
 ALL = slice(None)
 BIG = 4194304.0
 DS = (1, 2, 3)
 
 
+def peers(r, cores, topo):
+    c = cores[r]
+    off = [o for o in range(len(cores)) if topo.chip(cores[o]) != topo.chip(c)]
+    off.sort(key=lambda o: topo.die(cores[o]) != topo.die(c))
+    on = [o for o in range(len(cores)) if o != r and o not in off]
+    aide = [a for a in topo.cores_of(c) if a not in cores and topo.die(a) == topo.die(c) and topo.may_write(a, cores[off[0]])]
+    return off, on, aide[0]
+
+
+def aide_program(g, core, T, topo, r):
+    cores = list(T.cores)
+    off = peers(r, cores, topo)[0]
+    es = topo.engines(core, cores[off[0]])
+    jobs = [("hpt%d" % c, "apt", off, T.PT[:, c, r, :], T.PT[:, c, r, :]) for c in (0, 1)] if CFG["HP"] else []
+    jobs += [("hout", "aout%d" % r, off[1:], T.OUT[:, 1024:2048], T.RCV[:, 1024 * r:1024 * r + 1024])] if CFG["HO"] else []
+    for mine, theirs, rs, src, dst in jobs:
+        g.wait_ge(T.sem[mine], len(topo.engines(cores[r], core)) if mine == "hout" else len(es))
+        ids = [DstId(rid=topo.addr(cores[o])[0], pnc=topo.addr(cores[o])[1]) for o in rs]
+        g.remote_dma_fused([RemoteDMATransfer(dst_ids=ids, dma_engine_mask=topo.mask(core, cores[off[0]]), remote_sem=T.sem[theirs],
+                                              srcs=[src], dsts=[dst for o in rs], alu_op=0)], local_sem=T.sem["lout"])
+    if jobs:
+        g.wait_ge(T.sem["lout"], len(es) * len(jobs))
+
+
 def rank_program(g, core, T, topo):
     me = T.rank_of(core)
-    if me is None:
-        return
     cores = list(T.cores)
     nrank = len(cores)
+    if me is None:
+        for r in range(nrank):
+            if peers(r, cores, topo)[2] == core:
+                aide_program(g, core, T, topo, r)
+        return
     Q = {"v": g.vector, "s": g.scalar, "t": g.tensor, "g": g, "y": g.sync}
     know = {q: {} for q in Q}
     tot = {}
@@ -103,6 +132,7 @@ def rank_program(g, core, T, topo):
                         if oq != q:
                             evs.append(d[oq])
                             del d[oq]
+                    evs += [e[1] for e in log.get(r["n"] + "w", ()) if e[0] & r["m"]]
                     continue
                 for e in log.get(r["n"], ()):
                     if e[0] & r["m"] and e[1] & r["p"] and not (kind == "r" and e[2] == "r"):
@@ -114,6 +144,9 @@ def rank_program(g, core, T, topo):
             for r in lst:
                 if r["n"] in _PS:
                     log.setdefault(r["n"], {})[q] = ev
+                    if kind == "w":
+                        old = [e for e in log.get(r["n"] + "w", ()) if e[0] & ~r["m"]]
+                        log[r["n"] + "w"] = old + ([(r["m"], ev)] if q != "t" else [])
                     continue
                 old = log.get(r["n"], [])
                 if kind == "w":
@@ -146,15 +179,14 @@ def rank_program(g, core, T, topo):
         note("net", [], outs, (sem, tot[sem], {sem: tot[sem]}))
 
     others = [r for r in range(nrank) if r != me]
-    off = [r for r in others if topo.chip(cores[r]) != topo.chip(core)]
-    off.sort(key=lambda r: topo.die(cores[r]) != topo.die(core))
-    on = [r for r in others if r not in off]
+    off, on, aide = peers(me, cores, topo)
     e_off = list(topo.engines(core, cores[off[0]]))
     e_on = [e for e in topo.engines(core, cores[on[0]]) if e not in e_off]
+    e_all = e_off + e_on
     NB = len(e_off)
 
     def did(r):
-        rid, pid, _ = topo.addr(cores[r])
+        rid, pid, _ = topo.addr(aide if r is None else cores[r])
         return DstId(rid=rid, pnc=pid)
 
     def send(parts, lsem):
@@ -223,7 +255,7 @@ def rank_program(g, core, T, topo):
         return slice(n * b, n * b + n)
 
     def bank(name, a=0, b=512, ps=ALL):
-        w = SCRATCH[name][1][2]
+        w = 512 // SCRATCH[name][1][1]
         if b - a < w:
             return V(name, a // w, slice(a % w, a % w + b - a), ps=ps)
         return V(name, slice(a // w, b // w), ps=ps)
@@ -246,7 +278,7 @@ def rank_program(g, core, T, topo):
     AS = [[r for r in range(nrank) if r < r ^ d] for d in DS]
     BS = [[r ^ d for r in a] for a, d in zip(AS, DS)]
     PI = [[2 * r + w for r in a + b for w in (0, 1)] for a, b in zip(AS, BS)]
-    NS1, PV, PA, PC, EQ0, EQ1, MT = (CFG[n] for n in ("NS1", "PV", "PA", "PC", "EQ0", "EQ1", "MT"))
+    PV, PA, PC, GS, N0, N1, NO = (CFG[n] for n in ("PV", "PA", "PC", "GS", "N0", "N1", "NO"))
 
     order = off + on
     dma("y", "dsl", V("SL"), None, ext_in=T.sl[:, :])
@@ -263,8 +295,10 @@ def rank_program(g, core, T, topo):
     afs(V("B8a"), C("ONE", 0, 8), [[-16, 8]], GE, 0, 1)
     afs(V("B8"), V("B8a"), [[16, 8]], GE, 15, -1)
     vcopy(row("LISTS", me), V("SL"))
-    send_all("ali", "lli", row("LISTS", me))
+    send([("ali", off, e_off, row("LISTS", me), row("LISTS", me))], "lli")
     for n, q in enumerate(order):
+        if n == CFG["LA"]:
+            send_to(on[0], "ali", "lli", row("LISTS", me), row("LISTS", me))
         send_to(q, "ax%d" % me, "lx", leaving(n), xcol(me))
     expect("ali", NB * (nrank - 1), [row("LISTS", r) for r in others])
     for r in others:
@@ -273,9 +307,8 @@ def rank_program(g, core, T, topo):
     def zeros(n):
         return C("XW", 1040, 1040 + n)
     act(C("XW", 5136, 8208), zeros(3072))
-    fill(V("E4N"), 1.0 / 16)
     fill(V("C32", 0), 32.0)
-    fill(V("C32", 1), -32.0)
+    fill(V("C32", 1), -0.5)
     fill(C("XW", 0, 16), 0.0)
     fill(C("XW", XZ, XZ + 16), 0.0)
     ts(C("pi", 0, 1), V("PCI"), 15, None, AND)
@@ -304,9 +337,12 @@ def rank_program(g, core, T, topo):
     ts(V("w2"), V("PR"), 127, None, AND)
     vcopy(V("PT", 0, me), V("w1"))
     vcopy(V("PT", 1, me), V("w2"))
-    afs(V("E4"), V("E4N"), [[-1, 128], [0, 4]], EQU, 0, 1)
     for c in (0, 1):
-        send_all("apt", "lpt", V("PT", c, me))
+        if CFG["HP"]:
+            send([("hpt%d" % c, [None], e_on, V("PT", c, me), V("PT", c, me))], "lpt")
+            send_to(on[0], "apt", "lpt", V("PT", c, me), V("PT", c, me))
+        else:
+            send_all("apt", "lpt", V("PT", c, me))
     expect("apt", 2 * NB * (nrank - 1), [V("PT", ALL, r) for r in others])
     fill(V("ZS"), 0.0)
     for c in range(4):
@@ -319,11 +355,13 @@ def rank_program(g, core, T, topo):
     for nm in ("ZF", "ZQ"):
         act(V(nm), zeros(224))
         act(C(nm, 96, 128), row("IB", me, 32))
+    act(V("CSZ"), zeros(384))
+    act(V("ZB"), zeros(384))
+    act(V("IBS"), V("IB"), scale=1.0 / 16)
+    act(V("IBM"), V("IB"), scale=-1.0 / 16)
+    act(V("B8P"), V("B8"), scale=128.0)
     act(V("IBP"), V("IB"), scale=2 * BIG)
     act(V("IBN"), V("IB"), scale=-2 * BIG)
-    act(V("FQ"), zeros(128))
-    act(V("FN"), zeros(128))
-    act(V("FN", ALL, slice(16, 32)), zeros(64), bias=-0.5)
     act(V("IDT", 3), zeros(1024), IDENT, bias=V("P16"))
 
     def weights(k):
@@ -346,12 +384,12 @@ def rank_program(g, core, T, topo):
         mm(bank("PS3", 384, 512), C("ZF", 96 - 32 * r, 224 - 32 * r), row("LF", r), r == 0, r == nrank - 1)
 
     def ids_out(src, full):
-        act(V("IDX", ALL, 0, ALL, slice(0, 16)), src(0, 16))
-        act(V("IDX", ALL, 1, ALL, slice(8, 24)), src(0, 16))
-        act(V("IDX", ALL, 0, ALL, slice(16, 24)), src(0, 8))
-        act(V("IDX", ALL, 1, ALL, slice(0, 8)), src(8, 16))
+        act(V("IDX", ALL, 0), src(0, 16))
+        act(V("IDX", ALL, 1, slice(0, 8)), src(8, 16))
+        act(V("IDX", ALL, 1, slice(8, 16)), src(0, 8))
         for h in (0, 1):
-            act(V("IDO", slice(4 * h, 4 * h + 4)), full)
+            act(V("IDO", ALL, h), full)
+
 
     def ranks_open():
         for h in (0, 1):
@@ -365,12 +403,12 @@ def rank_program(g, core, T, topo):
         zs = C("ZS", 96 - 32 * r, 224 - 32 * r)
         if n < nrank - 1:
             columns(askers[n + 1])
+            if n == nrank - 2:
+                ranks_open()
             vgather(row("TAB", 2 * r, 1024), win, row("OFF", 2 * r, 64))
             sgather(row("TAB", 2 * r + 1, 1024), win, row("OFF", 2 * r + 1, 64))
             for i, b in enumerate(YB):
                 mm(V(b), zs, row("TAB", 4 * r + i, 512), n == 0, False)
-            if n == nrank - 2:
-                ranks_open()
         else:
             for i, b in enumerate(YB):
                 (sgather if i % 2 else vgather)(row("TAB", 4 * r + i, 512), win, row("OFF", 4 * r + i, 32))
@@ -380,20 +418,20 @@ def rank_program(g, core, T, topo):
             ts(row("POOL", i, 512), V(b), -128.0, None, ADD)
         else:
             act(row("POOL", i, 512), V(b), bias=-128.0)
-    act(V("E4N"), V("E4"), scale=-1.0)
     act(V("BP1", 0), V("BX", 0, ALL, 0), scale=16.0)
     act(V("BP2", 0), V("BX", 0, ALL, 0), scale=-16.0)
     act(V("BP3", 0), V("BX", 0, ALL, 0), scale=16.0)
-    act(V("FQ", ALL, slice(16, 32)), C("QK", 64, 128))
+    act(C("QKS", 0, 64), C("QK", 0, 64))
+    act(C("QKS", 64, 128), C("QK", 64, 128), scale=1.0 / 64)
     act(C("QBIG", 0, 64), C("QK", 0, 64), bias=-BIG)
     act(C("QBIG", 64, 128), C("QK", 64, 128), bias=BIG)
     vcopy(C("q0", 0, 64), bank("PS3", 320, 384))
-    vcopy(V("DI"), bank("PS3", 384, 512))
     ts(C("q1", 0, 64), C("q0", 0, 64), 16256, None, AND)
     ts(C("q1", 64, 128), C("q0", 0, 64), 127, None, AND)
     ts(C("WC", 0, 6), C("QK", 0, 6), V("P16"), None, EQU)
+    vcopy(V("DI"), bank("PS3", 384, 512))
     vcopy(V("IDS"), V("q1"))
-    ids_out(lambda a, b: V("IDS", ALL, slice(a, b)), bank("PS3", 256, 320))
+    ts(row("w1", 0), V("DI"), 15, None, AND)
     for c in range(4):
         for h in (0, 1):
             dma("y", "dpw", C("XW", 0, 16384, ps=slice(32 * c + 3 + h, 32 * c + 32, 16)), V("PT", h, ps=pb(me)))
@@ -410,36 +448,35 @@ def rank_program(g, core, T, topo):
         need("g", [("cg", tot["cg"], {})])
         iota(V("XOC", ps=pb(c)), [[4096 - 8192 * (c // 2), 2], [2048 - 4096 * (c % 2), 2], [0, 64]], 0, base=2048 * c)
 
-    def late_constants():
+    def late_constants(k):
         def w(i):
             return C("WC", i, i + 1)
-        act(V("ZA"), V("IDT", 1, slice(0, 2)))
-        for n in range(4):
-            act(V("ZB", slice(2 * n, 2 * n + 2)), V("IDT", 1, slice(0, 2), slice(0, 240)))
-        act(V("WB"), V("IDT", 1, 0, slice(0, 144)))
-        act(V("WY"), V("IDT", 1, 0, slice(0, 144)))
-        for out, a, s, b in ((6, 1, C("COL", 2, 3), 3), (7, 2, C("COL", 3, 4), 4), (8, 1, 8192.0, 5), (11, 1, 2.0, 2),
-                             (9, 2, 4096.0, 8), (12, 5, 4.0, 11), (13, 6, 1.0, 7), (10, 0, 16.0, 9), (15, 12, 256.0, 0)):
-            act(w(out), w(a), IDENT, bias=w(b), scale=s)
-        act(w(14), w(12), scale=256.0)
-        act(C("WB", 15, 128, 16), V("B8"), scale=w(13))
-        act(C("WY", 15, 128, 16), V("B8"), scale=w(10))
-        for e in (1, 3):
-            for b in range(4):
-                act(V("PX", e, pb(b)), row("IB", b ^ e, 32))
-        for k in (1, 2):
-            act(V("BP1", k), V("BX", k, ALL, 0), scale=16.0)
-            act(V("BP2", k), V("BX", k, ALL, 0), scale=-16.0)
-            act(V("BP3", k), V("BX", k, ALL, 0), scale=16.0)
-            act(V("B8K", k - 1), V("BX", k, ALL, 0), ABS, scale=1.0 / 32)
-        for k in (1, 2):
-            for c, (w, side) in enumerate(((0, 1), (14, 1), (15, 0))):
-                act(V("SEL", k, slice(4 * c, 4 * c + 4)), V("B8K", k - 1, slice(4 * side, 4 * side + 4)), scale=C("WC", w, w + 1))
-        for n in range(CFG["NPE"]):
-            for b in range(4):
-                act(V("PX", 2 * n, pb(b)), row("IB", order[n], 32))
-        act(V("IBQ"), V("IB"), scale=0.25)
-        act(V("IBH"), V("IB"), scale=0.5)
+        if k == 1:
+            act(V("ZA"), V("IDT", 1, slice(0, 2)))
+            act(V("WB"), V("IDT", 1, 0, slice(0, 144)))
+            for out, a, s, b in ((6, 1, C("COL", 2, 3), 3), (7, 2, C("COL", 3, 4), 4), (8, 1, 8192.0, 5), (11, 1, 2.0, 2),
+                                 (9, 2, 4096.0, 8), (12, 5, 4.0, 11), (13, 6, 1.0, 7), (10, 0, 16.0, 9), (15, 12, 256.0, 0)):
+                act(w(out), w(a), IDENT, bias=w(b), scale=s)
+            act(w(14), w(12), scale=256.0)
+            act(C("WB", 15, 128, 16), V("B8"), scale=w(13))
+            for e in (1, 2, 3):
+                for b in range(4):
+                    act(V("PX", e, pb(b)), row("IB", b ^ e, 32))
+        else:
+            act(V("WY"), V("IDT", 1, 0, slice(0, 144)))
+            for n in range(CFG["NPE"]):
+                for b in range(4):
+                    act(V("BC", n, pb(b)), row("IB", last[n], 32))
+            act(V("IBQ"), V("IB"), scale=0.25)
+            act(V("IBH"), V("IB"), scale=0.5)
+            act(C("WY", 15, 128, 16), V("B8"), scale=w(10))
+        act(V("B8K", slice(0, 4)), V("BX", k, slice(0, 4), 0), scale=1.0 / 32)
+        act(V("B8K", slice(4, 8)), V("BX", k, slice(4, 8), 0), scale=-2.0)
+        act(V("BP1", k), V("BX", k, ALL, 0), scale=16.0)
+        act(V("BP2", k), V("BX", k, ALL, 0), scale=-16.0)
+        act(V("BP3", k), V("BX", k, ALL, 0), scale=16.0)
+        for c, (i, side) in enumerate(((0, 1), (14, 1), (15, 0))):
+            act(V("SEL", k, slice(4 * c, 4 * c + 4)), row("B8K", side, 4), scale=w(i))
 
     def as_list(name, w, out):
         for j in range(16):
@@ -464,16 +501,28 @@ def rank_program(g, core, T, topo):
         tt(dl, lo, hi, MIN)
         tt(dh, lo, hi, MAX)
 
+    def rise(side, n):
+        s, first = ((1, 0), (2, 1), (1, 0), (4, 1), (2, 0), (1, 0), (8, 1), (4, 0), (2, 0), (1, 0))[n]
+        src, dst = ("SRA", "SRB") if n % 2 == 0 else ("SRB", "SRA")
+        ix = [slice(4 * side, 4 * side + 4)] + [ALL] * 4
+        lo, hi = list(ix), list(ix)
+        lo[bits[s] - 1], hi[bits[s] - 1] = 0, 1
+        if first:
+            hi[bits[s]:] = [slice(None, None, -1)] * (5 - bits[s])
+        for o, out, c in ((MIN, lo, 0), (MAX, hi, 1)):
+            tt(V("PS3", slice(0, 4), slice(c, 16, 2)) if side and n == 9 else V(dst, *out), V(src, *lo), V(src, *hi), o)
+
     def side_of(name, side):
         return V(name, slice(4 * side, 4 * side + 4))
 
     inf = ["INF0", "INF1", "INF0", "INF1"]
+    LEAD = CFG["LEAD"]
+    last = [(order + [me])[i] for i in CFG["LO"]]
+    FB = ("PS4", "PS5", "PS6", "PS7", "PS0", "PS1", "PS3", "PS2")
     def sums(src, a, b):
         for j in range(16):
             mm(V("PS2", slice(a // 8, b // 8), slice(0, 8)), V("IB"), C(src, 16 * a + j, 16 * b, 16), j == 0, j == 15)
 
-    SB = list(range(4 - NS1, 4))
-    VB = list(range(4 - NS1))
 
     for k, d in enumerate(DS):
         src = "POOL" if k == 0 else "V16"
@@ -483,120 +532,130 @@ def rank_program(g, core, T, topo):
         C16 = V("C16")
         if k > 0:
             ts(C("POOL", 0, PC), C("V16", 0, PC), -1536.0, None, ADD)
-        for b in SB[:1]:
-            mm(V(YB[b]), V("IB"), C(src, b, 2048, 4), True, False)
+        def mine(j, first):
+            out = bank(YB[2 + (j - NO) // 4], 128 * ((j - NO) % 4), 128 * ((j - NO) % 4) + 128)
+            if first:
+                mm(out, V("IB"), C(src, j, 2048, 16), (j - NO) % 4 == 0, False)
+            else:
+                mm(out, V("IBM"), C16, False, (j - NO) % 4 == 3 or j == 15)
+        for j in range(NO, min(NO + 4, 16)):
+            mine(j, True)
         ts(C16, V("PS2", slice(0, 16), slice(0, 8)), 0.0 if k == 0 else -24576.0, None, ADD)
         if k == 0:
-            ts(V("q1"), V("DI"), 15, None, AND)
-            ts(V("q0"), V("DI"), 4, None, SHR)
-            ts(V("q1"), V("q1"), 1024, None, MUL)
-        if k == 1:
-            for o in range(nrank):
-                ts(row("PREYL", o, 64), row("PREYX", o, 64), C("XOC", 64 * o, 64 * o + 1), None, SUB)
+            ts(row("w1", 1), V("DI"), 4, None, SHR)
+            ts(row("w2", 0), row("w1", 0), 1024, None, MUL)
+        mm(bank("PS5", 256, 384), V("IBS"), C16, True, True)
+        if GS:
+            mm(V("PS7", 31, slice(0, 8)), C16, V("B8P"), True, True)
+            act(V("CB"), V("PS7", 31, slice(0, 8)))
         mm(V("PS2", 0, slice(8, 16)), C16, V("B8N"), True, True)
-        for n, gg in enumerate(PI[k]):
-            mm(grp(n), row("NBE", gg), C16, False, n % 4 == 3)
-        mm(bank("PS3", 128, 256), C16, V("IB"), True, True)
-        act(V("CS"), bank("PS3", 128, 256))
+        for n in ((4, 5, 6, 7, 0, 1, 2, 3) if GS else range(8)):
+            mm(grp(n), row("NBE", PI[k][n]), C16, False, n % 4 == 3)
+        mm(bank("PS4", 256, 384), C16, V("IB"), True, True)
         swap("dpool%d" % k, ("POOL", 2048), ("POOL", 0), d, 2048)
-        for b in SB[1:]:
-            mm(V(YB[b]), V("IB"), C(src, b, 2048, 4), True, False)
-        if VB:
-            mm(V("PS5"), V("CS"), V("E4"), True, True)
+        for j in range(NO, min(NO + 4, 16)):
+            mine(j, False)
+
+        def own(j):
+            tt(row("Y1H", j), bank("PS5", 256, 384), C("POOL", j, 2048, 16), MAX)
+
+        def key(name, w, n, j, last=False):
+            mm(V("PS3", slice(0, 8), j), row(name, n), V(w, k), False, last)
+
+        def far(b):
+            n = min(512, 128 * (16 - NO) - 512 * b)
+            act(C("Y1", 512 * b, 512 * b + n), bank(YB[2 + b], 0, n), RELU, bias=C("NEG", min(k, 1), min(k, 1) + 1))
+        for j in range(N0):
+            own(j)
         for n, gg in enumerate(PI[k]):
-            ts(row("G", n), grp(n), V("PS2", 0, slice(8 + gg, 9 + gg)), None, GT)
+            if GS and n >= 4:
+                act(row("G", n), grp(n), SIGN, bias=C("CB", gg, gg + 1))
+            elif GS:
+                ts(row("G", n), grp(n), V("PS2", 0, slice(8 + gg, 9 + gg)), 2.0, GT, MUL)
+            else:
+                ts(row("G", n), grp(n), V("PS2", 0, slice(8 + gg, 9 + gg)), None, GT)
+        act(V("CSZ", ALL, slice(16, 32)), bank("PS4", 256, 384), scale=1.0 / 16)
+        if k == 0:
+            ids_out(lambda a, b: V("IDS", ALL, slice(a, b)), bank("PS3", 256, 320))
+        else:
+            ids_out(lambda a, b: V("PS3", slice(16, 24), slice(a, b)), V("PS3", slice(24, 28)))
+        if NO < 16:
+            far(0)
         mm(V("PS0"), V("ONE"), row("G", 0, 512), True, True)
-        for n in (range(4, 8) if MT else range(8)):
+        for n in range(4, 8):
             mm(V("PS2", 1, slice(8 + n, 9 + n)), row("G", n), C("ONE", 0, 1), True, True)
-        if not MT:
-            mm(V("PS1"), V("ONE"), row("G", 1, 512), True, True)
-
-        def far(n):
-            act(row("Y1", n, 512), V(YB[SB[n]]), RELU, bias=C("NEG", min(k, 1), min(k, 1) + 1))
-        for b in SB:
-            mm(V(YB[b]), V("CS"), V("E4N"), False, True)
-        for n in range(len(SB) - MT):
-            far(n)
-
-        def own(b):
-            tt(row("Y1H", b, 512), V("PS5"), C("POOL", b, 2048, 4), MAX)
-
-        def keys(name, w, n, b, last=False):
-            for j in range(4):
-                mm(V("PS3", slice(0, 8), 4 * j + b), C(name, 512 * n + j, 512 * n + 512, 4), V(w, k), False, last and j == 3)
-        n1 = len(VB) // 2
-        for b in VB[:n1]:
-            own(b)
-        mm(bank("PS3", 0, 128), V("IB"), V("QK"), True, False)
-        for b in SB:
-            mm(V("PS3", slice(0, 8), slice(b, 16, 4)), C16, V("BX", k, ALL, slice(b, 16, 4)), False, False)
-        for b in VB[:n1]:
-            keys("Y1H", "BP3", b, b)
-        for n in range(4 if MT else 8):
-            ts(row("M", n), grp(n), V("PS2", 1, slice(8 + (n ^ 4), 9 + (n ^ 4))), None, EQU)
-            if MT:
-                mm(grp(4 + n), row("M", n), V("IB"), True, True)
-        if MT:
-            act(row("M", 1, 512), V("PS1"))
-            far(len(SB) - 1)
-        act(V("MAF"), row("M", 0, 512))
+        for first in (True, False):
+            for j in range(NO + 4, 16):
+                mine(j, first)
+        for j in range(N0, N1):
+            own(j)
+        mm(bank("PS3", 0, 128), V("IB"), V("QKS"), True, False)
+        if NO < 16:
+            mm(V("PS3", slice(0, 8), slice(NO, 16)), C16, V("BX", k, ALL, slice(NO, 16)), False, False)
+        for j in range(N1):
+            key("Y1H", "BP3", j, j)
+        for n in range(4):
+            ts(row("M", n), grp(n), 127.0 if GS else 0.0, V("PS2", 1, slice(12 + n, 13 + n)), SUB, EQU)
+            mm(grp(4 + n), row("M", n), V("IB"), True, True)
+        act(row("M", 1, 512), V("PS1"))
+        if NO < 12:
+            far(1)
+        act(V("M64"), row("M", 0, 512), scale=64.0)
         for i in range(4):
             for c in (0, 1):
-                mm(V("PS4", slice(i, 8, 4), slice(0, 24)), row("M", i), V("IDX", c, ALL, i, slice(0, 24)), c == 0, c == 1)
-        for n, gg in enumerate(PI[k]):
-            if n == 4 and MT and len(SB) > 1:
-                keys("Y1", "BP1", 0, SB[0])
-            mm(bank("PS2", 256 + 16 * gg, 272 + 16 * gg), row("M", n), row("CS", gg ^ 2 * d, 16), True, True)
-        for b in VB[n1:]:
-            own(b)
+                mm(bank("PS4", 32 * i, 32 * i + 32), row("M", i), V("IDX", 4 * c + i), c == 0, c == 1)
+        for j in range(N1, NO):
+            own(j)
+
+        def means(n):
+            gg = PI[k][n]
+            mm(bank("PS0", 0, 128, ps=pb(gg // 2)), V("CSZ", gg ^ 2 * d, slice(16 - 16 * (gg % 2), 48 - 16 * (gg % 2))), row("M", n),
+               n % 2 == 0, n % 2 == 1)
+        for n in range(4):
+            means(n)
+        for j in range(N1, NO):
+            key("Y1H", "BP3", j, j)
+        for n in range(4, 8):
+            means(n)
+
+        def turned(r):
+            return [slice(None, None, -1) if r >> b & 1 else ALL for b in (2, 1, 0)]
 
         def same(r):
-            tt(row("EQ", r), V("PS4", slice(0, 8), slice(r, r + 16)), V("IDO"), EQU)
+            tt(V("EQ", slice(4 * r, 4 * r + 4)), V("PS4", slice(0, 16), *turned(r)), V("IDO"), EQU)
 
         def flags(r):
             for h in (0, 1):
-                e = row("EQ", 2 * r + h, 64)
-                mm(bank("PS3", 0, 64), V("IBN"), e, False, False)
-                mm(V("PS5", slice(0, 4), slice(r + 8 * h, r + 8 * h + 16)), V("IBP"), e, False, False)
-        for r in range(EQ0):
+                mm(bank("PS3", 0, 64), V("IBN"), V("EQ", slice(4 * r, 4 * r + 4), h), False, False)
+                mm(V("PS5", slice(0, 8), *turned(r)), V("IBP"), V("EQ", slice(4 * r, 4 * r + 4), h, turned(h)[2]), r + h == 0, False)
+        for r in range(8):
             same(r)
-        vcopy(V("CSM"), bank("PS2", 256, 384))
-        mm(V("PS0"), V("CSM"), V("E4"), True, True)
-        RB = V("PS5", slice(0, 4))
-        mm(RB, V("IB"), V("FQ"), True, False)
-        mm(RB, V("IBP"), V("FN"), False, False)
-        for b in VB[n1:]:
-            keys("Y1H", "BP3", b, b)
-        for r in range(EQ0, EQ1):
-            same(r)
-        for r in range(EQ1):
             flags(r)
-        todo = list(range(1 if MT and len(SB) > 1 else 0, len(SB)))
-        for b in range(4):
-            if b == 3:
-                for r in range(EQ1, 8):
-                    same(r)
-                    flags(r)
-            tt(row("Y2", b, 512), V("PS0"), C("POOL", b, 2048, 4), MAX)
-            if b < len(todo):
-                keys("Y1", "BP1", todo[b], SB[todo[b]])
-            keys("Y2", "BP2", b, b, b == 3)
-        vcopy(V("K1"), bank("PS3", 64, 128))
+        for j in range(NO, 16):
+            key("Y1", "BP1", j - NO, j)
+        for j in range(16):
+            tt(row("Y2", j), bank("PS0", 0, 128), C("POOL", j, 2048, 16), MAX)
+            key("Y2", "BP2", j, j, j == 15)
+        vcopy(C("K1", 0, 64), bank("PS3", 64, 128))
         tt(side_of("SRA", 0), bank("PS3", 0, 64), C("QBIG", 0, 64), MAX)
-        for i in range(4):
-            mm(V("PS5", i, slice(0, 16)), row("MAF", i), row("K1", i, 16), False, i == 3)
+        tt(C("K1", 64, 128), bank("PS3", 64, 128), C("K1", 0, 64), SUB)
+        for i in range(8):
+            mm(bank("PS5", 16 * (i % 4), 16 * (i % 4) + 16), row("M64", i % 4), row("K1", i, 16), False, i == 7)
+        for n in range(LEAD - 1):
+            rise(0, n)
         if k == 0:
-            tt(V("q0"), V("q0"), V("q1"), ADD)
-            vcopy(V("ILST"), V("q0"))
-        tt(V("T1"), V("PS5", slice(0, 4), slice(0, 16)), C("QBIG", 64, 128), MIN)
-        tt(side_of("SRA", 1), V("PS5", slice(0, 4), slice(16, 32)), V("T1"), MAX)
+            tt(row("w2", 1), row("w2", 0), row("w1", 1), ADD)
+        tt(side_of("SRA", 1), bank("PS5", 0, 64), C("QBIG", 64, 128), MIN)
+        rise(0, LEAD - 1)
+        if k == 0:
+            vcopy(V("ILST"), row("w2", 1))
         mm(bank("PS3", 256, 384), V("IB"), V("DB"), True, False)
         for i in range(4):
             mm(V("PS3", slice(16 + i, 24, 4)), row("M", i), V("TCC"), False, i == 3)
         LP = bank("PS2", 384, 512)
         mm(LP, V("T16", min(k, 1)), V("IB"), True, False)
         if k == 0:
-            late_constants()
+            late_constants(1)
             sgather(C("INF0", 0, 2048), V("XW"), V("ILST"))
             swap("dinf0", ("INF0", 2048), ("INF0", 0), d, 2048)
             mm(bank("PS7", 0, 256), V("IB"), V("XOC"), True, False)
@@ -621,6 +680,12 @@ def rank_program(g, core, T, topo):
                 part(1, 0)
                 keep(0)
             prey(3)
+            if k == 1:
+                late_constants(2)
+                for n in range(8):
+                    c = n % 4
+                    mm(bank("PS7", 0, 256), C("ZQ", 96 - 32 * c, 224 - 32 * c), V("PT", n // 4, ALL, slice(64 * c, 64 * c + 64)),
+                       n == 0, n == 7)
             if k == 2:
                 part(0, 1)
                 keep(1)
@@ -629,36 +694,36 @@ def rank_program(g, core, T, topo):
                 part(3, 0)
                 keep(2)
                 keep(3)
-        for s, kk, a, b in ((1, 2, "SRA", "SRB"), (2, 4, "SRB", "SRA"), (1, 4, "SRA", "SRB"),
-                            (4, 8, "SRB", "SRA"), (2, 8, "SRA", "SRB"), (1, 8, "SRB", "SRA")):
-            for kv in (0, 1):
-                step(a, b, s, kk, kv, desc=kv == 1)
-        for s, a, b in ((8, "SRA", "SRB"), (4, "SRB", "SRA"), (2, "SRA", "SRB"), (1, "SRB", "SRA")):
-            for side in (0, 1):
-                step(a, b, s, side=side, desc=side == 1)
-        tt(side_of("SRB", 0), side_of("SRA", 0), side_of("SRA", 1), MIN)
-        tt(side_of("SRB", 1), side_of("SRA", 0), side_of("SRA", 1), MAX)
+        for n in range(10):
+            rise(1, n)
+            if n + LEAD < 10:
+                rise(0, n + LEAD)
+        back = V("PS3", slice(0, 4), slice(None, None, -1))
+        tt(side_of("SRB", 0), back, side_of("SRA", 0), MIN)
+        tt(side_of("SRB", 1), back, side_of("SRA", 0), MAX)
         for s, a, b in ((8, "SRB", "SRA"), (4, "SRA", "SRB"), (2, "SRB", "SRA"), (1, "SRA", "SRB")):
             step(a, b, s, side=0)
             step(a, "SI" if s == 1 else b, s, side=1)
         za = slice(0, 4, 2) if k == 0 else slice(0, 2)
         zv = 2 * min(k, 1)
-        ts(V("T1"), side_of("SRB", 0), -3000000.0, 2 * BIG, LT, MUL)
+        ts(bank("PS3", 64, 128), side_of("SRB", 0), -3000000.0, 2 * BIG, LT, MUL)
         ts(C("QA", 64, 128), side_of("SI", 1), 31, None, AND)
-        tt(side_of("SRA", 0), side_of("SRB", 0), V("T1"), ADD)
+        tt(side_of("SRA", 0), bank("PS3", 64, 128), side_of("SRB", 0), ADD)
         ts(C("BB", 64, 128), C("QA", 64, 128), 16.0, None, LT)
         step("SRA", "SRB", 8, side=0)
-        vcopy(V("ZB", slice(4, 8), slice(112, 128)), C("QA", 64, 128))
+        vcopy(V("ZB", slice(4, 8), slice(16, 32)), C("QA", 64, 128))
         step("SRB", "SRA", 4, side=0)
-        tt(V("ZB", slice(0, 4), slice(112, 128)), C("BB", 64, 128), bank("PS3", 320, 384), MUL)
+        tt(V("ZB", slice(0, 4), slice(16, 32)), C("BB", 64, 128), bank("PS3", 320, 384), MUL)
         step("SRA", "SRB", 2, side=0)
-        if k == 0:
-            vcopy(V("PREYX"), bank("PS7", 0, 256))
+        if k < 2:
+            vcopy(row(("PREYX", "PREYL")[k], 0), bank("PS7", 0, 128))
         step("SRB", "SI", 1, side=0)
+        if k < 2:
+            vcopy(row(("PREYX", "PREYL")[k], 1), bank("PS7", 128, 256))
         for c in (1, 0):
             for i in range(4):
-                o = 16 * PI[k][4 + i]
-                mm(LP, V("ZB", 4 * c + i, slice(112 - o, 240 - o)), row("M", 4 + i), False, False)
+                o = 16 * (i % 2)
+                mm(bank("PS2", 384, 512, ps=pb(BS[k][i // 2])), V("ZB", 4 * c + i, slice(16 - o, 48 - o)), row("M", 4 + i), False, False)
         ts(C("BB", 0, 64), side_of("SI", 0), 4, 1, SHR, AND)
         ts(C("QA", 0, 64), side_of("SI", 0), 31, None, AND)
         tt(V("ZA", zv, za), C("BB", 0, 64), bank("PS3", 256, 320), MUL)
@@ -672,13 +737,20 @@ def rank_program(g, core, T, topo):
         for h in (0, 1):
             vgather(row("TAB", 2 * h, 512), V("POOL"), row("LST", 2 * h, 32))
             sgather(row("TAB", 2 * h + 1, 512), V("POOL"), row("LST", 2 * h + 1, 32))
-            for e in CFG["DE"] if k < 2 else ():
+            if k == 2:
+                for n in range(CFG["NPE"], nrank):
+                    if h == 1 or n < CFG["WH"]:
+                        a = 1024 * h if n < CFG["WH"] else 0
+                        nm, b = (("TAB", 2048), ("TAB", 4096), ("TAB", 6144), ("OWN", 0))[n]
+                        for c in range(4):
+                            dma("y", "dwin%d" % n, C(nm, b + a, b + 1024 * h + 1024, ps=pb(c)), C("TAB", a, 1024 * h + 1024, ps=pb(last[n])))
+            for e in CFG["DE"][h] if k < 2 else ():
                 swap("dtab%d%d" % (h, k), ("TAB", 2048 * e + 1024 * h), ("TAB", 1024 * h), e, 1024)
             if k < 2 and CFG["CPD"]:
                 a, b = 1024 * h, min(PV, 1024 * h + 1024)
-                dma("y", "dtab%d%d" % (h, k), C("OWN", a, b), C("TAB", a, b))
+                afs(C("OWN", a, b), C("TAB", a, b), [[0, b - a]], GE, 0, 0)
         pbk = ("PS0", "PS1", "PS4", "PS5", "PS6", "PS7", "PS3", "PS2")
-        jobs = [(e, i) for i in range(4) for e in (1, 2, 3) if e not in CFG["DE"]]
+        jobs = [(e, i) for i in range(4) for e in (1, 2, 3) if e not in CFG["DE"][i // 2]]
 
         def turn(n):
             mm(V(pbk[n]), V("PX", jobs[n][0]), row("TAB", jobs[n][1], 512), True, True)
@@ -716,12 +788,13 @@ def rank_program(g, core, T, topo):
             for h in (0, 1):
                 a = PV + w * h
                 mm(bank("PS%d" % (6 + h), 0, w), V("IB"), C("TAB", a, a + w), True, False)
-            ranks_open()
             ttg(C("SU", 0, PA), V("TAB"), C("PAL", 0, PA // 16), C("OWN", 0, PA), ADD)
             for h in (0, 1):
                 a = PV + w * h
                 sgather(row("REP", h, w), V("TAB"), C("PAL", a // 16, (a + w) // 16))
                 mm(bank("PS%d" % (6 + h), 0, w), V("IB"), row("REP", h, w), False, True)
+                if h == 0:
+                    ranks_open()
             ts(C("V16", 0, PA), C("SU", 0, PA), 0.5, 1536.25, MUL, ADD)
             sums("V16", 0, PA // 16)
             ttg(C("SU", PA, PV), V("TAB"), C("PAL", PA // 16, PV // 16), C("OWN", PA, PV), ADD)
@@ -730,29 +803,29 @@ def rank_program(g, core, T, topo):
                 a = PV + w * h
                 act(C("V16", a, a + w), bank("PS%d" % (6 + h), 0, w), scale=0.5, bias=1536.25)
             act(C("POOL", PC, 2048), C("V16", PC, 2048), bias=-1536.0)
-            ids_out(lambda a, b: V("PS3", slice(16, 24), slice(a, b)), V("PS3", slice(24, 28)))
         else:
             HALF = 1520.4375
             CV = CFG["CV"]
 
-            last = order + [me]
+            for r in others:
+                expect("aout%d" % r, len(e_all) if r in on and CFG["OA"] else NB, [row("RCV", r, 1024)])
+            expect("ayl", NB * (nrank - 1), [row("YL", r) for r in others])
+
             wins = [("TAB", 2048), ("TAB", 4096), ("TAB", 6144), ("OWN", 0)]
             NPE = CFG["NPE"]
-            for r in others:
-                expect("aout%d" % r, NB, [row("RCV", r, 1024)])
-            expect("ayl", NB * (nrank - 1), [row("YL", r) for r in others])
 
             def spread_out(n):
                 for i in range(4):
-                    mm(V("PS%d" % i), V("PX", 2 * n), row("TAB", i, 512), True, True)
+                    mm(V("PS%d" % i), V("BC", n), row("TAB", i, 512), True, True)
                 for i in range(4):
-                    (act if i % 2 else vcopy)(row("TAB", 4 * n + 4 + i, 512), V("PS%d" % i))
-            for n in range(NPE, nrank):
-                for c in range(4):
-                    dma("y", "dwin%d" % n, C(wins[n][0], wins[n][1], wins[n][1] + 2048, ps=pb(c)), C("TAB", 0, 2048, ps=pb(last[n])))
+                    (act if i % 2 else vcopy)(C(wins[n][0], wins[n][1] + 512 * i, wins[n][1] + 512 * i + 512), V("PS%d" % i))
 
-            def lists():
-                info(CFG["IV"])
+            def lists(h):
+                a, w = 1024 * h, CFG["IV"]
+                vgather(C(inf[3], a, a + w), V(inf[2]), C("LST", a // 16, (a + w) // 16))
+                sgather(C(inf[3], a + w, a + 1024), V(inf[2]), C("LST", (a + w) // 16, a // 16 + 64))
+
+            def lists_made():
                 as_list(inf[3], "WY", bank("PS2", 0, 128))
 
             def lists_out():
@@ -771,11 +844,15 @@ def rank_program(g, core, T, topo):
 
             def shut(n):
                 o = last[n]
-                nm, a = ("RCV", 2 * me) if o == me else ("OUT", 2 * n)
+                nm, a = ("RCV", 2 * me) if o == me else ("OUT", 2 * order.index(o))
                 ts(row(nm, a, 512), row("SU", n, 512), 0.5, HALF, MUL, ADD)
                 act(row(nm, a + 1, 512), V(YB[o]), scale=0.5, bias=HALF)
-                if o != me:
-                    send_to(o, "aout%d" % me, "lout", row("OUT", n, 1024), row("RCV", me, 1024))
+                if o == off[1] and CFG["HO"]:
+                    send([("hout", [None], e_all, row("OUT", 1, 1024), row("OUT", 1, 1024))], "lout")
+                elif o in on and CFG["OA"]:
+                    send([("aout%d" % me, on, e_all, row("OUT", 2, 1024), row("RCV", me, 1024))], "lout")
+                elif o != me:
+                    send_to(o, "aout%d" % me, "lout", row("OUT", order.index(o), 1024), row("RCV", me, 1024))
 
             def store(n):
                 q = last[n]
@@ -783,12 +860,12 @@ def rank_program(g, core, T, topo):
                 act(C("YXO", 1024 * q + CV, 1024 * q + 1024), C("RCV", 1024 * q + CV, 1024 * q + 1024), bias=-1408.0)
                 for c in range(4):
                     dma("y", "dyx%d" % n, None, row("YXO", q, 1024, ps=pb(c)), ext_out=T.yx[32 * q:32 * q + 32, 1024 * c:1024 * c + 1024])
-            steps = {"w": spread_out, "f": fetch, "s": shut, "c": store}
+            steps = {"w": spread_out, "f": fetch, "l": lists, "s": shut, "c": store}
             for word in CFG["END"].split():
                 if word[0] in steps:
                     steps[word[0]](int(word[1]))
                 else:
-                    {"L": lists, "O": lists_out, "Y": lists_store}[word]()
+                    {"L": lists_made, "O": lists_out, "Y": lists_store}[word]()
     for sem in sorted(tot):
         if know["g"].get(sem, 0) < tot[sem]:
             g.wait_ge(T.sem[sem], tot[sem])

from concourse.bass import DstId, RemoteDMATransfer
from concourse.mybir import AluOpType, ActivationFunctionType

BF, FH, FF, I4, U2 = "bfloat16", "float16", "float32", "int32", "uint16"
S6 = [128, 8, 2, 2, 2, 2]
CFG = {"PV": 1088, "PA": 896, "PC": 1088, "GS": 1, "N0": 4, "N1": 8, "NO": 12, "DE": ((2, 3, 1), ()), "CPD": 1, "LV": 3,
       "CV": 640, "IV": 640, "IA": 1024, "LO": (0, 1, 2, 3), "NPE": 1, "HP": 0, "HO": 0, "OA": 0, "LEAD": 2,
       "WH": 2, "LA": 1, "END": "w0 f0 l0 s0 f1 f2 s1 s2 l1 L c0 f3 O c2 s3 c1 c3 Y"}
XZ = 13328
_SB = {
    "SL": ([128, 128], I4), "PR": ([128, 256], I4), "LISTS": ([128, 512], U2), "LF": ([128, 512], FF), "OFF": ([128, 512], U2),
    "XW": ([128, XZ + 16 + 3072], BF), "X0": ([128, 4096], BF),
    "PT": ([128, 2, 4, 256], BF), "IDT": ([128, 4, 4, 256], BF), "PREYX": ([128, 256], U2), "PREYL": ([128, 256], U2), "XOC": ([128, 256], BF),
    "DI": ([128, 128], I4), "q0": ([128, 128], I4), "q1": ([128, 128], I4), "ILST": ([128, 128], U2),
    "w1": ([128, 256], I4), "w2": ([128, 256], I4), "IDS": ([128, 8, 16], BF),
    "TAB": ([128, 8192], BF), "POOL": ([128, 4096], BF), "INF0": ([128, 4096], BF), "INF1": ([128, 4096], BF),
    "H0": ([128, 4096], BF), "H1": ([128, 4096], BF), "REP": ([128, 2048], BF), "PP": ([128, 2048], FH), "OWN": ([128, 2048], BF),
    "SU": ([128, 2048], FH), "V16": ([128, 2048], FH), "OUT": ([128, 3072], FH), "RCV": ([128, 4096], FH),
    "YXO": ([128, 4096], FF), "YL": ([128, 512], FF),
    "C16": ([128, 128], FH), "CSZ": ([128, 8, 48], FH), "CB": ([128, 8], FF), "B8P": ([128, 8], BF),
    "IBS": ([128, 128], BF), "IBM": ([128, 128], BF),
    "G": ([128, 1024], BF), "M": ([128, 1024], BF), "M64": ([128, 512], BF), "QKS": ([128, 128], BF),
    "IDO": ([128, 4, 2, 16], FF), "IDX": ([128, 8, 2, 16], BF), "PAL": ([128, 128], U2),
    "Y1": ([128, 1024], FF), "Y1H": ([128, 2048], FH), "Y2": ([128, 2048], FH), "EQ": ([128, 32, 2, 2, 8], BF),
    "K1": ([128, 128], FH),
    "SRA": (S6, FF), "SRB": (S6, FF), "SI": (S6, I4), "QA": ([128, 128], I4), "BB": ([128, 128], I4),
    "ZA": ([128, 4, 4, 32], BF), "ZB": ([128, 8, 48], BF), "LST": ([128, 128], U2),
    "ONE": ([128, 128], BF), "IB": ([128, 128], BF), "IF": ([128, 128], FF), "BCQ": ([128, 128], FF), "TC": ([128, 1024], BF),
    "IBP": ([128, 128], BF), "IBN": ([128, 128], BF), "IBQ": ([128, 128], BF), "IBH": ([128, 128], BF),
    "PX": ([128, 4, 128], BF), "ZS": ([128, 224], BF), "ZQ": ([128, 224], BF), "ZF": ([128, 224], FF),
    "B8a": ([128, 8], BF), "B8": ([128, 8], BF), "B8N": ([128, 8], BF), "NBE": ([128, 1024], BF),
    "PCI": ([128, 1], I4), "pi": ([128, 4], I4), "P16": ([128, 1], FF), "COL": ([128, 8], FF), "WC": ([128, 16], FF),
    "T16": ([128, 2, 128], BF), "DB": ([128, 128], BF), "TCC": ([128, 32], BF), "QK": ([128, 128], BF),
    "QBIG": ([128, 128], FF), "NEG": ([128, 2], FF),
    "C32": ([128, 2, 64], BF), "bx": ([128, 64], BF), "BX": ([128, 3, 8, 16], BF),
    "BP1": ([128, 3, 8], FF), "BP2": ([128, 3, 8], FH), "BP3": ([128, 3, 8], FH),
    "B8K": ([128, 8], BF), "BC": ([128, 4, 128], BF), "SEL": ([128, 3, 12], BF), "WB": ([128, 144], BF), "WY": ([128, 144], BF),
}
SCRATCH = {k: ("sbuf", s, d) for k, (s, d) in _SB.items()}
_PS = {"PS%d" % i: ([128, 64, 2, 2, 2] if i in (4, 5) else [128, 32, 16], FF) for i in range(8)}
for _k, (_s, _d) in _PS.items():
    SCRATCH[_k] = ("psum", _s, _d)
SEMAPHORES = (["cv", "cs", "ct", "cg", "dsl", "dpr", "dcp", "dpw", "dyl", "ali", "apt", "ayl", "lli", "lpt", "lx", "lout", "lyl", "hpt0", "hpt1", "hout"]
              + [n + str(i) for n in ("dx", "ax", "aout", "dyx", "dwin") for i in range(4)]
              + [n + str(k) for n in ("dpool", "dinf", "dtab0", "dtab1") for k in range(3)])

ADD, SUB, MUL = AluOpType.add, AluOpType.subtract, AluOpType.mult
MAX, MIN = AluOpType.max, AluOpType.min
GT, GE, LT, EQU, NE = AluOpType.is_gt, AluOpType.is_ge, AluOpType.is_lt, AluOpType.is_equal, AluOpType.not_equal
SHR, AND = AluOpType.arith_shift_right, AluOpType.bitwise_and
COPY, RELU, ABS = ActivationFunctionType.Copy, ActivationFunctionType.Relu, ActivationFunctionType.Abs
IDENT, SIGN = ActivationFunctionType.Identity, ActivationFunctionType.Sign
ALL = slice(None)
BIG = 4194304.0
DS = (1, 2, 3)


def peers(r, cores, topo):
    c = cores[r]
    off = [o for o in range(len(cores)) if topo.chip(cores[o]) != topo.chip(c)]
    off.sort(key=lambda o: topo.die(cores[o]) != topo.die(c))
    on = [o for o in range(len(cores)) if o != r and o not in off]
    aide = [a for a in topo.cores_of(c) if a not in cores and topo.die(a) == topo.die(c) and topo.may_write(a, cores[off[0]])]
    return off, on, aide[0]


def aide_program(g, core, T, topo, r):
    cores = list(T.cores)
    off = peers(r, cores, topo)[0]
    es = topo.engines(core, cores[off[0]])
    jobs = [("hpt%d" % c, "apt", off, T.PT[:, c, r, :], T.PT[:, c, r, :]) for c in (0, 1)] if CFG["HP"] else []
    jobs += [("hout", "aout%d" % r, off[1:], T.OUT[:, 1024:2048], T.RCV[:, 1024 * r:1024 * r + 1024])] if CFG["HO"] else []
    for mine, theirs, rs, src, dst in jobs:
        g.wait_ge(T.sem[mine], len(topo.engines(cores[r], core)) if mine == "hout" else len(es))
        ids = [DstId(rid=topo.addr(cores[o])[0], pnc=topo.addr(cores[o])[1]) for o in rs]
        g.remote_dma_fused([RemoteDMATransfer(dst_ids=ids, dma_engine_mask=topo.mask(core, cores[off[0]]), remote_sem=T.sem[theirs],
                                              srcs=[src], dsts=[dst for o in rs], alu_op=0)], local_sem=T.sem["lout"])
    if jobs:
        g.wait_ge(T.sem["lout"], len(es) * len(jobs))


def rank_program(g, core, T, topo):
    me = T.rank_of(core)
    cores = list(T.cores)
    nrank = len(cores)
    if me is None:
        for r in range(nrank):
            if peers(r, cores, topo)[2] == core:
                aide_program(g, core, T, topo, r)
        return
    Q = {"v": g.vector, "s": g.scalar, "t": g.tensor, "g": g, "y": g.sync}
    know = {q: {} for q in Q}
    tot = {}
    log = {}

    def V(name, *idx, ps=ALL):
        shape = SCRATCH[name][1][1:]
        st = [1] * len(shape)
        for i in range(len(shape) - 2, -1, -1):
            st[i] = st[i + 1] * shape[i + 1]
        full = list(idx) + [ALL] * (len(shape) - len(idx))
        m = 1
        for x, n, w in reversed(list(zip(full, shape, st))):
            r = range(x, x + 1) if isinstance(x, int) else range(*x.indices(n))
            if m == (1 << w) - 1 and r.step == 1:
                m = ((1 << (w * len(r))) - 1) << (w * r[0])
            else:
                m = sum(m << (i * w) for i in r)
        return {"ap": T[name][tuple([ps] + full)], "n": name, "m": m, "p": sum(1 << i for i in range(*ps.indices(128)))}

    def C(name, a, b, step=1, **kw):
        return V(name, slice(a, b, step), **kw)

    def need(q, evs):
        for sem, cnt, sn in sorted(evs, key=lambda e: -len(e[2])):
            if know[q].get(sem, 0) >= cnt:
                continue
            c = tot[sem] if sem[0] in "dl" else cnt
            Q[q].wait_ge(T.sem[sem], c)
            k = know[q]
            for s_, c_ in list(sn.items()) + [(sem, c)]:
                if k.get(s_, 0) < c_:
                    k[s_] = c_

    def touch(q, ins, outs):
        evs = []
        for kind, lst in (("r", ins), ("w", outs)):
            for r in lst:
                if r["n"] in _PS:
                    d = log.setdefault(r["n"], {})
                    for oq in list(d):
                        if oq != q:
                            evs.append(d[oq])
                            del d[oq]
                    evs += [e[1] for e in log.get(r["n"] + "w", ()) if e[0] & r["m"]]
                    continue
                for e in log.get(r["n"], ()):
                    if e[0] & r["m"] and e[1] & r["p"] and not (kind == "r" and e[2] == "r"):
                        evs.append(e[3])
        return evs

    def note(q, ins, outs, ev):
        for kind, lst in (("r", ins), ("w", outs)):
            for r in lst:
                if r["n"] in _PS:
                    log.setdefault(r["n"], {})[q] = ev
                    if kind == "w":
                        old = [e for e in log.get(r["n"] + "w", ()) if e[0] & ~r["m"]]
                        log[r["n"] + "w"] = old + ([(r["m"], ev)] if q != "t" else [])
                    continue
                old = log.get(r["n"], [])
                if kind == "w":
                    old = [e for e in old if e[0] & ~r["m"] or e[1] & ~r["p"]]
                else:
                    old = [e for e in old if e[:3] != (r["m"], r["p"], "r") or e[3][0] != ev[0]]
                log[r["n"]] = old + [(r["m"], r["p"], kind, ev)]

    def done(q, sem, n):
        tot[sem] = tot.get(sem, 0) + n
        d = dict(know[q])
        d[sem] = tot[sem]
        return (sem, tot[sem], d)

    def op(q, fn, ins, outs):
        need(q, touch(q, ins, outs))
        ev = done(q, "c" + q, 1)
        fn().then_inc(T.sem["c" + q], 1)
        note(q, ins, outs, ev)

    def dma(q, sem, out, in_, ext_out=None, ext_in=None):
        ins, outs = [in_] if in_ else [], [out] if out else []
        need(q, touch(q, ins, outs))
        ev = done(q, sem, 16)
        Q[q].dma_start(out["ap"] if out else ext_out, in_["ap"] if in_ else ext_in).then_inc(T.sem[sem], 16)
        note(q, ins, outs, ev)

    def expect(sem, cnt, outs):
        tot[sem] = tot.get(sem, 0) + cnt
        note("net", [], outs, (sem, tot[sem], {sem: tot[sem]}))

    others = [r for r in range(nrank) if r != me]
    off, on, aide = peers(me, cores, topo)
    e_off = list(topo.engines(core, cores[off[0]]))
    e_on = [e for e in topo.engines(core, cores[on[0]]) if e not in e_off]
    e_all = e_off + e_on
    NB = len(e_off)

    def did(r):
        rid, pid, _ = topo.addr(aide if r is None else cores[r])
        return DstId(rid=rid, pnc=pid)

    def send(parts, lsem):
        need("g", touch("g", [p[3] for p in parts], []))
        tr = [RemoteDMATransfer(dst_ids=[did(r) for r in rs], dma_engine_mask=sum(1 << e for e in es), remote_sem=T.sem[sem],
                                srcs=[x["ap"]], dsts=[y["ap"] for r in rs], alu_op=0) for sem, rs, es, x, y in parts]
        ev = done("g", lsem, sum(len(p[2]) for p in parts))
        g.remote_dma_fused(tr, local_sem=T.sem[lsem])
        note("g", [p[3] for p in parts], [], ev)

    def send_all(sem, lsem, x):
        send([(sem, off, e_off, x, x), (sem, on, e_on, x, x)], lsem)

    def send_to(r, sem, lsem, x, y):
        send([(sem, [r], e_on if r in on else e_off, x, y)], lsem)

    def ts(out, a, s1, s2, op0, op1=None):
        ins = [a] + [s for s in (s1, s2) if isinstance(s, dict)]
        x1 = s1["ap"] if isinstance(s1, dict) else s1
        x2 = s2["ap"] if isinstance(s2, dict) else s2
        if op1 is None:
            op("v", lambda: g.vector.tensor_scalar(out["ap"], a["ap"], x1, None, op0), ins, [out])
        else:
            op("v", lambda: g.vector.tensor_scalar(out["ap"], a["ap"], x1, x2, op0, op1), ins, [out])

    def tt(out, a, b, o):
        op("v", lambda: g.vector.tensor_tensor(out["ap"], a["ap"], b["ap"], o), [a, b], [out])

    def ttg(out, win, lst, b, o):
        op("v", lambda: g.vector.tensor_tensor(out["ap"], win["ap"].indirect(lst["ap"]), b["ap"], o), [win, lst, b], [out])

    def vcopy(out, a):
        op("v", lambda: g.vector.tensor_copy(out["ap"], a["ap"]), [a], [out])

    def vgather(out, win, lst):
        op("v", lambda: g.vector.tensor_copy(out["ap"], win["ap"].indirect(lst["ap"])), [win, lst], [out])

    def sgather(out, win, lst):
        op("s", lambda: g.scalar.activation(out["ap"], win["ap"].indirect(lst["ap"]), COPY), [win, lst], [out])

    def act(out, a, fn=COPY, bias=0.0, scale=1.0):
        ins = [a] + [s for s in (bias, scale) if isinstance(s, dict)]
        b = bias["ap"] if isinstance(bias, dict) else bias
        s = scale["ap"] if isinstance(scale, dict) else scale
        op("s", lambda: g.scalar.activation(out["ap"], a["ap"], fn, bias=b, scale=s), ins, [out])

    def fill(out, c):
        op("v", lambda: g.vector.memset(out["ap"], c), [], [out])

    def mm(out, l, r, start, stop):
        op("t", lambda: g.tensor.matmul(out["ap"], l["ap"], r["ap"], start, stop), [l, r], [out])

    def iota(out, pattern, cm, small=True, base=0):
        if small:
            op("g", lambda: g.iota(out["ap"], pattern, base, cm, allow_small_or_imprecise_dtypes=True), [], [out])
        else:
            op("g", lambda: g.iota(out["ap"], pattern, base, cm), [], [out])

    def afs(out, a, pattern, cmp, base, cm):
        op("g", lambda: g.affine_select(out["ap"], a["ap"], pattern, cmp, 0.0, base, cm), [a], [out])

    def row(name, i, n=128, **kw):
        return C(name, n * i, n * i + n, **kw)

    def pb(b, n=32):
        return slice(n * b, n * b + n)

    def bank(name, a=0, b=512, ps=ALL):
        w = 512 // SCRATCH[name][1][1]
        if b - a < w:
            return V(name, a // w, slice(a % w, a % w + b - a), ps=ps)
        return V(name, slice(a // w, b // w), ps=ps)

    def grp(gg):
        return bank("PS%d" % (gg // 4), 128 * (gg % 4), 128 * (gg % 4) + 128)

    def xcol(o, ps=ALL):
        return C("XW", 16 + 4096 * o, 1040 + 4096 * o, ps=ps)

    def leaving(n, ps=ALL):
        return C("XW", XZ + 16 + 1024 * n, XZ + 1040 + 1024 * n, ps=ps)

    def swap(sem, dst, src, e, n):
        w = 64 if e == 2 else 32
        for b in range(128 // w):
            o = b ^ (e * 32 // w)
            dma("y", sem, C(dst[0], dst[1], dst[1] + n, ps=pb(b, w)), C(src[0], src[1], src[1] + n, ps=pb(o, w)))

    AS = [[r for r in range(nrank) if r < r ^ d] for d in DS]
    BS = [[r ^ d for r in a] for a, d in zip(AS, DS)]
    PI = [[2 * r + w for r in a + b for w in (0, 1)] for a, b in zip(AS, BS)]
    PV, PA, PC, GS, N0, N1, NO = (CFG[n] for n in ("PV", "PA", "PC", "GS", "N0", "N1", "NO"))

    order = off + on
    dma("y", "dsl", V("SL"), None, ext_in=T.sl[:, :])
    for n, q in enumerate(order + [me]):
        for c in range(4):
            dst = leaving(n, pb(c)) if q != me else xcol(me, pb(c))
            dma("ys"[c % 2], "dx%d" % n, dst, None, ext_in=T.x[32 * q:32 * q + 32, 1024 * c:1024 * c + 1024])
        if n == 1:
            dma("s", "dpr", V("PR"), None, ext_in=T.prey[:, :])
    fill(V("ONE"), 1.0)
    fill(C("XW", 1040, 4112), 0.0)
    iota(V("PCI"), [[0, 1]], 1, False)
    afs(V("IB"), V("ONE"), [[-1, 128]], EQU, 0, 1)
    afs(V("B8a"), C("ONE", 0, 8), [[-16, 8]], GE, 0, 1)
    afs(V("B8"), V("B8a"), [[16, 8]], GE, 15, -1)
    vcopy(row("LISTS", me), V("SL"))
    send([("ali", off, e_off, row("LISTS", me), row("LISTS", me))], "lli")
    for n, q in enumerate(order):
        if n == CFG["LA"]:
            send_to(on[0], "ali", "lli", row("LISTS", me), row("LISTS", me))
        send_to(q, "ax%d" % me, "lx", leaving(n), xcol(me))
    expect("ali", NB * (nrank - 1), [row("LISTS", r) for r in others])
    for r in others:
        expect("ax%d" % r, NB, [xcol(r)])

    def zeros(n):
        return C("XW", 1040, 1040 + n)
    act(C("XW", 5136, 8208), zeros(3072))
    fill(V("C32", 0), 32.0)
    fill(V("C32", 1), -0.5)
    fill(C("XW", 0, 16), 0.0)
    fill(C("XW", XZ, XZ + 16), 0.0)
    ts(C("pi", 0, 1), V("PCI"), 15, None, AND)
    ts(C("pi", 1, 2), V("PCI"), 5, None, SHR)
    ts(C("pi", 2, 3), V("PCI"), 6, None, SHR)
    ts(C("pi", 3, 4), V("PCI"), 5, 1, SHR, AND)
    vcopy(V("IF"), V("IB"))
    vcopy(row("LF", me), V("SL"))
    vcopy(V("P16"), C("pi", 0, 1))
    ts(C("COL", 0, 1), C("pi", 1, 2), -1024.0, 16.0, MUL, ADD)
    ts(C("COL", 1, 2), C("pi", 1, 2), 2048.0, None, MUL)
    ts(C("COL", 2, 3), C("pi", 2, 3), -8192.0, 4096.0, MUL, ADD)
    ts(C("COL", 3, 4), C("pi", 3, 4), -4096.0, 2048.0, MUL, ADD)
    for c in range(4):
        vcopy(row("BCQ", c, 32), row("IB", me, 32))

    def spread(r):
        mm(grp(r), V("BCQ"), row("LF", r), True, True)

    def columns(r):
        ts(row("OFF", r), grp(r), C("COL", 0, 1), float(XZ), ADD, MIN)
    spread(me)
    fill(C("XW", 9232, 12304), 0.0)
    columns(me)
    ts(V("w1"), V("PR"), 1920, None, AND)
    ts(V("w2"), V("PR"), 127, None, AND)
    vcopy(V("PT", 0, me), V("w1"))
    vcopy(V("PT", 1, me), V("w2"))
    for c in (0, 1):
        if CFG["HP"]:
            send([("hpt%d" % c, [None], e_on, V("PT", c, me), V("PT", c, me))], "lpt")
            send_to(on[0], "apt", "lpt", V("PT", c, me), V("PT", c, me))
        else:
            send_all("apt", "lpt", V("PT", c, me))
    expect("apt", 2 * NB * (nrank - 1), [V("PT", ALL, r) for r in others])
    fill(V("ZS"), 0.0)
    for c in range(4):
        vcopy(C("ZS", 96, 128, ps=pb(c)), row("IB", c, 32, ps=pb(c)))
    for i in range(8):
        ts(row("NBE", i), V("ONE"), C("B8", i, i + 1), -128.0, MUL, MUL)
    ts(V("B8N"), V("B8"), -128.0, None, MUL)
    fill(C("NEG", 0, 1), 0.0)
    fill(C("NEG", 1, 2), -1536.0)
    for nm in ("ZF", "ZQ"):
        act(V(nm), zeros(224))
        act(C(nm, 96, 128), row("IB", me, 32))
    act(V("CSZ"), zeros(384))
    act(V("ZB"), zeros(384))
    act(V("IBS"), V("IB"), scale=1.0 / 16)
    act(V("IBM"), V("IB"), scale=-1.0 / 16)
    act(V("B8P"), V("B8"), scale=128.0)
    act(V("IBP"), V("IB"), scale=2 * BIG)
    act(V("IBN"), V("IB"), scale=-2 * BIG)
    act(V("IDT", 3), zeros(1024), IDENT, bias=V("P16"))

    def weights(k):
        for side, rs in enumerate((AS[k], BS[k])):
            s = 32 * (rs[1] - rs[0])
            afs(V("bx"), V("C32", side), [[-s, 2], [-16, 2], [0, 16]], GE, -32 * rs[0], 1)
            afs(V("BX", k, slice(4 * side, 4 * side + 4)), V("bx"), [[s, 2], [16, 2], [0, 16]], GE, 32 * rs[0] + 15, -1)
    iota(V("QK"), [[16, 2], [0, 4], [1, 16]], 0)
    weights(0)
    iota(V("TC"), [[0, 8], [1, 128]], -1)
    iota(V("IDT", 0), [[0, 4], [1, 256]], 0)
    iota(V("IDT", 1), [[1, 2], [0, 512]], 0)
    iota(V("IDT", 2), [[0, 2], [1, 2], [0, 256]], 0)
    for r in order[::-1]:
        vcopy(row("LF", r), row("LISTS", r))
        spread(r)
    for n, r in enumerate(AS[0] + BS[0]):
        mm(bank("PS3", 256 + 32 * n, 288 + 32 * n), row("LF", r), row("IF", me, 32), True, True)
    for r in range(nrank):
        mm(bank("PS3", 384, 512), C("ZF", 96 - 32 * r, 224 - 32 * r), row("LF", r), r == 0, r == nrank - 1)

    def ids_out(src, full):
        act(V("IDX", ALL, 0), src(0, 16))
        act(V("IDX", ALL, 1, slice(0, 8)), src(8, 16))
        act(V("IDX", ALL, 1, slice(8, 16)), src(0, 8))
        for h in (0, 1):
            act(V("IDO", ALL, h), full)


    def ranks_open():
        for h in (0, 1):
            mm(V("PS%d" % h), V("IB"), row("TC", h, 512), True, False)
    for o in [me] + order[::-1]:
        dma("y", "dcp", row("X0", o, 1024), xcol(o))
    YB = ("PS4", "PS5", "PS6", "PS7")
    win = C("XW", 0, XZ + 16)
    askers = [me] + order[::-1]
    for n, r in enumerate(askers):
        zs = C("ZS", 96 - 32 * r, 224 - 32 * r)
        if n < nrank - 1:
            columns(askers[n + 1])
            if n == nrank - 2:
                ranks_open()
            vgather(row("TAB", 2 * r, 1024), win, row("OFF", 2 * r, 64))
            sgather(row("TAB", 2 * r + 1, 1024), win, row("OFF", 2 * r + 1, 64))
            for i, b in enumerate(YB):
                mm(V(b), zs, row("TAB", 4 * r + i, 512), n == 0, False)
        else:
            for i, b in enumerate(YB):
                (sgather if i % 2 else vgather)(row("TAB", 4 * r + i, 512), win, row("OFF", 4 * r + i, 32))
                mm(V(b), zs, row("TAB", 4 * r + i, 512), False, True)
    for i, b in enumerate(YB):
        if i % 2 == 0:
            ts(row("POOL", i, 512), V(b), -128.0, None, ADD)
        else:
            act(row("POOL", i, 512), V(b), bias=-128.0)
    act(V("BP1", 0), V("BX", 0, ALL, 0), scale=16.0)
    act(V("BP2", 0), V("BX", 0, ALL, 0), scale=-16.0)
    act(V("BP3", 0), V("BX", 0, ALL, 0), scale=16.0)
    act(C("QKS", 0, 64), C("QK", 0, 64))
    act(C("QKS", 64, 128), C("QK", 64, 128), scale=1.0 / 64)
    act(C("QBIG", 0, 64), C("QK", 0, 64), bias=-BIG)
    act(C("QBIG", 64, 128), C("QK", 64, 128), bias=BIG)
    vcopy(C("q0", 0, 64), bank("PS3", 320, 384))
    ts(C("q1", 0, 64), C("q0", 0, 64), 16256, None, AND)
    ts(C("q1", 64, 128), C("q0", 0, 64), 127, None, AND)
    ts(C("WC", 0, 6), C("QK", 0, 6), V("P16"), None, EQU)
    vcopy(V("DI"), bank("PS3", 384, 512))
    vcopy(V("IDS"), V("q1"))
    ts(row("w1", 0), V("DI"), 15, None, AND)
    for c in range(4):
        for h in (0, 1):
            dma("y", "dpw", C("XW", 0, 16384, ps=slice(32 * c + 3 + h, 32 * c + 32, 16)), V("PT", h, ps=pb(me)))
    for c in (3, 0, 1, 2):
        dma("y", "dpw", C("XW", 0, 16384, ps=slice(c + 2 * (c // 3), 128, 16)), V("IDT", c))
    for side, base in enumerate((2032, 2064)):
        iota(row("DB", side, 64), [[0, 64]], 32 * side - 16, base=base)
        iota(row("TCC", side, 16), [[0, 16]], 16 - 32 * side)
    iota(V("T16", 0), [[0, 2], [-16, 2], [0, 32]], 16)
    iota(V("T16", 1), [[-16, 2], [0, 64]], 16)
    weights(1)
    weights(2)
    for c in range(4):
        need("g", [("cg", tot["cg"], {})])
        iota(V("XOC", ps=pb(c)), [[4096 - 8192 * (c // 2), 2], [2048 - 4096 * (c % 2), 2], [0, 64]], 0, base=2048 * c)

    def late_constants(k):
        def w(i):
            return C("WC", i, i + 1)
        if k == 1:
            act(V("ZA"), V("IDT", 1, slice(0, 2)))
            act(V("WB"), V("IDT", 1, 0, slice(0, 144)))
            for out, a, s, b in ((6, 1, C("COL", 2, 3), 3), (7, 2, C("COL", 3, 4), 4), (8, 1, 8192.0, 5), (11, 1, 2.0, 2),
                                 (9, 2, 4096.0, 8), (12, 5, 4.0, 11), (13, 6, 1.0, 7), (10, 0, 16.0, 9), (15, 12, 256.0, 0)):
                act(w(out), w(a), IDENT, bias=w(b), scale=s)
            act(w(14), w(12), scale=256.0)
            act(C("WB", 15, 128, 16), V("B8"), scale=w(13))
            for e in (1, 2, 3):
                for b in range(4):
                    act(V("PX", e, pb(b)), row("IB", b ^ e, 32))
        else:
            act(V("WY"), V("IDT", 1, 0, slice(0, 144)))
            for n in range(CFG["NPE"]):
                for b in range(4):
                    act(V("BC", n, pb(b)), row("IB", last[n], 32))
            act(V("IBQ"), V("IB"), scale=0.25)
            act(V("IBH"), V("IB"), scale=0.5)
            act(C("WY", 15, 128, 16), V("B8"), scale=w(10))
        act(V("B8K", slice(0, 4)), V("BX", k, slice(0, 4), 0), scale=1.0 / 32)
        act(V("B8K", slice(4, 8)), V("BX", k, slice(4, 8), 0), scale=-2.0)
        act(V("BP1", k), V("BX", k, ALL, 0), scale=16.0)
        act(V("BP2", k), V("BX", k, ALL, 0), scale=-16.0)
        act(V("BP3", k), V("BX", k, ALL, 0), scale=16.0)
        for c, (i, side) in enumerate(((0, 1), (14, 1), (15, 0))):
            act(V("SEL", k, slice(4 * c, 4 * c + 4)), row("B8K", side, 4), scale=w(i))

    def as_list(name, w, out):
        for j in range(16):
            mm(out, C(w, 15 - j, 143 - j), C(name, j, 2048, 16), j == 0, j == 15)

    bits = {1: 5, 2: 4, 4: 3, 8: 2}

    def half(name, s, sv, k=None, kv=None, side=None):
        ix = [ALL] * 6
        ix[bits[s]] = sv
        if k is not None:
            ix[bits[k]] = kv
        if side is not None:
            ix[1] = slice(4 * side, 4 * side + 4)
        return V(name, *ix[1:])

    def step(src, dst, s, k=None, kv=None, side=None, desc=False):
        lo, hi = half(src, s, 0, k, kv, side), half(src, s, 1, k, kv, side)
        dl, dh = half(dst, s, 0, k, kv, side), half(dst, s, 1, k, kv, side)
        if desc:
            dl, dh = dh, dl
        tt(dl, lo, hi, MIN)
        tt(dh, lo, hi, MAX)

    def rise(side, n):
        s, first = ((1, 0), (2, 1), (1, 0), (4, 1), (2, 0), (1, 0), (8, 1), (4, 0), (2, 0), (1, 0))[n]
        src, dst = ("SRA", "SRB") if n % 2 == 0 else ("SRB", "SRA")
        ix = [slice(4 * side, 4 * side + 4)] + [ALL] * 4
        lo, hi = list(ix), list(ix)
        lo[bits[s] - 1], hi[bits[s] - 1] = 0, 1
        if first:
            hi[bits[s]:] = [slice(None, None, -1)] * (5 - bits[s])
        for o, out, c in ((MIN, lo, 0), (MAX, hi, 1)):
            tt(V("PS3", slice(0, 4), slice(c, 16, 2)) if side and n == 9 else V(dst, *out), V(src, *lo), V(src, *hi), o)

    def side_of(name, side):
        return V(name, slice(4 * side, 4 * side + 4))

    inf = ["INF0", "INF1", "INF0", "INF1"]
    LEAD = CFG["LEAD"]
    last = [(order + [me])[i] for i in CFG["LO"]]
    FB = ("PS4", "PS5", "PS6", "PS7", "PS0", "PS1", "PS3", "PS2")
    def sums(src, a, b):
        for j in range(16):
            mm(V("PS2", slice(a // 8, b // 8), slice(0, 8)), V("IB"), C(src, 16 * a + j, 16 * b, 16), j == 0, j == 15)


    for k, d in enumerate(DS):
        src = "POOL" if k == 0 else "V16"
        if k == 0:
            sums(src, 0, 64)
        sums(src, 64 if k == 0 else PA // 16, 128)
        C16 = V("C16")
        if k > 0:
            ts(C("POOL", 0, PC), C("V16", 0, PC), -1536.0, None, ADD)
        def mine(j, first):
            out = bank(YB[2 + (j - NO) // 4], 128 * ((j - NO) % 4), 128 * ((j - NO) % 4) + 128)
            if first:
                mm(out, V("IB"), C(src, j, 2048, 16), (j - NO) % 4 == 0, False)
            else:
                mm(out, V("IBM"), C16, False, (j - NO) % 4 == 3 or j == 15)
        for j in range(NO, min(NO + 4, 16)):
            mine(j, True)
        ts(C16, V("PS2", slice(0, 16), slice(0, 8)), 0.0 if k == 0 else -24576.0, None, ADD)
        if k == 0:
            ts(row("w1", 1), V("DI"), 4, None, SHR)
            ts(row("w2", 0), row("w1", 0), 1024, None, MUL)
        mm(bank("PS5", 256, 384), V("IBS"), C16, True, True)
        if GS:
            mm(V("PS7", 31, slice(0, 8)), C16, V("B8P"), True, True)
            act(V("CB"), V("PS7", 31, slice(0, 8)))
        mm(V("PS2", 0, slice(8, 16)), C16, V("B8N"), True, True)
        for n in ((4, 5, 6, 7, 0, 1, 2, 3) if GS else range(8)):
            mm(grp(n), row("NBE", PI[k][n]), C16, False, n % 4 == 3)
        mm(bank("PS4", 256, 384), C16, V("IB"), True, True)
        swap("dpool%d" % k, ("POOL", 2048), ("POOL", 0), d, 2048)
        for j in range(NO, min(NO + 4, 16)):
            mine(j, False)

        def own(j):
            tt(row("Y1H", j), bank("PS5", 256, 384), C("POOL", j, 2048, 16), MAX)

        def key(name, w, n, j, last=False):
            mm(V("PS3", slice(0, 8), j), row(name, n), V(w, k), False, last)

        def far(b):
            n = min(512, 128 * (16 - NO) - 512 * b)
            act(C("Y1", 512 * b, 512 * b + n), bank(YB[2 + b], 0, n), RELU, bias=C("NEG", min(k, 1), min(k, 1) + 1))
        for j in range(N0):
            own(j)
        for n, gg in enumerate(PI[k]):
            if GS and n >= 4:
                act(row("G", n), grp(n), SIGN, bias=C("CB", gg, gg + 1))
            elif GS:
                ts(row("G", n), grp(n), V("PS2", 0, slice(8 + gg, 9 + gg)), 2.0, GT, MUL)
            else:
                ts(row("G", n), grp(n), V("PS2", 0, slice(8 + gg, 9 + gg)), None, GT)
        act(V("CSZ", ALL, slice(16, 32)), bank("PS4", 256, 384), scale=1.0 / 16)
        if k == 0:
            ids_out(lambda a, b: V("IDS", ALL, slice(a, b)), bank("PS3", 256, 320))
        else:
            ids_out(lambda a, b: V("PS3", slice(16, 24), slice(a, b)), V("PS3", slice(24, 28)))
        if NO < 16:
            far(0)
        mm(V("PS0"), V("ONE"), row("G", 0, 512), True, True)
        for n in range(4, 8):
            mm(V("PS2", 1, slice(8 + n, 9 + n)), row("G", n), C("ONE", 0, 1), True, True)
        for first in (True, False):
            for j in range(NO + 4, 16):
                mine(j, first)
        for j in range(N0, N1):
            own(j)
        mm(bank("PS3", 0, 128), V("IB"), V("QKS"), True, False)
        if NO < 16:
            mm(V("PS3", slice(0, 8), slice(NO, 16)), C16, V("BX", k, ALL, slice(NO, 16)), False, False)
        for j in range(N1):
            key("Y1H", "BP3", j, j)
        for n in range(4):
            ts(row("M", n), grp(n), 127.0 if GS else 0.0, V("PS2", 1, slice(12 + n, 13 + n)), SUB, EQU)
            mm(grp(4 + n), row("M", n), V("IB"), True, True)
        act(row("M", 1, 512), V("PS1"))
        if NO < 12:
            far(1)
        act(V("M64"), row("M", 0, 512), scale=64.0)
        for i in range(4):
            for c in (0, 1):
                mm(bank("PS4", 32 * i, 32 * i + 32), row("M", i), V("IDX", 4 * c + i), c == 0, c == 1)
        for j in range(N1, NO):
            own(j)

        def means(n):
            gg = PI[k][n]
            mm(bank("PS0", 0, 128, ps=pb(gg // 2)), V("CSZ", gg ^ 2 * d, slice(16 - 16 * (gg % 2), 48 - 16 * (gg % 2))), row("M", n),
               n % 2 == 0, n % 2 == 1)
        for n in range(4):
            means(n)
        for j in range(N1, NO):
            key("Y1H", "BP3", j, j)
        for n in range(4, 8):
            means(n)

        def turned(r):
            return [slice(None, None, -1) if r >> b & 1 else ALL for b in (2, 1, 0)]

        def same(r):
            tt(V("EQ", slice(4 * r, 4 * r + 4)), V("PS4", slice(0, 16), *turned(r)), V("IDO"), EQU)

        def flags(r):
            for h in (0, 1):
                mm(bank("PS3", 0, 64), V("IBN"), V("EQ", slice(4 * r, 4 * r + 4), h), False, False)
                mm(V("PS5", slice(0, 8), *turned(r)), V("IBP"), V("EQ", slice(4 * r, 4 * r + 4), h, turned(h)[2]), r + h == 0, False)
        for r in range(8):
            same(r)
            flags(r)
        for j in range(NO, 16):
            key("Y1", "BP1", j - NO, j)
        for j in range(16):
            tt(row("Y2", j), bank("PS0", 0, 128), C("POOL", j, 2048, 16), MAX)
            key("Y2", "BP2", j, j, j == 15)
        vcopy(C("K1", 0, 64), bank("PS3", 64, 128))
        tt(side_of("SRA", 0), bank("PS3", 0, 64), C("QBIG", 0, 64), MAX)
        tt(C("K1", 64, 128), bank("PS3", 64, 128), C("K1", 0, 64), SUB)
        for i in range(8):
            mm(bank("PS5", 16 * (i % 4), 16 * (i % 4) + 16), row("M64", i % 4), row("K1", i, 16), False, i == 7)
        for n in range(LEAD - 1):
            rise(0, n)
        if k == 0:
            tt(row("w2", 1), row("w2", 0), row("w1", 1), ADD)
        tt(side_of("SRA", 1), bank("PS5", 0, 64), C("QBIG", 64, 128), MIN)
        rise(0, LEAD - 1)
        if k == 0:
            vcopy(V("ILST"), row("w2", 1))
        mm(bank("PS3", 256, 384), V("IB"), V("DB"), True, False)
        for i in range(4):
            mm(V("PS3", slice(16 + i, 24, 4)), row("M", i), V("TCC"), False, i == 3)
        LP = bank("PS2", 384, 512)
        mm(LP, V("T16", min(k, 1)), V("IB"), True, False)
        if k == 0:
            late_constants(1)
            sgather(C("INF0", 0, 2048), V("XW"), V("ILST"))
            swap("dinf0", ("INF0", 2048), ("INF0", 0), d, 2048)
            mm(bank("PS7", 0, 256), V("IB"), V("XOC"), True, False)
            for n in range(8):
                c = n % 4
                mm(bank("PS7", 0, 256), C("ZQ", 96 - 32 * c, 224 - 32 * c), V("PT", n // 4, ALL, slice(64 * c, 64 * c + 64)),
                   False, n == 7)
        else:
            def part(o, h):
                for n, (w, nm) in enumerate((("IBQ", "X0"), ("IBQ", "H0"), ("IBH", "H1"))):
                    mm(V(YB[o] if h else "PS%d" % (o % 2)), V(w), row(nm, 2 * o + h, 512), n == 0, n == 2 and not h)

            def prey(o):
                sgather(row("H%d" % (k - 1), o, 1024), V("TAB"), row("PREYX", o, 64))

            def keep(o):
                act(row("PP", o, 512), V("PS%d" % (o % 2)))
            for o in range(3):
                prey(o)
            if k == 2:
                part(0, 0)
                part(1, 0)
                keep(0)
            prey(3)
            if k == 1:
                late_constants(2)
                for n in range(8):
                    c = n % 4
                    mm(bank("PS7", 0, 256), C("ZQ", 96 - 32 * c, 224 - 32 * c), V("PT", n // 4, ALL, slice(64 * c, 64 * c + 64)),
                       n == 0, n == 7)
            if k == 2:
                part(0, 1)
                keep(1)
                part(2, 0)
                part(1, 1)
                part(3, 0)
                keep(2)
                keep(3)
        for n in range(10):
            rise(1, n)
            if n + LEAD < 10:
                rise(0, n + LEAD)
        back = V("PS3", slice(0, 4), slice(None, None, -1))
        tt(side_of("SRB", 0), back, side_of("SRA", 0), MIN)
        tt(side_of("SRB", 1), back, side_of("SRA", 0), MAX)
        for s, a, b in ((8, "SRB", "SRA"), (4, "SRA", "SRB"), (2, "SRB", "SRA"), (1, "SRA", "SRB")):
            step(a, b, s, side=0)
            step(a, "SI" if s == 1 else b, s, side=1)
        za = slice(0, 4, 2) if k == 0 else slice(0, 2)
        zv = 2 * min(k, 1)
        ts(bank("PS3", 64, 128), side_of("SRB", 0), -3000000.0, 2 * BIG, LT, MUL)
        ts(C("QA", 64, 128), side_of("SI", 1), 31, None, AND)
        tt(side_of("SRA", 0), bank("PS3", 64, 128), side_of("SRB", 0), ADD)
        ts(C("BB", 64, 128), C("QA", 64, 128), 16.0, None, LT)
        step("SRA", "SRB", 8, side=0)
        vcopy(V("ZB", slice(4, 8), slice(16, 32)), C("QA", 64, 128))
        step("SRB", "SRA", 4, side=0)
        tt(V("ZB", slice(0, 4), slice(16, 32)), C("BB", 64, 128), bank("PS3", 320, 384), MUL)
        step("SRA", "SRB", 2, side=0)
        if k < 2:
            vcopy(row(("PREYX", "PREYL")[k], 0), bank("PS7", 0, 128))
        step("SRB", "SI", 1, side=0)
        if k < 2:
            vcopy(row(("PREYX", "PREYL")[k], 1), bank("PS7", 128, 256))
        for c in (1, 0):
            for i in range(4):
                o = 16 * (i % 2)
                mm(bank("PS2", 384, 512, ps=pb(BS[k][i // 2])), V("ZB", 4 * c + i, slice(16 - o, 48 - o)), row("M", 4 + i), False, False)
        ts(C("BB", 0, 64), side_of("SI", 0), 4, 1, SHR, AND)
        ts(C("QA", 0, 64), side_of("SI", 0), 31, None, AND)
        tt(V("ZA", zv, za), C("BB", 0, 64), bank("PS3", 256, 320), MUL)
        vcopy(V("ZA", zv + 1, za), C("QA", 0, 64))
        for c in (0, 1):
            mm(LP, V("ZA", zv + c), V("IB"), False, c == 1)
        vcopy(V("LST"), LP)
        if k == 2:
            part(2, 1)
            part(3, 1)
        for h in (0, 1):
            vgather(row("TAB", 2 * h, 512), V("POOL"), row("LST", 2 * h, 32))
            sgather(row("TAB", 2 * h + 1, 512), V("POOL"), row("LST", 2 * h + 1, 32))
            if k == 2:
                for n in range(CFG["NPE"], nrank):
                    if h == 1 or n < CFG["WH"]:
                        a = 1024 * h if n < CFG["WH"] else 0
                        nm, b = (("TAB", 2048), ("TAB", 4096), ("TAB", 6144), ("OWN", 0))[n]
                        for c in range(4):
                            dma("y", "dwin%d" % n, C(nm, b + a, b + 1024 * h + 1024, ps=pb(c)), C("TAB", a, 1024 * h + 1024, ps=pb(last[n])))
            for e in CFG["DE"][h] if k < 2 else ():
                swap("dtab%d%d" % (h, k), ("TAB", 2048 * e + 1024 * h), ("TAB", 1024 * h), e, 1024)
            if k < 2 and CFG["CPD"]:
                a, b = 1024 * h, min(PV, 1024 * h + 1024)
                afs(C("OWN", a, b), C("TAB", a, b), [[0, b - a]], GE, 0, 0)
        pbk = ("PS0", "PS1", "PS4", "PS5", "PS6", "PS7", "PS3", "PS2")
        jobs = [(e, i) for i in range(4) for e in (1, 2, 3) if e not in CFG["DE"][i // 2]]

        def turn(n):
            mm(V(pbk[n]), V("PX", jobs[n][0]), row("TAB", jobs[n][1], 512), True, True)

        def land(n, scalar):
            dst = row("TAB", 4 * jobs[n][0] + jobs[n][1], 512)
            if scalar:
                act(dst, V(pbk[n]))
            else:
                vcopy(dst, V(pbk[n]))

        def info(a):
            vgather(C(inf[k + 1], 0, a), V(inf[k]), C("LST", 0, a // 16))
            sgather(C(inf[k + 1], a, 2048), V(inf[k]), C("LST", a // 16, 128))
        if k < 2:
            for n in range(len(jobs)):
                turn(n)
            info(CFG["IA"])
            swap("dinf%d" % (k + 1), (inf[k + 1], 2048), (inf[k + 1], 0), DS[k + 1], 2048)
            if len(jobs) == 8:
                land(7, True)
            as_list(inf[k + 1], "WB", bank("PS2", 0, 128))
            rest = list(range(min(len(jobs), 7)))
            nv = CFG["LV"]
            for n in rest[:nv]:
                land(n, False)
            for n in rest[:nv - 1:-1]:
                land(n, True)
            if not CFG["CPD"]:
                vcopy(C("OWN", 0, PV), C("TAB", 0, PV))
            ts(V("PAL"), bank("PS2", 0, 128), C("COL", 1, 2), None, ADD)
            for j in range(16):
                mm(V("PS3", slice(16, 28), j), C(inf[k + 1], j, 2048, 16), V("SEL", k + 1), True, True)
            w = (2048 - PV) // 2
            for h in (0, 1):
                a = PV + w * h
                mm(bank("PS%d" % (6 + h), 0, w), V("IB"), C("TAB", a, a + w), True, False)
            ttg(C("SU", 0, PA), V("TAB"), C("PAL", 0, PA // 16), C("OWN", 0, PA), ADD)
            for h in (0, 1):
                a = PV + w * h
                sgather(row("REP", h, w), V("TAB"), C("PAL", a // 16, (a + w) // 16))
                mm(bank("PS%d" % (6 + h), 0, w), V("IB"), row("REP", h, w), False, True)
                if h == 0:
                    ranks_open()
            ts(C("V16", 0, PA), C("SU", 0, PA), 0.5, 1536.25, MUL, ADD)
            sums("V16", 0, PA // 16)
            ttg(C("SU", PA, PV), V("TAB"), C("PAL", PA // 16, PV // 16), C("OWN", PA, PV), ADD)
            ts(C("V16", PA, PV), C("SU", PA, PV), 0.5, 1536.25, MUL, ADD)
            for h in (0, 1):
                a = PV + w * h
                act(C("V16", a, a + w), bank("PS%d" % (6 + h), 0, w), scale=0.5, bias=1536.25)
            act(C("POOL", PC, 2048), C("V16", PC, 2048), bias=-1536.0)
        else:
            HALF = 1520.4375
            CV = CFG["CV"]

            for r in others:
                expect("aout%d" % r, len(e_all) if r in on and CFG["OA"] else NB, [row("RCV", r, 1024)])
            expect("ayl", NB * (nrank - 1), [row("YL", r) for r in others])

            wins = [("TAB", 2048), ("TAB", 4096), ("TAB", 6144), ("OWN", 0)]
            NPE = CFG["NPE"]

            def spread_out(n):
                for i in range(4):
                    mm(V("PS%d" % i), V("BC", n), row("TAB", i, 512), True, True)
                for i in range(4):
                    (act if i % 2 else vcopy)(C(wins[n][0], wins[n][1] + 512 * i, wins[n][1] + 512 * i + 512), V("PS%d" % i))

            def lists(h):
                a, w = 1024 * h, CFG["IV"]
                vgather(C(inf[3], a, a + w), V(inf[2]), C("LST", a // 16, (a + w) // 16))
                sgather(C(inf[3], a + w, a + 1024), V(inf[2]), C("LST", (a + w) // 16, a // 16 + 64))

            def lists_made():
                as_list(inf[3], "WY", bank("PS2", 0, 128))

            def lists_out():
                vcopy(row("YL", me), bank("PS2", 0, 128))
                send_all("ayl", "lyl", row("YL", me))

            def lists_store():
                for q in range(nrank):
                    dma("y", "dyl", None, row("YL", q, ps=pb(me)), ext_out=T.yl[32 * q:32 * q + 32, :])

            def fetch(n):
                o, w = last[n], C(wins[n][0], wins[n][1], wins[n][1] + 2048)
                ttg(row("SU", n, 512), w, row("PREYL", 2 * o, 32), row("PP", o, 512), ADD)
                sgather(row("REP", n, 512), w, row("PREYL", 2 * o + 1, 32))
                mm(V(YB[o]), V("IB"), row("REP", n, 512), False, True)

            def shut(n):
                o = last[n]
                nm, a = ("RCV", 2 * me) if o == me else ("OUT", 2 * order.index(o))
                ts(row(nm, a, 512), row("SU", n, 512), 0.5, HALF, MUL, ADD)
                act(row(nm, a + 1, 512), V(YB[o]), scale=0.5, bias=HALF)
                if o == off[1] and CFG["HO"]:
                    send([("hout", [None], e_all, row("OUT", 1, 1024), row("OUT", 1, 1024))], "lout")
                elif o in on and CFG["OA"]:
                    send([("aout%d" % me, on, e_all, row("OUT", 2, 1024), row("RCV", me, 1024))], "lout")
                elif o != me:
                    send_to(o, "aout%d" % me, "lout", row("OUT", order.index(o), 1024), row("RCV", me, 1024))

            def store(n):
                q = last[n]
                ts(C("YXO", 1024 * q, 1024 * q + CV), C("RCV", 1024 * q, 1024 * q + CV), -1408.0, None, ADD)
                act(C("YXO", 1024 * q + CV, 1024 * q + 1024), C("RCV", 1024 * q + CV, 1024 * q + 1024), bias=-1408.0)
                for c in range(4):
                    dma("y", "dyx%d" % n, None, row("YXO", q, 1024, ps=pb(c)), ext_out=T.yx[32 * q:32 * q + 32, 1024 * c:1024 * c + 1024])
            steps = {"w": spread_out, "f": fetch, "l": lists, "s": shut, "c": store}
            for word in CFG["END"].split():
                if word[0] in steps:
                    steps[word[0]](int(word[1]))
                else:
                    {"L": lists_made, "O": lists_out, "Y": lists_store}[word]()
    for sem in sorted(tot):
        if know["g"].get(sem, 0) < tot[sem]:
            g.wait_ge(T.sem[sem], tot[sem])
